import numpy as np
import ml_dtypes


def mxq(x, axis, fmt="e4m3"):
    dtype, down = {"e4m3": (ml_dtypes.float8_e4m3fn, 7), "e5m2": (ml_dtypes.float8_e5m2, 14)}[fmt]
    v = np.moveaxis(np.asarray(x, np.float32).astype(ml_dtypes.bfloat16).astype(np.float64), axis, -1)
    blocks = v.reshape(v.shape[:-1] + (-1, 32))
    amax = np.abs(blocks).max(-1, keepdims=True)
    byte = np.maximum(np.where(amax > 0, np.frexp(amax)[1] - 1 + 127, 0) - down, 1)
    scale = np.exp2(byte - 127.0)
    codes = (blocks / scale).astype(np.float32).astype(dtype).astype(np.float64)
    return np.moveaxis((codes * scale).reshape(v.shape), -1, axis)


WIDE = False


def mx_kscale(k):
    if not WIDE:
        return np.ones(k)
    levels = np.array([10, -10, 5, -5, 0])
    if k % 512:
        return np.exp2(np.random.permutation(np.resize(levels, k // 32))).repeat(32)
    a = np.empty((k // 512, 16))
    for p in range(k // 512):
        a[p, :8] = np.random.permutation(np.resize(levels, 8))
        for g in range(8):
            far = levels[np.abs(levels - a[p, g]) >= 10]
            a[p, g + 8] = far[np.random.randint(len(far))]
    return np.exp2(a.ravel()).repeat(32)


def f64(x):
    return np.asarray(x).astype(np.float64)


def striped(idx):
    return np.tile(idx.reshape(-1, 16).T, (8, 1)).astype(np.uint16)


def unstriped(offs):
    return offs[:16].T.reshape(-1).astype(np.int64)


def striped8(idx):
    return np.concatenate([x.reshape(-1, 16).T for x in idx]).astype(np.uint16)


def runs(offs, k):
    lists = np.stack([offs[16 * r : 16 * r + 16].T.reshape(-1) for r in range(8)]).astype(np.int64)
    return lists[np.arange(k) % 512 // 64]


def pack_weight(w):
    k, n = w.shape
    w = f64(np.asarray(w, np.float32).astype(ml_dtypes.bfloat16)).reshape(k // 32, 32, n)
    amax = np.abs(w).max(1)
    byte = np.clip(np.where(amax > 0, np.frexp(amax)[1] - 1 + 127 - 7, 1), 1, 254)
    scaled = (w * np.exp2(127.0 - byte)[:, None, :]).reshape(k, n).astype(np.float32)
    words = np.ascontiguousarray(scaled.reshape(k // 512, 128, 4, n).transpose(0, 1, 3, 2)).astype(ml_dtypes.float8_e4m3fn).view(np.uint8)
    return words, np.ascontiguousarray(byte.astype(np.uint8).reshape(k // 512, 16, n))


def unpack_weight(words, scales):
    g, p, n, _ = words.shape
    vals = np.ascontiguousarray(words).view(ml_dtypes.float8_e4m3fn).astype(np.float64) * np.repeat(np.exp2(scales.astype(np.float64) - 127.0), 8, axis=1)[..., None]
    return vals.transpose(0, 1, 3, 2).reshape(g * 512, n)


def relu(v):
    return np.maximum(v, 0.0)

def planes(y):
    n, m = y.shape
    v = y.astype(np.float32).astype(ml_dtypes.bfloat16).astype(np.float64).reshape(n // 32, 32, m)
    top = np.abs(v).max(1)
    byte = np.clip(np.where(top > 0, np.frexp(top)[1] - 1 + 127 - 7, 1), 1, 254)
    codes = (v * np.exp2(127.0 - byte)[:, None, :]).reshape(n, m).astype(np.float32).astype(ml_dtypes.float8_e4m3fn).view(np.uint8)
    words = codes.reshape(n // 512, 128, 4, m).transpose(0, 1, 3, 2)
    return np.ascontiguousarray(words), np.ascontiguousarray(byte.astype(np.uint8).reshape(n // 512, 16, m))


K, T, S, V, N, H = 512, 2048, 512, 256, 512, 512


def setup_inputs():
    n = np.random.standard_normal
    s = mx_kscale(K)[:, None]
    u = mx_kscale(H)
    packed_xT = pack_weight(n((K, T)) * s)
    packed_w1 = pack_weight(n((K, H)) / np.sqrt(K) / s)
    packed_w3 = pack_weight(n((H, N)) / np.sqrt(H) / u[:, None])
    return {
        "x_words": packed_xT[0],
        "x_scales": packed_xT[1],
        "w1_words": packed_w1[0],
        "w1_scales": packed_w1[1],
        "w2": (n((K, H)) / np.sqrt(K) / s * u).astype(np.float32),
        "bg": (n((H, V)) * u[:, None]).astype(np.float32),
        "w3_words": packed_w3[0],
        "w3_scales": packed_w3[1],
        "offs": striped(np.random.permutation(T)[:S]),
        "p1": striped8(np.stack([np.random.permutation(S)[:V] for _ in range(8)])),
        "p2": striped8(np.stack([np.random.permutation(S)[:V] for _ in range(8)])),
    }


def reference(x_words, x_scales, w1_words, w1_scales, w2, bg, w3_words, w3_scales, offs, p1, p2):
    xq = unpack_weight(x_words, x_scales)[:, unstriped(offs)]
    val = mxq(f64(w2), 0, "e4m3").T @ xq
    c1 = val[np.arange(H)[:, None], runs(p1, H)]
    s = relu(unpack_weight(w1_words, w1_scales).T @ xq)
    s1 = np.exp(-1.0 * (s[np.arange(H)[:, None], runs(p1, H)]))
    c2 = val[np.arange(H)[:, None], runs(p2, H)]
    s2 = np.exp(-1.0 * (s[np.arange(H)[:, None], runs(p2, H)]))
    h = c2 + s2 * (f64(bg) - c2)
    z = c1 + s1 * (h - c1)
    out_0 = unpack_weight(w3_words, w3_scales).T @ mxq(z, 0, "e4m3")
    return (out_0,) + planes(out_0)

@@ -1,0 +1,208 @@
+from contextlib import ExitStack
+
+import concourse.mybir as mybir
+
+K, T, S, V, N, H = 512, 2048, 512, 256, 512, 512
+FLOPS = 2 * K * S * H * 2 + 2 * H * N * V
+
+F32 = mybir.dt.float32
+BF16 = mybir.dt.bfloat16
+I32 = mybir.dt.int32
+U32 = mybir.dt.uint32
+U16 = mybir.dt.uint16
+U8 = mybir.dt.uint8
+FP8X4 = mybir.dt.float8_e4m3fn_x4
+ALU = mybir.AluOpType
+ACT = mybir.ActivationFunctionType
+
+P = 128
+PACK = 4
+QUAD = 32
+X_ROW, W1_ROW, W3_ROW = 4, 8, 12
+
+
+def words_i32(ap):
+    return ap[0].rearrange("p n t -> p (n t)").bitcast(I32)
+
+
+def load_scales(queue, plane, scales, row):
+    for q in range(4):
+        queue.dma_start(
+            out=plane[QUAD * q + row : QUAD * q + row + 4, :].bitcast(I32),
+            in_=scales[0, 4 * q : 4 * q + 4, :].bitcast(I32),
+        )
+
+
+def deal(nc, dst, src, run):
+    nc.vector.tensor_copy(
+        out=dst[:].rearrange("p (t c i) -> p c t i", t=PACK, i=run),
+        in_=src[:].rearrange("p (c i t) -> p c t i", t=PACK, i=run),
+    )
+
+
+def tile_picked_nerfvol_none_po_kernel(
+    tc, x_words, x_scales, w1_words, w1_scales, w2, bg, w3_words, w3_scales, offs, p1, p2, out_0, out_1, out_2
+):
+    nc = tc.nc
+    with ExitStack() as ctx:
+        keep = ctx.enter_context(tc.tile_pool(name="keep", bufs=1))
+        psum_val = ctx.enter_context(tc.psum_pool(name="psum_val", bufs=4))
+        psum_s = ctx.enter_context(tc.psum_pool(name="psum_s", bufs=2))
+        psum_out = ctx.enter_context(tc.psum_pool(name="psum_out", bufs=2))
+
+        offs_sb = keep.tile([P, S // 16], U16, name="offs_sb")
+        p1_sb = keep.tile([P, V // 16], U16, name="p1_sb")
+        p2_sb = keep.tile([P, V // 16], U16, name="p2_sb")
+        xw = keep.tile([P, T], U32, name="xw", align_bytes=64)
+        xs = keep.tile([P, T], U8, name="xs", align_bytes=64)
+        w1w_raw = keep.tile([P, H], U32, name="w1w_raw", tag="stage_a", align_bytes=64)
+        ws_raw = keep.tile([P, H], U8, name="ws_raw", align_bytes=64)
+        w2_raw = [keep.tile([P, PACK, H // 2], F32, name=f"w2_raw{i}", tag=f"stage_b{i}", align_bytes=64) for i in range(2)]
+        warm_in = keep.tile([P, 1], F32, name="warm_in")
+        warm_out = keep.tile([P, 1], F32, name="warm_out")
+
+        nc.vector.memset(xs[:].bitcast(I32), 0)
+        nc.vector.memset(warm_in[:], 0.0)
+        nc.gpsimd.memset(ws_raw[:].bitcast(I32), 0)
+
+        w2_rows = w2.rearrange("(p j) c -> p j c", j=PACK)
+        nc.sync.dma_start(offs_sb[:], offs)
+        nc.sync.dma_start(p2_sb[:], p2)
+        nc.sync.dma_start(p1_sb[:], p1)
+        nc.sync.dma_start(out=w1w_raw[:].bitcast(I32), in_=words_i32(w1_words))
+        nc.sync.dma_start(out=xw[:].bitcast(I32), in_=words_i32(x_words))
+        load_scales(nc.scalar, xs, x_scales, X_ROW)
+        nc.scalar.activation(warm_out[:], warm_in[:], ACT.Exp)
+        nc.sync.dma_start(out=w2_raw[0][:], in_=w2_rows[:, :, 0 : H // 2])
+        nc.sync.dma_start(out=w2_raw[1][:], in_=w2_rows[:, :, H // 2 : H])
+        load_scales(nc.gpsimd, ws_raw, w1_scales, W1_ROW)
+
+        w1w = keep.tile([P, H], U32, name="w1w", tag="dealt_words", align_bytes=64)
+        deal(nc, w1w, w1w_raw, 4)
+        xg_w = keep.tile([P, S], U32, name="xg_w", align_bytes=64)
+        xg_s = keep.tile([P, S], U8, name="xg_s", align_bytes=64)
+        nc.vector.tensor_copy(xg_s[:], xs[:].indirect(offs_sb[:]))
+        for h in range(2):
+            nc.vector.tensor_copy(xg_w[:, h * 256 : (h + 1) * 256], xw[:].indirect(offs_sb[:, h * 16 : (h + 1) * 16]))
+
+        w1s = keep.tile([P, H], U8, name="w1s", tag="dealt_scales", align_bytes=64)
+        deal(nc, w1s, ws_raw, 16)
+        bg_sb = keep.tile([P, PACK, V], F32, name="bg_sb", tag="stage_a", align_bytes=64)
+        nc.sync.dma_start(out=bg_sb[:], in_=bg.rearrange("(p t) v -> p t v", t=PACK))
+
+        w2b = keep.tile([P, PACK, P, PACK], BF16, name="w2b", align_bytes=64)
+        for i, cast in enumerate((nc.scalar.copy, nc.vector.tensor_copy)):
+            cast(
+                out=w2b[:, :, i * 64 : (i + 1) * 64, :].rearrange("p t m j -> p m j t"),
+                in_=w2_raw[i][:].rearrange("p j (m t) -> p m j t", t=PACK),
+            )
+        w2w = keep.tile([P, H], U32, name="w2w", align_bytes=64)
+        w2s = keep.tile([P, H], U8, name="w2s", align_bytes=64)
+        for t0, t1 in ((0, 1), (1, 2), (2, 4)):
+            nc.vector.quantize_mx(
+                out=w2w[:, t0 * P : t1 * P].bitcast(FP8X4),
+                scales=w2s[:, t0 * P : t1 * P],
+                in_=w2b[:, t0:t1].rearrange("p t m j -> p (t m j)"),
+            )
+
+        w3w_raw = keep.tile([P, N], U32, name="w3w_raw", tag="stage_b0", align_bytes=64)
+        nc.sync.dma_start(out=w3w_raw[:].bitcast(I32), in_=words_i32(w3_words))
+        load_scales(nc.sync, ws_raw, w3_scales, W3_ROW)
+
+        def project(words, scales, row, t, pool):
+            bank = pool.tile([P, S], F32, name="bank")
+            for h in range(2):
+                cols = slice(h * 256, (h + 1) * 256)
+                nc.tensor.matmul_mx(
+                    out=bank[:, cols],
+                    lhsT=words[:, t * P : (t + 1) * P].bitcast(FP8X4),
+                    lhsT_scale=scales[row:P, t * P : (t + 1) * P],
+                    rhs=xg_w[:, cols].bitcast(FP8X4),
+                    rhs_scale=xg_s[X_ROW:P, cols],
+                    start=True,
+                    stop=True,
+                )
+            return bank
+
+        h_all = keep.tile([P, PACK, V], F32, name="h_all", align_bytes=64)
+        w_all = keep.tile([P, PACK, V], F32, name="w_all", align_bytes=64)
+        for pair in ((0, 1), (2, 3)):
+            val, dens, e1, e2, a, b, g = {}, {}, {}, {}, {}, {}, {}
+            for t in pair:
+                val[t] = keep.tile([P, S], F32, name=f"val{t}")
+                evacuate = nc.vector.tensor_copy if t == 0 else nc.scalar.copy
+                evacuate(val[t][:], project(w2w, w2s, 0, t, psum_val)[:])
+            for t in pair:
+                dens[t] = keep.tile([P, S], F32, name=f"dens{t}")
+                nc.scalar.activation(dens[t][:], project(w1w, w1s, W1_ROW, t, psum_s)[:], ACT.Relu)
+                e2[t] = keep.tile([P, V], F32, name=f"e2_{t}")
+                nc.scalar.activation(e2[t][:], dens[t][:].indirect(p2_sb[:]), ACT.Exp, scale=-1.0)
+            for t in pair:
+                e1[t] = keep.tile([P, V], F32, name=f"e1_{t}")
+                nc.scalar.activation(e1[t][:], dens[t][:].indirect(p1_sb[:]), ACT.Exp, scale=-1.0)
+            for t in pair:
+                a[t] = keep.tile([P, V], F32, name=f"a{t}")
+                nc.vector.tensor_tensor(a[t][:], val[t][:].indirect(p2_sb[:]), bg_sb[:, t, :], ALU.subtract)
+            for t in pair:
+                b[t] = keep.tile([P, V], F32, name=f"b{t}")
+                nc.vector.scalar_tensor_tensor(b[t][:], e2[t][:], 1.0, a[t][:], ALU.subtract, ALU.mult)
+            for t in pair:
+                nc.vector.tensor_tensor(h_all[:, t, :], bg_sb[:, t, :], b[t][:], ALU.subtract)
+            for t in pair:
+                g[t] = keep.tile([P, V], F32, name=f"g{t}")
+                nc.vector.tensor_tensor(g[t][:], val[t][:].indirect(p1_sb[:]), h_all[:, t, :], ALU.subtract)
+            for t in pair:
+                nc.vector.scalar_tensor_tensor(w_all[:, t, :], e1[t][:], 1.0, g[t][:], ALU.subtract, ALU.mult)
+
+
+        w3w = keep.tile([P, N], U32, name="w3w", tag="dealt_words", align_bytes=64)
+        deal(nc, w3w, w3w_raw, 4)
+        w3s = keep.tile([P, N], U8, name="w3s", tag="dealt_scales", align_bytes=64)
+        deal(nc, w3s, ws_raw, 16)
+        zw = keep.tile([P, V], U32, name="zw", align_bytes=64)
+        zs = keep.tile([P, V], U8, name="zs", align_bytes=64)
+        ow = keep.tile([P, V], U32, name="ow", align_bytes=64)
+        osc = keep.tile([P, V], U8, name="osc", align_bytes=64)
+        zb = [keep.tile([P, P, PACK], BF16, name=f"zb{h}", align_bytes=64) for h in range(2)]
+        ob = [keep.tile([P, P, PACK], BF16, name=f"ob{h}", align_bytes=64) for h in range(2)]
+        of = [keep.tile([P, PACK, P], F32, name=f"of{h}", align_bytes=64) for h in range(2)]
+        rays = [slice(h * P, (h + 1) * P) for h in range(2)]
+        for h in range(2):
+            nc.vector.tensor_tensor(
+                zb[h][:].rearrange("p (c i) t -> p c t i", i=4),
+                h_all[:, :, rays[h]].rearrange("p t (c i) -> p c t i", i=4),
+                w_all[:, :, rays[h]].rearrange("p t (c i) -> p c t i", i=4),
+                ALU.subtract,
+            )
+        banks = []
+        for h in range(2):
+            nc.vector.quantize_mx(
+                out=zw[:, rays[h]].bitcast(FP8X4), scales=zs[:, rays[h]], in_=zb[h][:].rearrange("p v t -> p (v t)")
+            )
+            bank = psum_out.tile([P, PACK, P], F32, name="out_bank")
+            for t in range(PACK):
+                nc.tensor.matmul_mx(
+                    out=bank[:, t, :],
+                    lhsT=w3w[:, t * P : (t + 1) * P].bitcast(FP8X4),
+                    lhsT_scale=w3s[W3_ROW:P, t * P : (t + 1) * P],
+                    rhs=zw[:, rays[h]].bitcast(FP8X4),
+                    rhs_scale=zs[:, rays[h]],
+                    start=True,
+                    stop=True,
+                )
+            banks.append(bank)
+        out_rows = out_0.rearrange("(p t) v -> p t v", t=PACK)
+        for h in range(2):
+            nc.vector.tensor_copy(out=ob[h][:], in_=banks[h][:].rearrange("p t v -> p v t"))
+            nc.scalar.copy(of[h][:], banks[h][:])
+            nc.sync.dma_start(out=out_rows[:, :, rays[h]], in_=of[h][:])
+        for h in range(2):
+            nc.vector.quantize_mx(
+                out=ow[:, rays[h]].bitcast(FP8X4), scales=osc[:, rays[h]], in_=ob[h][:].rearrange("p v t -> p (v t)")
+            )
+        nc.sync.dma_start(out=words_i32(out_1), in_=ow[:].bitcast(I32))
+        for q in range(4):
+            queue = nc.sync if q % 2 else nc.scalar
+            queue.dma_start(
+                out=out_2[0, 4 * q : 4 * q + 4, :].bitcast(I32), in_=osc[QUAD * q : QUAD * q + 4, :].bitcast(I32)
+            )

@@ -46,56 +46,55 @@ def tile_picked_nerfvol_none_po_kernel(
     nc = tc.nc
     with ExitStack() as ctx:
         keep = ctx.enter_context(tc.tile_pool(name="keep", bufs=1))
-        psum_val = ctx.enter_context(tc.psum_pool(name="psum_val", bufs=4))
-        psum_s = ctx.enter_context(tc.psum_pool(name="psum_s", bufs=2))
-        psum_out = ctx.enter_context(tc.psum_pool(name="psum_out", bufs=2))
+        psum = ctx.enter_context(tc.psum_pool(name="psum", bufs=1))
 
         offs_sb = keep.tile([P, S // 16], U16, name="offs_sb")
         p1_sb = keep.tile([P, V // 16], U16, name="p1_sb")
         p2_sb = keep.tile([P, V // 16], U16, name="p2_sb")
-        xw = keep.tile([P, T], U32, name="xw", align_bytes=64)
-        xs = keep.tile([P, T], U8, name="xs", align_bytes=64)
-        w1w_raw = keep.tile([P, H], U32, name="w1w_raw", tag="stage_a", align_bytes=64)
+        xw = keep.tile([P, T], U32, name="xw", tag="xw", align_bytes=64)
+        xs = keep.tile([P, T], U8, name="xs", tag="xs", align_bytes=64)
+        w1w_raw = keep.tile([P, H], U32, name="w1w_raw", align_bytes=64)
         ws_raw = keep.tile([P, H], U8, name="ws_raw", align_bytes=64)
-        w2_raw = [keep.tile([P, PACK, H // 2], F32, name=f"w2_raw{i}", tag=f"stage_b{i}", align_bytes=64) for i in range(2)]
-        warm_in = keep.tile([P, 1], F32, name="warm_in")
-        warm_out = keep.tile([P, 1], F32, name="warm_out")
+        warm_out = keep.tile([P, 1], F32, name="warm_out", tag="w2_raw", align_bytes=64)
 
+        nc.vector.memset(ws_raw[:].bitcast(I32), 0)
         nc.vector.memset(xs[:].bitcast(I32), 0)
-        nc.vector.memset(warm_in[:], 0.0)
-        nc.gpsimd.memset(ws_raw[:].bitcast(I32), 0)
+        nc.scalar.activation(warm_out[:], ws_raw[:, 0:4].bitcast(F32), ACT.Exp)
 
+        w2_raw = keep.tile([P, 2, PACK, H // 2], F32, name="w2_raw", tag="w2_raw", align_bytes=64)
         w2_rows = w2.rearrange("(p j) c -> p j c", j=PACK)
         nc.sync.dma_start(offs_sb[:], offs)
         nc.sync.dma_start(p2_sb[:], p2)
         nc.sync.dma_start(p1_sb[:], p1)
         nc.sync.dma_start(out=w1w_raw[:].bitcast(I32), in_=words_i32(w1_words))
         nc.sync.dma_start(out=xw[:].bitcast(I32), in_=words_i32(x_words))
-        load_scales(nc.scalar, xs, x_scales, X_ROW)
-        nc.scalar.activation(warm_out[:], warm_in[:], ACT.Exp)
-        nc.sync.dma_start(out=w2_raw[0][:], in_=w2_rows[:, :, 0 : H // 2])
-        nc.sync.dma_start(out=w2_raw[1][:], in_=w2_rows[:, :, H // 2 : H])
-        load_scales(nc.gpsimd, ws_raw, w1_scales, W1_ROW)
+        load_scales(nc.sync, xs, x_scales, X_ROW)
+        nc.sync.dma_start(out=w2_raw[:, 0], in_=w2_rows[:, :, 0 : H // 2])
+        nc.sync.dma_start(out=w2_raw[:, 1], in_=w2_rows[:, :, H // 2 : H])
+        load_scales(nc.sync, ws_raw, w1_scales, W1_ROW)
 
-        w1w = keep.tile([P, H], U32, name="w1w", tag="dealt_words", align_bytes=64)
+        w1w = keep.tile([P, H], U32, name="w1w", align_bytes=64)
         deal(nc, w1w, w1w_raw, 4)
         xg_w = keep.tile([P, S], U32, name="xg_w", align_bytes=64)
         xg_s = keep.tile([P, S], U8, name="xg_s", align_bytes=64)
+        nc.vector.tensor_copy(xg_w[:], xw[:].indirect(offs_sb[:]))
         nc.vector.tensor_copy(xg_s[:], xs[:].indirect(offs_sb[:]))
-        for h in range(2):
-            nc.vector.tensor_copy(xg_w[:, h * 256 : (h + 1) * 256], xw[:].indirect(offs_sb[:, h * 16 : (h + 1) * 16]))
 
-        w1s = keep.tile([P, H], U8, name="w1s", tag="dealt_scales", align_bytes=64)
-        deal(nc, w1s, ws_raw, 16)
-        bg_sb = keep.tile([P, PACK, V], F32, name="bg_sb", tag="stage_a", align_bytes=64)
-        nc.sync.dma_start(out=bg_sb[:], in_=bg.rearrange("(p t) v -> p t v", t=PACK))
+        w3w_raw = keep.tile([P, N], U32, name="w3w_raw", tag="xw", align_bytes=64)
+        nc.sync.dma_start(out=w3w_raw[:].bitcast(I32), in_=words_i32(w3_words))
+        bg_sb = keep.tile([P, PACK, V], F32, name="bg_sb", tag="xs", align_bytes=64)
+        bg_rows = bg.rearrange("(p t) v -> p t v", t=PACK)
+        for pair in (slice(0, 2), slice(2, 4)):
+            nc.sync.dma_start(out=bg_sb[:, pair, :], in_=bg_rows[:, pair, :])
 
         w2b = keep.tile([P, PACK, P, PACK], BF16, name="w2b", align_bytes=64)
         for i, cast in enumerate((nc.scalar.copy, nc.vector.tensor_copy)):
             cast(
                 out=w2b[:, :, i * 64 : (i + 1) * 64, :].rearrange("p t m j -> p m j t"),
-                in_=w2_raw[i][:].rearrange("p j (m t) -> p m j t", t=PACK),
+                in_=w2_raw[:, i].rearrange("p j (m t) -> p m j t", t=PACK),
             )
+        w1s = keep.tile([P, H], U8, name="w1s", tag="w2_raw", align_bytes=64)
+        deal(nc, w1s, ws_raw, 16)
         w2w = keep.tile([P, H], U32, name="w2w", align_bytes=64)
         w2s = keep.tile([P, H], U8, name="w2s", align_bytes=64)
         for t0, t1 in ((0, 1), (1, 2), (2, 4)):
@@ -105,36 +104,34 @@ def tile_picked_nerfvol_none_po_kernel(
                 in_=w2b[:, t0:t1].rearrange("p t m j -> p (t m j)"),
             )
 
-        w3w_raw = keep.tile([P, N], U32, name="w3w_raw", tag="stage_b0", align_bytes=64)
-        nc.sync.dma_start(out=w3w_raw[:].bitcast(I32), in_=words_i32(w3_words))
         load_scales(nc.sync, ws_raw, w3_scales, W3_ROW)
+        w3w = keep.tile([P, N], U32, name="w3w", align_bytes=64)
+        deal(nc, w3w, w3w_raw, 4)
 
-        def project(words, scales, row, t, pool):
-            bank = pool.tile([P, S], F32, name="bank")
-            for h in range(2):
-                cols = slice(h * 256, (h + 1) * 256)
-                nc.tensor.matmul_mx(
-                    out=bank[:, cols],
-                    lhsT=words[:, t * P : (t + 1) * P].bitcast(FP8X4),
-                    lhsT_scale=scales[row:P, t * P : (t + 1) * P],
-                    rhs=xg_w[:, cols].bitcast(FP8X4),
-                    rhs_scale=xg_s[X_ROW:P, cols],
-                    start=True,
-                    stop=True,
-                )
+        def project(words, scales, row, t, bank_no):
+            bank = psum.tile([P, S], F32, name="bank", tag=f"bank{bank_no}")
+            nc.tensor.matmul_mx(
+                out=bank[:],
+                lhsT=words[:, t * P : (t + 1) * P].bitcast(FP8X4),
+                lhsT_scale=scales[row:P, t * P : (t + 1) * P],
+                rhs=xg_w[:].bitcast(FP8X4),
+                rhs_scale=xg_s[X_ROW:P, :],
+                start=True,
+                stop=True,
+            )
             return bank
 
         h_all = keep.tile([P, PACK, V], F32, name="h_all", align_bytes=64)
         w_all = keep.tile([P, PACK, V], F32, name="w_all", align_bytes=64)
+        val, dens, e1, e2, a, b, g = {}, {}, {}, {}, {}, {}, {}
+
         for pair in ((0, 1), (2, 3)):
-            val, dens, e1, e2, a, b, g = {}, {}, {}, {}, {}, {}, {}
-            for t in pair:
-                val[t] = keep.tile([P, S], F32, name=f"val{t}")
-                evacuate = nc.vector.tensor_copy if t == 0 else nc.scalar.copy
-                evacuate(val[t][:], project(w2w, w2s, 0, t, psum_val)[:])
             for t in pair:
                 dens[t] = keep.tile([P, S], F32, name=f"dens{t}")
-                nc.scalar.activation(dens[t][:], project(w1w, w1s, W1_ROW, t, psum_s)[:], ACT.Relu)
+                nc.scalar.activation(dens[t][:], project(w1w, w1s, W1_ROW, t, t)[:], ACT.Relu)
+                val[t] = keep.tile([P, S], F32, name=f"val{t}")
+                copy_out = nc.vector.tensor_copy if t == 0 else nc.scalar.copy
+                copy_out(val[t][:], project(w2w, w2s, 0, t, t + 1)[:])
                 e2[t] = keep.tile([P, V], F32, name=f"e2_{t}")
                 nc.scalar.activation(e2[t][:], dens[t][:].indirect(p2_sb[:]), ACT.Exp, scale=-1.0)
             for t in pair:
@@ -144,7 +141,7 @@ def tile_picked_nerfvol_none_po_kernel(
                 a[t] = keep.tile([P, V], F32, name=f"a{t}")
                 nc.vector.tensor_tensor(a[t][:], val[t][:].indirect(p2_sb[:]), bg_sb[:, t, :], ALU.subtract)
             for t in pair:
-                b[t] = keep.tile([P, V], F32, name=f"b{t}")
+                b[t] = keep.tile([P, V], F32, name=f"b{t}", tag=f"b{t}", align_bytes=64)
                 nc.vector.scalar_tensor_tensor(b[t][:], e2[t][:], 1.0, a[t][:], ALU.subtract, ALU.mult)
             for t in pair:
                 nc.vector.tensor_tensor(h_all[:, t, :], bg_sb[:, t, :], b[t][:], ALU.subtract)
@@ -154,10 +151,7 @@ def tile_picked_nerfvol_none_po_kernel(
             for t in pair:
                 nc.vector.scalar_tensor_tensor(w_all[:, t, :], e1[t][:], 1.0, g[t][:], ALU.subtract, ALU.mult)
 
-
-        w3w = keep.tile([P, N], U32, name="w3w", tag="dealt_words", align_bytes=64)
-        deal(nc, w3w, w3w_raw, 4)
-        w3s = keep.tile([P, N], U8, name="w3s", tag="dealt_scales", align_bytes=64)
+        w3s = keep.tile([P, N], U8, name="w3s", tag="b1", align_bytes=64)
         deal(nc, w3s, ws_raw, 16)
         zw = keep.tile([P, V], U32, name="zw", align_bytes=64)
         zs = keep.tile([P, V], U8, name="zs", align_bytes=64)
@@ -179,7 +173,7 @@ def tile_picked_nerfvol_none_po_kernel(
             nc.vector.quantize_mx(
                 out=zw[:, rays[h]].bitcast(FP8X4), scales=zs[:, rays[h]], in_=zb[h][:].rearrange("p v t -> p (v t)")
             )
-            bank = psum_out.tile([P, PACK, P], F32, name="out_bank")
+            bank = psum.tile([P, PACK, P], F32, name="out_bank", tag=f"bank{5 + h}")
             for t in range(PACK):
                 nc.tensor.matmul_mx(
                     out=bank[:, t, :],
@@ -192,15 +186,18 @@ def tile_picked_nerfvol_none_po_kernel(
                 )
             banks.append(bank)
         out_rows = out_0.rearrange("(p t) v -> p t v", t=PACK)
-        for h in range(2):
-            nc.vector.tensor_copy(out=ob[h][:], in_=banks[h][:].rearrange("p t v -> p v t"))
+        out_words = words_i32(out_1)
+        for h, queue in enumerate((nc.sync, nc.scalar)):
             nc.scalar.copy(of[h][:], banks[h][:])
-            nc.sync.dma_start(out=out_rows[:, :, rays[h]], in_=of[h][:])
-        for h in range(2):
+            queue.dma_start(out=out_rows[:, :, rays[h]], in_=of[h][:])
+            nc.vector.tensor_copy(
+                out=ob[h][:].rearrange("p (c i) t -> p c t i", i=4),
+                in_=of[h][:].rearrange("p t (c i) -> p c t i", i=4),
+            )
             nc.vector.quantize_mx(
                 out=ow[:, rays[h]].bitcast(FP8X4), scales=osc[:, rays[h]], in_=ob[h][:].rearrange("p v t -> p (v t)")
             )
-        nc.sync.dma_start(out=words_i32(out_1), in_=ow[:].bitcast(I32))
+            nc.sync.dma_start(out=out_words[:, rays[h]], in_=ow[:, rays[h]].bitcast(I32))
         for q in range(4):
             queue = nc.sync if q % 2 else nc.scalar
             queue.dma_start(

@@ -46,74 +46,94 @@ def tile_picked_nerfvol_none_po_kernel(
     nc = tc.nc
     with ExitStack() as ctx:
         keep = ctx.enter_context(tc.tile_pool(name="keep", bufs=1))
+        stage = ctx.enter_context(tc.tile_pool(name="stage", bufs=1))
         psum = ctx.enter_context(tc.psum_pool(name="psum", bufs=1))
 
         offs_sb = keep.tile([P, S // 16], U16, name="offs_sb")
         p1_sb = keep.tile([P, V // 16], U16, name="p1_sb")
         p2_sb = keep.tile([P, V // 16], U16, name="p2_sb")
-        xw = keep.tile([P, T], U32, name="xw", tag="xw", align_bytes=64)
+        xw = stage.tile([P, T], U32, name="xw", offset=10240)
         xs = keep.tile([P, T], U8, name="xs", tag="xs", align_bytes=64)
-        w1w_raw = keep.tile([P, H], U32, name="w1w_raw", align_bytes=64)
-        ws_raw = keep.tile([P, H], U8, name="ws_raw", align_bytes=64)
-        warm_out = keep.tile([P, 1], F32, name="warm_out", tag="w2_raw", align_bytes=64)
-
-        nc.vector.memset(ws_raw[:].bitcast(I32), 0)
+        ws_raw = stage.tile([P, H], U8, name="ws_raw", offset=20480, align_bytes=64)
+        warm_out = stage.tile([P, 16], F32, name="warm_out", offset=2048 - 32)
         nc.vector.memset(xs[:].bitcast(I32), 0)
-        nc.scalar.activation(warm_out[:], ws_raw[:, 0:4].bitcast(F32), ACT.Exp)
+        nc.gpsimd.memset(ws_raw[:].bitcast(I32), 0)
+        nc.scalar.activation(warm_out[:], ws_raw[:, 0:64].bitcast(F32), ACT.Exp)
 
-        w2_raw = keep.tile([P, 2, PACK, H // 2], F32, name="w2_raw", tag="w2_raw", align_bytes=64)
-        w2_rows = w2.rearrange("(p j) c -> p j c", j=PACK)
         nc.sync.dma_start(offs_sb[:], offs)
         nc.sync.dma_start(p2_sb[:], p2)
         nc.sync.dma_start(p1_sb[:], p1)
-        nc.sync.dma_start(out=w1w_raw[:].bitcast(I32), in_=words_i32(w1_words))
         nc.sync.dma_start(out=xw[:].bitcast(I32), in_=words_i32(x_words))
         load_scales(nc.sync, xs, x_scales, X_ROW)
-        nc.sync.dma_start(out=w2_raw[:, 0], in_=w2_rows[:, :, 0 : H // 2])
-        nc.sync.dma_start(out=w2_raw[:, 1], in_=w2_rows[:, :, H // 2 : H])
+        w1w_raw = stage.tile([P, H], U32, name="w1w_raw", offset=0)
+        nc.sync.dma_start(out=w1w_raw[:].bitcast(I32), in_=words_i32(w1_words))
+        w2_raw = stage.tile([P, 2, PACK, H // 2], F32, name="w2_raw", offset=2048)
+        w2_rows = w2.rearrange("(p j) c -> p j c", j=PACK)
+        for i in range(2):
+            nc.sync.dma_start(out=w2_raw[:, i], in_=w2_rows[:, :, i * 256 : (i + 1) * 256])
         load_scales(nc.sync, ws_raw, w1_scales, W1_ROW)
 
+        xg_w = keep.tile([P, S], U32, name="xg_w", align_bytes=64)
+        nc.vector.tensor_copy(xg_w[:], xw[:].indirect(offs_sb[:]))
+        xg_s = keep.tile([P, S], U8, name="xg_s", align_bytes=64)
+        nc.vector.tensor_copy(xg_s[:], xs[:].indirect(offs_sb[:]))
         w1w = keep.tile([P, H], U32, name="w1w", align_bytes=64)
         deal(nc, w1w, w1w_raw, 4)
-        xg_w = keep.tile([P, S], U32, name="xg_w", align_bytes=64)
-        xg_s = keep.tile([P, S], U8, name="xg_s", align_bytes=64)
-        nc.vector.tensor_copy(xg_w[:], xw[:].indirect(offs_sb[:]))
-        nc.vector.tensor_copy(xg_s[:], xs[:].indirect(offs_sb[:]))
+        w1s = keep.tile([P, H], U8, name="w1s", align_bytes=64)
+        dealt = w1s[:].rearrange("p (t c i) -> p c t i", t=PACK, i=16)
+        raw = ws_raw[:].rearrange("p (c i t) -> p c t i", t=PACK, i=16)
+        for t0, t1 in ((0, 1), (1, PACK)):
+            nc.vector.tensor_copy(out=dealt[:, :, t0:t1, :], in_=raw[:, :, t0:t1, :])
 
-        w3w_raw = keep.tile([P, N], U32, name="w3w_raw", tag="xw", align_bytes=64)
-        nc.sync.dma_start(out=w3w_raw[:].bitcast(I32), in_=words_i32(w3_words))
-        bg_sb = keep.tile([P, PACK, V], F32, name="bg_sb", tag="xs", align_bytes=64)
+        bg_sb = stage.tile([P, PACK, V], F32, name="bg_sb", offset=10240)
         bg_rows = bg.rearrange("(p t) v -> p t v", t=PACK)
-        for pair in (slice(0, 2), slice(2, 4)):
-            nc.sync.dma_start(out=bg_sb[:, pair, :], in_=bg_rows[:, pair, :])
+        nc.sync.dma_start(out=bg_sb[:, 0:2, :], in_=bg_rows[:, 0:2, :])
+        w3w_raw = stage.tile([P, N], U32, name="w3w_raw", offset=10240 + 4096)
+        nc.sync.dma_start(out=w3w_raw[:].bitcast(I32), in_=words_i32(w3_words))
+        nc.sync.dma_start(out=bg_sb[:, 2:4, :], in_=bg_rows[:, 2:4, :])
+        w3s_raw = stage.tile([P, N], U8, name="w3s_raw", offset=10240 + 6144)
+        nc.gpsimd.memset(w3s_raw[:].bitcast(I32), 0)
+        load_scales(nc.sync, w3s_raw, w3_scales, W3_ROW)
 
-        w2b = keep.tile([P, PACK, P, PACK], BF16, name="w2b", align_bytes=64)
-        for i, cast in enumerate((nc.scalar.copy, nc.vector.tensor_copy)):
-            cast(
-                out=w2b[:, :, i * 64 : (i + 1) * 64, :].rearrange("p t m j -> p m j t"),
-                in_=w2_raw[:, i].rearrange("p j (m t) -> p m j t", t=PACK),
-            )
-        w1s = keep.tile([P, H], U8, name="w1s", tag="w2_raw", align_bytes=64)
-        deal(nc, w1s, ws_raw, 16)
         w2w = keep.tile([P, H], U32, name="w2w", align_bytes=64)
-        w2s = keep.tile([P, H], U8, name="w2s", align_bytes=64)
-        for t0, t1 in ((0, 1), (1, 2), (2, 4)):
-            nc.vector.quantize_mx(
-                out=w2w[:, t0 * P : t1 * P].bitcast(FP8X4),
-                scales=w2s[:, t0 * P : t1 * P],
-                in_=w2b[:, t0:t1].rearrange("p t m j -> p (t m j)"),
+        w2s = [
+            stage.tile([P, 2 * P], U8, name="w2s0", offset=20480 - 192, align_bytes=64),
+            stage.tile([P, 2 * P], U8, name="w2s1", offset=20480 + 64, align_bytes=64),
+        ]
+        w2b = [keep.tile([P, 2, P, PACK], BF16, name=f"w2b{i}", align_bytes=64) for i in range(2)]
+
+        def cast_w2(copy, half, pair):
+            copy(
+                out=w2b[pair][:, :, 64 * half : 64 * (half + 1), :].rearrange("p t m j -> p m j t"),
+                in_=w2_raw[:, half].rearrange("p j (m t) -> p m j t", t=PACK)[:, :, :, 2 * pair : 2 * pair + 2],
             )
 
-        load_scales(nc.sync, ws_raw, w3_scales, W3_ROW)
-        w3w = keep.tile([P, N], U32, name="w3w", align_bytes=64)
-        deal(nc, w3w, w3w_raw, 4)
+        def quantise_w2(t0, t1):
+            pair, u0, u1 = t0 // 2, t0 % 2, (t1 - 1) % 2 + 1
+            nc.vector.quantize_mx(
+                out=w2w[:, P * t0 : P * t1].bitcast(FP8X4),
+                scales=w2s[pair][:, P * u0 : P * u1],
+                in_=w2b[pair][:, u0:u1].rearrange("p t m j -> p (t m j)"),
+            )
 
-        def project(words, scales, row, t, bank_no):
+        cast_w2(nc.scalar.copy, 0, 0)
+        cast_w2(nc.scalar.copy, 0, 1)
+        cast_w2(nc.scalar.copy, 1, 0)
+        cast_w2(nc.scalar.copy, 1, 1)
+        quantise_w2(0, 1)
+        quantise_w2(1, 2)
+        quantise_w2(2, 4)
+        w3w = stage.tile([P, N], U32, name="w3w", offset=20480 + 320, align_bytes=64)
+        deal(nc, w3w, w3w_raw, 4)
+        w3s = keep.tile([P, N], U8, name="w3s", align_bytes=64)
+        deal(nc, w3s, w3s_raw, 16)
+
+        def project(words, scales, t, bank_no):
             bank = psum.tile([P, S], F32, name="bank", tag=f"bank{bank_no}")
             nc.tensor.matmul_mx(
                 out=bank[:],
                 lhsT=words[:, t * P : (t + 1) * P].bitcast(FP8X4),
-                lhsT_scale=scales[row:P, t * P : (t + 1) * P],
+                lhsT_scale=scales,
                 rhs=xg_w[:].bitcast(FP8X4),
                 rhs_scale=xg_s[X_ROW:P, :],
                 start=True,
@@ -125,34 +145,67 @@ def tile_picked_nerfvol_none_po_kernel(
         w_all = keep.tile([P, PACK, V], F32, name="w_all", align_bytes=64)
         val, dens, e1, e2, a, b, g = {}, {}, {}, {}, {}, {}, {}
 
-        for pair in ((0, 1), (2, 3)):
-            for t in pair:
-                dens[t] = keep.tile([P, S], F32, name=f"dens{t}")
-                nc.scalar.activation(dens[t][:], project(w1w, w1s, W1_ROW, t, t)[:], ACT.Relu)
-                val[t] = keep.tile([P, S], F32, name=f"val{t}")
-                copy_out = nc.vector.tensor_copy if t == 0 else nc.scalar.copy
-                copy_out(val[t][:], project(w2w, w2s, 0, t, t + 1)[:])
-                e2[t] = keep.tile([P, V], F32, name=f"e2_{t}")
-                nc.scalar.activation(e2[t][:], dens[t][:].indirect(p2_sb[:]), ACT.Exp, scale=-1.0)
-            for t in pair:
-                e1[t] = keep.tile([P, V], F32, name=f"e1_{t}")
-                nc.scalar.activation(e1[t][:], dens[t][:].indirect(p1_sb[:]), ACT.Exp, scale=-1.0)
-            for t in pair:
-                a[t] = keep.tile([P, V], F32, name=f"a{t}")
-                nc.vector.tensor_tensor(a[t][:], val[t][:].indirect(p2_sb[:]), bg_sb[:, t, :], ALU.subtract)
-            for t in pair:
-                b[t] = keep.tile([P, V], F32, name=f"b{t}", tag=f"b{t}", align_bytes=64)
-                nc.vector.scalar_tensor_tensor(b[t][:], e2[t][:], 1.0, a[t][:], ALU.subtract, ALU.mult)
-            for t in pair:
-                nc.vector.tensor_tensor(h_all[:, t, :], bg_sb[:, t, :], b[t][:], ALU.subtract)
-            for t in pair:
-                g[t] = keep.tile([P, V], F32, name=f"g{t}")
-                nc.vector.tensor_tensor(g[t][:], val[t][:].indirect(p1_sb[:]), h_all[:, t, :], ALU.subtract)
-            for t in pair:
-                nc.vector.scalar_tensor_tensor(w_all[:, t, :], e1[t][:], 1.0, g[t][:], ALU.subtract, ALU.mult)
+        def evacuate_val(t):
+            val[t] = keep.tile([P, S], F32, name=f"val{t}")
+            copy_out = nc.vector.tensor_copy if t == 0 else nc.scalar.copy
+            copy_out(val[t][:], project(w2w, w2s[t // 2][:, (t % 2) * P : (t % 2 + 1) * P], t, (2 * t + 1) % 3)[:])
 
-        w3s = keep.tile([P, N], U8, name="w3s", tag="b1", align_bytes=64)
-        deal(nc, w3s, ws_raw, 16)
+        def evacuate_dens(t):
+            dens[t] = keep.tile([P, S], F32, name=f"dens{t}")
+            nc.scalar.activation(dens[t][:], project(w1w, w1s[W1_ROW:P, t * P : (t + 1) * P], t, (2 * t) % 3)[:], ACT.Relu)
+
+        def through(store, lists, t, name):
+            store[t] = keep.tile([P, V], F32, name=f"{name}_{t}", tag=f"{name}_{t}", align_bytes=64)
+            nc.scalar.activation(store[t][:], dens[t][:].indirect(lists[:]), ACT.Exp, scale=-1.0)
+
+        def far_diff(t):
+            a[t] = keep.tile([P, V], F32, name=f"a{t}", tag=f"a{t}", align_bytes=64)
+            nc.vector.tensor_tensor(a[t][:], val[t][:].indirect(p2_sb[:]), bg_sb[:, t, :], ALU.subtract)
+
+        def far_weigh(t):
+            b[t] = keep.tile([P, V], F32, name=f"b{t}", tag=f"b{t}", align_bytes=64)
+            nc.vector.scalar_tensor_tensor(b[t][:], e2[t][:], 1.0, a[t][:], ALU.subtract, ALU.mult)
+
+        def far_blend(t):
+            nc.vector.tensor_tensor(h_all[:, t, :], bg_sb[:, t, :], b[t][:], ALU.subtract)
+
+        def near_diff(t):
+            g[t] = keep.tile([P, V], F32, name=f"g{t}")
+            nc.vector.tensor_tensor(g[t][:], val[t][:].indirect(p1_sb[:]), h_all[:, t, :], ALU.subtract)
+
+        def near_blend(t):
+            nc.vector.scalar_tensor_tensor(w_all[:, t, :], e1[t][:], 1.0, g[t][:], ALU.subtract, ALU.mult)
+
+        evacuate_dens(0)
+        evacuate_val(0)
+        evacuate_dens(1)
+        through(e2, p2_sb, 0, "e2")
+        evacuate_val(1)
+        through(e2, p2_sb, 1, "e2")
+        far_diff(0)
+        far_weigh(0)
+        far_diff(1)
+        far_blend(0)
+        far_weigh(1)
+        near_diff(0)
+        far_blend(1)
+        for t in (2, 3):
+            evacuate_dens(t)
+            evacuate_val(t)
+        far_diff(2)
+        near_diff(1)
+        for t in (2, 3):
+            through(e1, p1_sb, t - 2, "e1")
+            through(e2, p2_sb, t, "e2")
+        near_blend(0)
+        far_diff(3)
+        near_blend(1)
+        for t in (2, 3):
+            through(e1, p1_sb, t, "e1")
+        for step in (far_weigh, far_blend, near_diff, near_blend):
+            for t in (2, 3):
+                step(t)
+
         zw = keep.tile([P, V], U32, name="zw", align_bytes=64)
         zs = keep.tile([P, V], U8, name="zs", align_bytes=64)
         ow = keep.tile([P, V], U32, name="ow", align_bytes=64)
@@ -173,7 +226,7 @@ def tile_picked_nerfvol_none_po_kernel(
             nc.vector.quantize_mx(
                 out=zw[:, rays[h]].bitcast(FP8X4), scales=zs[:, rays[h]], in_=zb[h][:].rearrange("p v t -> p (v t)")
             )
-            bank = psum.tile([P, PACK, P], F32, name="out_bank", tag=f"bank{5 + h}")
+            bank = psum.tile([P, PACK, P], F32, name="out_bank", tag=f"bank{6 + h}")
             for t in range(PACK):
                 nc.tensor.matmul_mx(
                     out=bank[:, t, :],

@@ -26,15 +26,15 @@ def words_i32(ap):
 
 
 def load_scales(queue, plane, scales, row):
-    for q in range(4):
+    for r in range(4):
         queue.dma_start(
-            out=plane[QUAD * q + row : QUAD * q + row + 4, :].bitcast(I32),
-            in_=scales[0, 4 * q : 4 * q + 4, :].bitcast(I32),
+            out=plane[:].bitcast(I32)[row + r : P : QUAD, :],
+            in_=scales[0].bitcast(I32)[r:16:4, :],
         )
 
 
-def deal(nc, dst, src, run):
-    nc.vector.tensor_copy(
+def deal(engine, dst, src, run):
+    engine.tensor_copy(
         out=dst[:].rearrange("p (t c i) -> p c t i", t=PACK, i=run),
         in_=src[:].rearrange("p (c i t) -> p c t i", t=PACK, i=run),
     )
@@ -69,21 +69,18 @@ def tile_picked_nerfvol_none_po_kernel(
         nc.sync.dma_start(out=w1w_raw[:].bitcast(I32), in_=words_i32(w1_words))
         w2_raw = stage.tile([P, 2, PACK, H // 2], F32, name="w2_raw", offset=2048)
         w2_rows = w2.rearrange("(p j) c -> p j c", j=PACK)
-        for i in range(2):
-            nc.sync.dma_start(out=w2_raw[:, i], in_=w2_rows[:, :, i * 256 : (i + 1) * 256])
+        nc.sync.dma_start(out=w2_raw[:, 0], in_=w2_rows[:, :, 0:256])
         load_scales(nc.sync, ws_raw, w1_scales, W1_ROW)
+        nc.sync.dma_start(out=w2_raw[:, 1], in_=w2_rows[:, :, 256:512])
 
         xg_w = keep.tile([P, S], U32, name="xg_w", align_bytes=64)
         nc.vector.tensor_copy(xg_w[:], xw[:].indirect(offs_sb[:]))
         xg_s = keep.tile([P, S], U8, name="xg_s", align_bytes=64)
         nc.vector.tensor_copy(xg_s[:], xs[:].indirect(offs_sb[:]))
         w1w = keep.tile([P, H], U32, name="w1w", align_bytes=64)
-        deal(nc, w1w, w1w_raw, 4)
+        deal(nc.gpsimd, w1w, w1w_raw, 4)
         w1s = keep.tile([P, H], U8, name="w1s", align_bytes=64)
-        dealt = w1s[:].rearrange("p (t c i) -> p c t i", t=PACK, i=16)
-        raw = ws_raw[:].rearrange("p (c i t) -> p c t i", t=PACK, i=16)
-        for t0, t1 in ((0, 1), (1, PACK)):
-            nc.vector.tensor_copy(out=dealt[:, :, t0:t1, :], in_=raw[:, :, t0:t1, :])
+        deal(nc.vector, w1s, ws_raw, 16)
 
         bg_sb = stage.tile([P, PACK, V], F32, name="bg_sb", offset=10240)
         bg_rows = bg.rearrange("(p t) v -> p t v", t=PACK)
@@ -118,15 +115,15 @@ def tile_picked_nerfvol_none_po_kernel(
 
         cast_w2(nc.scalar.copy, 0, 0)
         cast_w2(nc.scalar.copy, 0, 1)
-        cast_w2(nc.scalar.copy, 1, 0)
-        cast_w2(nc.scalar.copy, 1, 1)
+        cast_w2(nc.vector.tensor_copy, 1, 0)
+        cast_w2(nc.vector.tensor_copy, 1, 1)
         quantise_w2(0, 1)
         quantise_w2(1, 2)
         quantise_w2(2, 4)
         w3w = stage.tile([P, N], U32, name="w3w", offset=20480 + 320, align_bytes=64)
-        deal(nc, w3w, w3w_raw, 4)
+        deal(nc.gpsimd, w3w, w3w_raw, 4)
         w3s = keep.tile([P, N], U8, name="w3s", align_bytes=64)
-        deal(nc, w3s, w3s_raw, 16)
+        deal(nc.gpsimd, w3s, w3s_raw, 16)
 
         def project(words, scales, t, bank_no):
             bank = psum.tile([P, S], F32, name="bank", tag=f"bank{bank_no}")
@@ -145,17 +142,22 @@ def tile_picked_nerfvol_none_po_kernel(
         w_all = keep.tile([P, PACK, V], F32, name="w_all", align_bytes=64)
         val, dens, e1, e2, a, b, g = {}, {}, {}, {}, {}, {}, {}
 
+        e1_first = stage.tile([P, 2, V], F32, name="e1_first", offset=20320 - 2048)
+
         def evacuate_val(t):
             val[t] = keep.tile([P, S], F32, name=f"val{t}")
-            copy_out = nc.vector.tensor_copy if t == 0 else nc.scalar.copy
-            copy_out(val[t][:], project(w2w, w2s[t // 2][:, (t % 2) * P : (t % 2 + 1) * P], t, (2 * t + 1) % 3)[:])
+            copy_out = nc.vector.tensor_copy if t < 2 else nc.scalar.copy
+            copy_out(val[t][:], project(w2w, w2s[t // 2][:, (t % 2) * P : (t % 2 + 1) * P], t, (t + 2) % 4)[:])
 
         def evacuate_dens(t):
             dens[t] = keep.tile([P, S], F32, name=f"dens{t}")
-            nc.scalar.activation(dens[t][:], project(w1w, w1s[W1_ROW:P, t * P : (t + 1) * P], t, (2 * t) % 3)[:], ACT.Relu)
+            nc.scalar.activation(dens[t][:], project(w1w, w1s[W1_ROW:P, t * P : (t + 1) * P], t, t)[:], ACT.Relu)
 
         def through(store, lists, t, name):
-            store[t] = keep.tile([P, V], F32, name=f"{name}_{t}", tag=f"{name}_{t}", align_bytes=64)
+            if name == "e1" and t < 2:
+                store[t] = e1_first[:, t, :]
+            else:
+                store[t] = keep.tile([P, V], F32, name=f"{name}_{t}", tag=f"{name}_{t}", align_bytes=64)
             nc.scalar.activation(store[t][:], dens[t][:].indirect(lists[:]), ACT.Exp, scale=-1.0)
 
         def far_diff(t):
@@ -177,18 +179,18 @@ def tile_picked_nerfvol_none_po_kernel(
             nc.vector.scalar_tensor_tensor(w_all[:, t, :], e1[t][:], 1.0, g[t][:], ALU.subtract, ALU.mult)
 
         evacuate_dens(0)
-        evacuate_val(0)
         evacuate_dens(1)
         through(e2, p2_sb, 0, "e2")
+        evacuate_val(0)
         evacuate_val(1)
         through(e2, p2_sb, 1, "e2")
         far_diff(0)
-        far_weigh(0)
         far_diff(1)
-        far_blend(0)
+        far_weigh(0)
         far_weigh(1)
-        near_diff(0)
+        far_blend(0)
         far_blend(1)
+        near_diff(0)
         for t in (2, 3):
             evacuate_dens(t)
             evacuate_val(t)
@@ -253,6 +255,4 @@ def tile_picked_nerfvol_none_po_kernel(
             nc.sync.dma_start(out=out_words[:, rays[h]], in_=ow[:, rays[h]].bitcast(I32))
         for q in range(4):
             queue = nc.sync if q % 2 else nc.scalar
-            queue.dma_start(
-                out=out_2[0, 4 * q : 4 * q + 4, :].bitcast(I32), in_=osc[QUAD * q : QUAD * q + 4, :].bitcast(I32)
-            )
+            queue.dma_start(out=out_2[0].bitcast(I32)[q:16:4, :], in_=osc[:].bitcast(I32)[q:P:QUAD, :])

@@ -55,10 +55,10 @@ def tile_picked_nerfvol_none_po_kernel(
         xw = stage.tile([P, T], U32, name="xw", offset=10240)
         xs = keep.tile([P, T], U8, name="xs", tag="xs", align_bytes=64)
         ws_raw = stage.tile([P, H], U8, name="ws_raw", offset=20480, align_bytes=64)
-        warm_out = stage.tile([P, 16], F32, name="warm_out", offset=2048 - 32)
+        zeros = stage.tile([P, H // 4], I32, name="zeros", offset=2048 - 256)
         nc.vector.memset(xs[:].bitcast(I32), 0)
-        nc.gpsimd.memset(ws_raw[:].bitcast(I32), 0)
-        nc.scalar.activation(warm_out[:], ws_raw[:, 0:64].bitcast(F32), ACT.Exp)
+        nc.gpsimd.memset(zeros[:], 0)
+        nc.vector.tensor_copy(ws_raw[:].bitcast(I32), zeros[:])
 
         nc.sync.dma_start(offs_sb[:], offs)
         nc.sync.dma_start(p2_sb[:], p2)
@@ -202,9 +202,7 @@ def tile_picked_nerfvol_none_po_kernel(
         near_blend(0)
         far_diff(3)
         near_blend(1)
-        for t in (2, 3):
-            through(e1, p1_sb, t, "e1")
-        for step in (far_weigh, far_blend, near_diff, near_blend):
+        for step in (far_weigh, far_blend):
             for t in (2, 3):
                 step(t)
 
@@ -216,15 +214,31 @@ def tile_picked_nerfvol_none_po_kernel(
         ob = [keep.tile([P, P, PACK], BF16, name=f"ob{h}", align_bytes=64) for h in range(2)]
         of = [keep.tile([P, PACK, P], F32, name=f"of{h}", align_bytes=64) for h in range(2)]
         rays = [slice(h * P, (h + 1) * P) for h in range(2)]
-        for h in range(2):
+        e1_last = [keep.tile([P, 2, P], F32, name=f"e1_last{h}") for h in range(2)]
+        g_last = [keep.tile([P, 2, P], F32, name=f"g_last{h}") for h in range(2)]
+        banks = []
+
+        def near_last(h, t):
+            entries = p1_sb[:, 8 * h : 8 * (h + 1)]
+            nc.scalar.activation(e1_last[h][:, t - 2, :], dens[t][:].indirect(entries), ACT.Exp, scale=-1.0)
+            nc.vector.tensor_tensor(
+                g_last[h][:, t - 2, :], val[t][:].indirect(entries), h_all[:, t, rays[h]], ALU.subtract
+            )
+
+        def weigh_last(h):
+            nc.vector.scalar_tensor_tensor(
+                w_all[:, 2:4, rays[h]], e1_last[h][:], 1.0, g_last[h][:], ALU.subtract, ALU.mult
+            )
+
+        def composite(h):
             nc.vector.tensor_tensor(
                 zb[h][:].rearrange("p (c i) t -> p c t i", i=4),
                 h_all[:, :, rays[h]].rearrange("p t (c i) -> p c t i", i=4),
                 w_all[:, :, rays[h]].rearrange("p t (c i) -> p c t i", i=4),
                 ALU.subtract,
             )
-        banks = []
-        for h in range(2):
+
+        def last_product(h):
             nc.vector.quantize_mx(
                 out=zw[:, rays[h]].bitcast(FP8X4), scales=zs[:, rays[h]], in_=zb[h][:].rearrange("p v t -> p (v t)")
             )
@@ -240,6 +254,13 @@ def tile_picked_nerfvol_none_po_kernel(
                     stop=True,
                 )
             banks.append(bank)
+
+        for h in range(2):
+            near_last(h, 2)
+            near_last(h, 3)
+            weigh_last(h)
+            composite(h)
+            last_product(h)
         out_rows = out_0.rearrange("(p t) v -> p t v", t=PACK)
         out_words = words_i32(out_1)
         for h, queue in enumerate((nc.sync, nc.scalar)):

@@ -18,18 +18,33 @@ ACT = mybir.ActivationFunctionType
 P = 128
 PACK = 4
 QUAD = 32
+BLOCKS = 16
+LINE = 16
 X_ROW, W1_ROW, W3_ROW = 4, 8, 12
+FIRST, LAST = (0, 1), (2, 3)
+
+W1_WORDS_AT = 0
+W2_AT = W1_WORDS_AT + 4 * H
+ZEROS_AT = W2_AT - H // 2
+X_WORDS_AT = W2_AT + 4 * PACK * H
+BG_AT = X_WORDS_AT
+W3_WORDS_AT = BG_AT + 4 * PACK * V
+W3_SCALES_AT = W3_WORDS_AT + 4 * N
+W1_SCALES_AT = X_WORDS_AT + 4 * T + 4 * 2 * V
+W2_SCALES_AT = (W1_SCALES_AT - 192, W1_SCALES_AT + 64)
+W3_DEALT_AT = W2_SCALES_AT[1] + 2 * P
+NEAR_FIRST_AT = W2_SCALES_AT[0] + 32 - 4 * 2 * V
 
 
 def words_i32(ap):
     return ap[0].rearrange("p n t -> p (n t)").bitcast(I32)
 
 
-def load_scales(queue, plane, scales, row):
-    for r in range(4):
-        queue.dma_start(
-            out=plane[:].bitcast(I32)[row + r : P : QUAD, :],
-            in_=scales[0].bitcast(I32)[r:16:4, :],
+def load_scales(nc, plane, scales, first):
+    for r in range(PACK):
+        nc.sync.dma_start(
+            out=plane[:].bitcast(I32)[first + r : P : QUAD, :],
+            in_=scales[0].bitcast(I32)[r:BLOCKS:PACK, :],
         )
 
 
@@ -38,6 +53,14 @@ def deal(engine, dst, src, run):
         out=dst[:].rearrange("p (t c i) -> p c t i", t=PACK, i=run),
         in_=src[:].rearrange("p (c i t) -> p c t i", t=PACK, i=run),
     )
+
+
+def by_tile(ap):
+    return ap.rearrange("p t (c i) -> p c t i", i=PACK)
+
+
+def by_word(tile):
+    return tile[:].rearrange("p (c i) t -> p c t i", i=PACK)
 
 
 def tile_picked_nerfvol_none_po_kernel(
@@ -52,87 +75,77 @@ def tile_picked_nerfvol_none_po_kernel(
         offs_sb = keep.tile([P, S // 16], U16, name="offs_sb")
         p1_sb = keep.tile([P, V // 16], U16, name="p1_sb")
         p2_sb = keep.tile([P, V // 16], U16, name="p2_sb")
-        xw = stage.tile([P, T], U32, name="xw", offset=10240)
-        xs = keep.tile([P, T], U8, name="xs", tag="xs", align_bytes=64)
-        ws_raw = stage.tile([P, H], U8, name="ws_raw", offset=20480, align_bytes=64)
-        zeros = stage.tile([P, H // 4], I32, name="zeros", offset=2048 - 256)
+        xw = stage.tile([P, T], U32, name="xw", offset=X_WORDS_AT)
+        xs = keep.tile([P, T], U8, name="xs", align_bytes=64)
+        w1s_raw = stage.tile([P, H], U8, name="w1s_raw", offset=W1_SCALES_AT, align_bytes=64)
+        zeros = stage.tile([P, H // 4], I32, name="zeros", offset=ZEROS_AT)
         nc.vector.memset(xs[:].bitcast(I32), 0)
         nc.gpsimd.memset(zeros[:], 0)
-        nc.vector.tensor_copy(ws_raw[:].bitcast(I32), zeros[:])
+        nc.vector.tensor_copy(w1s_raw[:].bitcast(I32), zeros[:])
 
         nc.sync.dma_start(offs_sb[:], offs)
         nc.sync.dma_start(p2_sb[:], p2)
         nc.sync.dma_start(p1_sb[:], p1)
         nc.sync.dma_start(out=xw[:].bitcast(I32), in_=words_i32(x_words))
-        load_scales(nc.sync, xs, x_scales, X_ROW)
-        w1w_raw = stage.tile([P, H], U32, name="w1w_raw", offset=0)
+        load_scales(nc, xs, x_scales, X_ROW)
+        w1w_raw = stage.tile([P, H], U32, name="w1w_raw", offset=W1_WORDS_AT)
         nc.sync.dma_start(out=w1w_raw[:].bitcast(I32), in_=words_i32(w1_words))
-        w2_raw = stage.tile([P, 2, PACK, H // 2], F32, name="w2_raw", offset=2048)
+        w2_raw = stage.tile([P, 2, PACK, H // 2], F32, name="w2_raw", offset=W2_AT)
         w2_rows = w2.rearrange("(p j) c -> p j c", j=PACK)
-        nc.sync.dma_start(out=w2_raw[:, 0], in_=w2_rows[:, :, 0:256])
-        load_scales(nc.sync, ws_raw, w1_scales, W1_ROW)
-        nc.sync.dma_start(out=w2_raw[:, 1], in_=w2_rows[:, :, 256:512])
+        nc.sync.dma_start(out=w2_raw[:, 0], in_=w2_rows[:, :, 0 : H // 2])
+        load_scales(nc, w1s_raw, w1_scales, W1_ROW)
+        nc.sync.dma_start(out=w2_raw[:, 1], in_=w2_rows[:, :, H // 2 : H])
 
         xg_w = keep.tile([P, S], U32, name="xg_w", align_bytes=64)
         nc.vector.tensor_copy(xg_w[:], xw[:].indirect(offs_sb[:]))
         xg_s = keep.tile([P, S], U8, name="xg_s", align_bytes=64)
         nc.vector.tensor_copy(xg_s[:], xs[:].indirect(offs_sb[:]))
         w1w = keep.tile([P, H], U32, name="w1w", align_bytes=64)
-        deal(nc.gpsimd, w1w, w1w_raw, 4)
+        deal(nc.gpsimd, w1w, w1w_raw, LINE // 4)
         w1s = keep.tile([P, H], U8, name="w1s", align_bytes=64)
-        deal(nc.vector, w1s, ws_raw, 16)
+        deal(nc.vector, w1s, w1s_raw, LINE)
 
-        bg_sb = stage.tile([P, PACK, V], F32, name="bg_sb", offset=10240)
+        bg_sb = stage.tile([P, PACK, V], F32, name="bg_sb", offset=BG_AT)
         bg_rows = bg.rearrange("(p t) v -> p t v", t=PACK)
         nc.sync.dma_start(out=bg_sb[:, 0:2, :], in_=bg_rows[:, 0:2, :])
-        w3w_raw = stage.tile([P, N], U32, name="w3w_raw", offset=10240 + 4096)
+        w3w_raw = stage.tile([P, N], U32, name="w3w_raw", offset=W3_WORDS_AT)
         nc.sync.dma_start(out=w3w_raw[:].bitcast(I32), in_=words_i32(w3_words))
         nc.sync.dma_start(out=bg_sb[:, 2:4, :], in_=bg_rows[:, 2:4, :])
-        w3s_raw = stage.tile([P, N], U8, name="w3s_raw", offset=10240 + 6144)
+        w3s_raw = stage.tile([P, N], U8, name="w3s_raw", offset=W3_SCALES_AT)
         nc.gpsimd.memset(w3s_raw[:].bitcast(I32), 0)
-        load_scales(nc.sync, w3s_raw, w3_scales, W3_ROW)
+        load_scales(nc, w3s_raw, w3_scales, W3_ROW)
 
         w2w = keep.tile([P, H], U32, name="w2w", align_bytes=64)
         w2s = [
-            stage.tile([P, 2 * P], U8, name="w2s0", offset=20480 - 192, align_bytes=64),
-            stage.tile([P, 2 * P], U8, name="w2s1", offset=20480 + 64, align_bytes=64),
+            stage.tile([P, 2 * P], U8, name=f"w2s{pair}", offset=W2_SCALES_AT[pair], align_bytes=64)
+            for pair in range(2)
         ]
-        w2b = [keep.tile([P, 2, P, PACK], BF16, name=f"w2b{i}", align_bytes=64) for i in range(2)]
-
-        def cast_w2(copy, half, pair):
-            copy(
-                out=w2b[pair][:, :, 64 * half : 64 * (half + 1), :].rearrange("p t m j -> p m j t"),
-                in_=w2_raw[:, half].rearrange("p j (m t) -> p m j t", t=PACK)[:, :, :, 2 * pair : 2 * pair + 2],
-            )
-
-        def quantise_w2(t0, t1):
-            pair, u0, u1 = t0 // 2, t0 % 2, (t1 - 1) % 2 + 1
+        w2b = [keep.tile([P, 2, P, PACK], BF16, name=f"w2b{pair}", align_bytes=64) for pair in range(2)]
+        for half, cast in enumerate((nc.scalar.copy, nc.vector.tensor_copy)):
+            for pair in range(2):
+                cast(
+                    out=w2b[pair][:, :, half * P // 2 : (half + 1) * P // 2, :].rearrange("p u m j -> p m j u"),
+                    in_=w2_raw[:, half].rearrange("p j (m t) -> p m j t", t=PACK)[:, :, :, 2 * pair : 2 * pair + 2],
+                )
+        for pair, u0, u1 in ((0, 0, 1), (0, 1, 2), (1, 0, 2)):
             nc.vector.quantize_mx(
-                out=w2w[:, P * t0 : P * t1].bitcast(FP8X4),
+                out=w2w[:, P * (2 * pair + u0) : P * (2 * pair + u1)].bitcast(FP8X4),
                 scales=w2s[pair][:, P * u0 : P * u1],
-                in_=w2b[pair][:, u0:u1].rearrange("p t m j -> p (t m j)"),
+                in_=w2b[pair][:, u0:u1].rearrange("p u m j -> p (u m j)"),
             )
-
-        cast_w2(nc.scalar.copy, 0, 0)
-        cast_w2(nc.scalar.copy, 0, 1)
-        cast_w2(nc.vector.tensor_copy, 1, 0)
-        cast_w2(nc.vector.tensor_copy, 1, 1)
-        quantise_w2(0, 1)
-        quantise_w2(1, 2)
-        quantise_w2(2, 4)
-        w3w = stage.tile([P, N], U32, name="w3w", offset=20480 + 320, align_bytes=64)
-        deal(nc.gpsimd, w3w, w3w_raw, 4)
+        w3w = stage.tile([P, N], U32, name="w3w", offset=W3_DEALT_AT, align_bytes=64)
+        deal(nc.gpsimd, w3w, w3w_raw, LINE // 4)
         w3s = keep.tile([P, N], U8, name="w3s", align_bytes=64)
-        deal(nc.gpsimd, w3s, w3s_raw, 16)
+        deal(nc.gpsimd, w3s, w3s_raw, LINE)
 
-        def project(words, scales, t, bank_no):
-            bank = psum.tile([P, S], F32, name="bank", tag=f"bank{bank_no}")
+        def project(words, scales, t, bank_no, cols=slice(0, S)):
+            bank = psum.tile([P, cols.stop - cols.start], F32, name="bank", tag=f"bank{bank_no}")
             nc.tensor.matmul_mx(
                 out=bank[:],
                 lhsT=words[:, t * P : (t + 1) * P].bitcast(FP8X4),
                 lhsT_scale=scales,
-                rhs=xg_w[:].bitcast(FP8X4),
-                rhs_scale=xg_s[X_ROW:P, :],
+                rhs=xg_w[:, cols].bitcast(FP8X4),
+                rhs_scale=xg_s[X_ROW:P, cols],
                 start=True,
                 stop=True,
             )
@@ -140,32 +153,36 @@ def tile_picked_nerfvol_none_po_kernel(
 
         h_all = keep.tile([P, PACK, V], F32, name="h_all", align_bytes=64)
         w_all = keep.tile([P, PACK, V], F32, name="w_all", align_bytes=64)
-        val, dens, e1, e2, a, b, g = {}, {}, {}, {}, {}, {}, {}
-
-        e1_first = stage.tile([P, 2, V], F32, name="e1_first", offset=20320 - 2048)
+        val, dens, e2, a, b, g = {}, {}, {}, {}, {}, {}
+        e1_first = stage.tile([P, 2, V], F32, name="e1_first", offset=NEAR_FIRST_AT)
 
         def evacuate_val(t):
             val[t] = keep.tile([P, S], F32, name=f"val{t}")
-            copy_out = nc.vector.tensor_copy if t < 2 else nc.scalar.copy
-            copy_out(val[t][:], project(w2w, w2s[t // 2][:, (t % 2) * P : (t % 2 + 1) * P], t, (t + 2) % 4)[:])
+            scales = w2s[t // 2][:, (t % 2) * P : (t % 2 + 1) * P]
+            if t in FIRST:
+                for half in range(2):
+                    cols = slice(half * S // 2, (half + 1) * S // 2)
+                    nc.vector.tensor_copy(val[t][:, cols], project(w2w, scales, t, 2 + t + 2 * half, cols)[:])
+            else:
+                nc.scalar.copy(val[t][:], project(w2w, scales, t, t - 2)[:])
 
         def evacuate_dens(t):
             dens[t] = keep.tile([P, S], F32, name=f"dens{t}")
             nc.scalar.activation(dens[t][:], project(w1w, w1s[W1_ROW:P, t * P : (t + 1) * P], t, t)[:], ACT.Relu)
 
-        def through(store, lists, t, name):
-            if name == "e1" and t < 2:
-                store[t] = e1_first[:, t, :]
-            else:
-                store[t] = keep.tile([P, V], F32, name=f"{name}_{t}", tag=f"{name}_{t}", align_bytes=64)
-            nc.scalar.activation(store[t][:], dens[t][:].indirect(lists[:]), ACT.Exp, scale=-1.0)
+        def exp_of(out, t, entries):
+            nc.scalar.activation(out, dens[t][:].indirect(entries), ACT.Exp, scale=-1.0)
+
+        def far_exp(t):
+            e2[t] = keep.tile([P, V], F32, name=f"e2_{t}", align_bytes=64)
+            exp_of(e2[t][:], t, p2_sb[:])
 
         def far_diff(t):
-            a[t] = keep.tile([P, V], F32, name=f"a{t}", tag=f"a{t}", align_bytes=64)
+            a[t] = keep.tile([P, V], F32, name=f"a{t}", align_bytes=64)
             nc.vector.tensor_tensor(a[t][:], val[t][:].indirect(p2_sb[:]), bg_sb[:, t, :], ALU.subtract)
 
         def far_weigh(t):
-            b[t] = keep.tile([P, V], F32, name=f"b{t}", tag=f"b{t}", align_bytes=64)
+            b[t] = keep.tile([P, V], F32, name=f"b{t}", align_bytes=64)
             nc.vector.scalar_tensor_tensor(b[t][:], e2[t][:], 1.0, a[t][:], ALU.subtract, ALU.mult)
 
         def far_blend(t):
@@ -175,105 +192,88 @@ def tile_picked_nerfvol_none_po_kernel(
             g[t] = keep.tile([P, V], F32, name=f"g{t}")
             nc.vector.tensor_tensor(g[t][:], val[t][:].indirect(p1_sb[:]), h_all[:, t, :], ALU.subtract)
 
-        def near_blend(t):
-            nc.vector.scalar_tensor_tensor(w_all[:, t, :], e1[t][:], 1.0, g[t][:], ALU.subtract, ALU.mult)
+        def near_weigh(t):
+            nc.vector.scalar_tensor_tensor(w_all[:, t, :], e1_first[:, t, :], 1.0, g[t][:], ALU.subtract, ALU.mult)
 
-        evacuate_dens(0)
-        evacuate_dens(1)
-        through(e2, p2_sb, 0, "e2")
-        evacuate_val(0)
-        evacuate_val(1)
-        through(e2, p2_sb, 1, "e2")
-        far_diff(0)
-        far_diff(1)
-        far_weigh(0)
-        far_weigh(1)
-        far_blend(0)
-        far_blend(1)
+        for t in FIRST:
+            evacuate_dens(t)
+        far_exp(0)
+        for t in FIRST:
+            evacuate_val(t)
+        far_exp(1)
+        for step in (far_diff, far_weigh, far_blend):
+            for t in FIRST:
+                step(t)
         near_diff(0)
-        for t in (2, 3):
+        for t in LAST:
             evacuate_dens(t)
             evacuate_val(t)
         far_diff(2)
         near_diff(1)
-        for t in (2, 3):
-            through(e1, p1_sb, t - 2, "e1")
-            through(e2, p2_sb, t, "e2")
-        near_blend(0)
+        for t_first, t_last in zip(FIRST, LAST):
+            exp_of(e1_first[:, t_first, :], t_first, p1_sb[:])
+            far_exp(t_last)
+        near_weigh(0)
         far_diff(3)
-        near_blend(1)
+        near_weigh(1)
         for step in (far_weigh, far_blend):
-            for t in (2, 3):
+            for t in LAST:
                 step(t)
 
         zw = keep.tile([P, V], U32, name="zw", align_bytes=64)
         zs = keep.tile([P, V], U8, name="zs", align_bytes=64)
         ow = keep.tile([P, V], U32, name="ow", align_bytes=64)
         osc = keep.tile([P, V], U8, name="osc", align_bytes=64)
-        zb = [keep.tile([P, P, PACK], BF16, name=f"zb{h}", align_bytes=64) for h in range(2)]
-        ob = [keep.tile([P, P, PACK], BF16, name=f"ob{h}", align_bytes=64) for h in range(2)]
-        of = [keep.tile([P, PACK, P], F32, name=f"of{h}", align_bytes=64) for h in range(2)]
-        rays = [slice(h * P, (h + 1) * P) for h in range(2)]
-        e1_last = [keep.tile([P, 2, P], F32, name=f"e1_last{h}") for h in range(2)]
-        g_last = [keep.tile([P, 2, P], F32, name=f"g_last{h}") for h in range(2)]
-        banks = []
-
-        def near_last(h, t):
-            entries = p1_sb[:, 8 * h : 8 * (h + 1)]
-            nc.scalar.activation(e1_last[h][:, t - 2, :], dens[t][:].indirect(entries), ACT.Exp, scale=-1.0)
-            nc.vector.tensor_tensor(
-                g_last[h][:, t - 2, :], val[t][:].indirect(entries), h_all[:, t, rays[h]], ALU.subtract
-            )
-
-        def weigh_last(h):
+        zb = [keep.tile([P, P, PACK], BF16, name=f"zb{half}", align_bytes=64) for half in range(2)]
+        ob = [keep.tile([P, P, PACK], BF16, name=f"ob{half}", align_bytes=64) for half in range(2)]
+        of = [keep.tile([P, PACK, P], F32, name=f"of{half}", align_bytes=64) for half in range(2)]
+        e1_last = [keep.tile([P, 2, P], F32, name=f"e1_last{half}") for half in range(2)]
+        g_last = [keep.tile([P, 2, P], F32, name=f"g_last{half}") for half in range(2)]
+        out_banks = []
+        for half in range(2):
+            rays = slice(half * P, (half + 1) * P)
+            entries = p1_sb[:, half * P // 16 : (half + 1) * P // 16]
+            for u, t in enumerate(LAST):
+                exp_of(e1_last[half][:, u, :], t, entries)
+                nc.vector.tensor_tensor(
+                    g_last[half][:, u, :], val[t][:].indirect(entries), h_all[:, t, rays], ALU.subtract
+                )
             nc.vector.scalar_tensor_tensor(
-                w_all[:, 2:4, rays[h]], e1_last[h][:], 1.0, g_last[h][:], ALU.subtract, ALU.mult
+                w_all[:, 2:4, rays], e1_last[half][:], 1.0, g_last[half][:], ALU.subtract, ALU.mult
             )
-
-        def composite(h):
             nc.vector.tensor_tensor(
-                zb[h][:].rearrange("p (c i) t -> p c t i", i=4),
-                h_all[:, :, rays[h]].rearrange("p t (c i) -> p c t i", i=4),
-                w_all[:, :, rays[h]].rearrange("p t (c i) -> p c t i", i=4),
-                ALU.subtract,
+                by_word(zb[half]), by_tile(h_all[:, :, rays]), by_tile(w_all[:, :, rays]), ALU.subtract
             )
-
-        def last_product(h):
             nc.vector.quantize_mx(
-                out=zw[:, rays[h]].bitcast(FP8X4), scales=zs[:, rays[h]], in_=zb[h][:].rearrange("p v t -> p (v t)")
+                out=zw[:, rays].bitcast(FP8X4), scales=zs[:, rays], in_=zb[half][:].rearrange("p v t -> p (v t)")
             )
-            bank = psum.tile([P, PACK, P], F32, name="out_bank", tag=f"bank{6 + h}")
+            banks = [
+                psum.tile([P, 2, P], F32, name="out_bank", tag=f"bank{4 + 2 * half + pair}") for pair in range(2)
+            ]
             for t in range(PACK):
                 nc.tensor.matmul_mx(
-                    out=bank[:, t, :],
+                    out=banks[t // 2][:, t % 2, :],
                     lhsT=w3w[:, t * P : (t + 1) * P].bitcast(FP8X4),
                     lhsT_scale=w3s[W3_ROW:P, t * P : (t + 1) * P],
-                    rhs=zw[:, rays[h]].bitcast(FP8X4),
-                    rhs_scale=zs[:, rays[h]],
+                    rhs=zw[:, rays].bitcast(FP8X4),
+                    rhs_scale=zs[:, rays],
                     start=True,
                     stop=True,
                 )
-            banks.append(bank)
+            out_banks.append(banks)
 
-        for h in range(2):
-            near_last(h, 2)
-            near_last(h, 3)
-            weigh_last(h)
-            composite(h)
-            last_product(h)
         out_rows = out_0.rearrange("(p t) v -> p t v", t=PACK)
         out_words = words_i32(out_1)
-        for h, queue in enumerate((nc.sync, nc.scalar)):
-            nc.scalar.copy(of[h][:], banks[h][:])
-            queue.dma_start(out=out_rows[:, :, rays[h]], in_=of[h][:])
-            nc.vector.tensor_copy(
-                out=ob[h][:].rearrange("p (c i) t -> p c t i", i=4),
-                in_=of[h][:].rearrange("p t (c i) -> p c t i", i=4),
-            )
+        for half, (second_copy, queue) in enumerate(((nc.vector.tensor_copy, nc.sync), (nc.scalar.copy, nc.scalar))):
+            rays = slice(half * P, (half + 1) * P)
+            nc.scalar.copy(of[half][:, 0:2, :], out_banks[half][0][:])
+            second_copy(of[half][:, 2:4, :], out_banks[half][1][:])
+            queue.dma_start(out=out_rows[:, :, rays], in_=of[half][:])
+            nc.vector.tensor_copy(out=by_word(ob[half]), in_=by_tile(of[half][:]))
             nc.vector.quantize_mx(
-                out=ow[:, rays[h]].bitcast(FP8X4), scales=osc[:, rays[h]], in_=ob[h][:].rearrange("p v t -> p (v t)")
+                out=ow[:, rays].bitcast(FP8X4), scales=osc[:, rays], in_=ob[half][:].rearrange("p v t -> p (v t)")
             )
-            nc.sync.dma_start(out=out_words[:, rays[h]], in_=ow[:, rays[h]].bitcast(I32))
-        for q in range(4):
-            queue = nc.sync if q % 2 else nc.scalar
-            queue.dma_start(out=out_2[0].bitcast(I32)[q:16:4, :], in_=osc[:].bitcast(I32)[q:P:QUAD, :])
+            nc.sync.dma_start(out=out_words[:, rays], in_=ow[:, rays].bitcast(I32))
+        for r in range(PACK):
+            queue = nc.sync if r % 2 else nc.scalar
+            queue.dma_start(out=out_2[0].bitcast(I32)[r:BLOCKS:PACK, :], in_=osc[:].bitcast(I32)[r:P:QUAD, :])

@@ -29,11 +29,13 @@ ZEROS_AT = W2_AT - H // 2
 X_WORDS_AT = W2_AT + 4 * PACK * H
 BG_AT = X_WORDS_AT
 W3_WORDS_AT = BG_AT + 4 * PACK * V
-W3_SCALES_AT = W3_WORDS_AT + 4 * N
-W1_SCALES_AT = X_WORDS_AT + 4 * T + 4 * 2 * V
-W2_SCALES_AT = (W1_SCALES_AT - 192, W1_SCALES_AT + 64)
-W3_DEALT_AT = W2_SCALES_AT[1] + 2 * P
-NEAR_FIRST_AT = W2_SCALES_AT[0] + 32 - 4 * 2 * V
+W3_SCALES_AT = W1_WORDS_AT
+W1_SCALES_AT = X_WORDS_AT + 4 * T + 4 * 3 * V
+W2_SCALES_AT = (W1_SCALES_AT - 64, W1_SCALES_AT + 64)
+HELD_AT = W2_SCALES_AT[0] + 32 - 4 * 3 * V
+W2B_AT = W2_SCALES_AT[1] + 3 * P
+W2B_LAST_AT = W2B_AT + 4 * H
+W3_DEALT_AT = W2B_LAST_AT + N
 
 
 def words_i32(ap):
@@ -48,10 +50,10 @@ def load_scales(nc, plane, scales, first):
         )
 
 
-def deal(engine, dst, src, run):
+def deal(engine, dst, src, run, t0=0, t1=PACK):
     engine.tensor_copy(
-        out=dst[:].rearrange("p (t c i) -> p c t i", t=PACK, i=run),
-        in_=src[:].rearrange("p (c i t) -> p c t i", t=PACK, i=run),
+        out=dst[:].rearrange("p (t c i) -> p c t i", t=PACK, i=run)[:, :, t0:t1, :],
+        in_=src[:].rearrange("p (c i t) -> p c t i", t=PACK, i=run)[:, :, t0:t1, :],
     )
 
 
@@ -76,7 +78,7 @@ def tile_picked_nerfvol_none_po_kernel(
         p1_sb = keep.tile([P, V // 16], U16, name="p1_sb")
         p2_sb = keep.tile([P, V // 16], U16, name="p2_sb")
         xw = stage.tile([P, T], U32, name="xw", offset=X_WORDS_AT)
-        xs = keep.tile([P, T], U8, name="xs", align_bytes=64)
+        xs = keep.tile([P, T], U8, name="xs", tag="xs", align_bytes=64)
         w1s_raw = stage.tile([P, H], U8, name="w1s_raw", offset=W1_SCALES_AT, align_bytes=64)
         zeros = stage.tile([P, H // 4], I32, name="zeros", offset=ZEROS_AT)
         nc.vector.memset(xs[:].bitcast(I32), 0)
@@ -84,59 +86,67 @@ def tile_picked_nerfvol_none_po_kernel(
         nc.vector.tensor_copy(w1s_raw[:].bitcast(I32), zeros[:])
 
         nc.sync.dma_start(offs_sb[:], offs)
-        nc.sync.dma_start(p2_sb[:], p2)
-        nc.sync.dma_start(p1_sb[:], p1)
-        nc.sync.dma_start(out=xw[:].bitcast(I32), in_=words_i32(x_words))
+        for part in range(2):
+            cols = slice(part * T // 4, (part + 1) * T // 4)
+            nc.sync.dma_start(out=xw[:, cols].bitcast(I32), in_=words_i32(x_words)[:, cols])
         load_scales(nc, xs, x_scales, X_ROW)
+        nc.sync.dma_start(out=xw[:, T // 2 : T].bitcast(I32), in_=words_i32(x_words)[:, T // 2 : T])
         w1w_raw = stage.tile([P, H], U32, name="w1w_raw", offset=W1_WORDS_AT)
         nc.sync.dma_start(out=w1w_raw[:].bitcast(I32), in_=words_i32(w1_words))
         w2_raw = stage.tile([P, 2, PACK, H // 2], F32, name="w2_raw", offset=W2_AT)
         w2_rows = w2.rearrange("(p j) c -> p j c", j=PACK)
-        nc.sync.dma_start(out=w2_raw[:, 0], in_=w2_rows[:, :, 0 : H // 2])
         load_scales(nc, w1s_raw, w1_scales, W1_ROW)
+        nc.sync.dma_start(out=w2_raw[:, 0], in_=w2_rows[:, :, 0 : H // 2])
         nc.sync.dma_start(out=w2_raw[:, 1], in_=w2_rows[:, :, H // 2 : H])
+        nc.sync.dma_start(p2_sb[:], p2)
+        nc.sync.dma_start(p1_sb[:], p1)
 
-        xg_w = keep.tile([P, S], U32, name="xg_w", align_bytes=64)
-        nc.vector.tensor_copy(xg_w[:], xw[:].indirect(offs_sb[:]))
         xg_s = keep.tile([P, S], U8, name="xg_s", align_bytes=64)
         nc.vector.tensor_copy(xg_s[:], xs[:].indirect(offs_sb[:]))
+        xg_w = keep.tile([P, S], U32, name="xg_w", tag="xs", align_bytes=64)
+        nc.vector.tensor_copy(xg_w[:], xw[:].indirect(offs_sb[:]))
         w1w = keep.tile([P, H], U32, name="w1w", align_bytes=64)
-        deal(nc.gpsimd, w1w, w1w_raw, LINE // 4)
+        deal(nc.gpsimd, w1w, w1w_raw, LINE // 4, 0, 1)
+        deal(nc.gpsimd, w1w, w1w_raw, LINE // 4, 1, PACK)
         w1s = keep.tile([P, H], U8, name="w1s", align_bytes=64)
-        deal(nc.vector, w1s, w1s_raw, LINE)
+        deal(nc.vector, w1s, w1s_raw, LINE, 0, 1)
+        deal(nc.vector, w1s, w1s_raw, LINE, 1, PACK)
 
         bg_sb = stage.tile([P, PACK, V], F32, name="bg_sb", offset=BG_AT)
         bg_rows = bg.rearrange("(p t) v -> p t v", t=PACK)
         nc.sync.dma_start(out=bg_sb[:, 0:2, :], in_=bg_rows[:, 0:2, :])
         w3w_raw = stage.tile([P, N], U32, name="w3w_raw", offset=W3_WORDS_AT)
         nc.sync.dma_start(out=w3w_raw[:].bitcast(I32), in_=words_i32(w3_words))
-        nc.sync.dma_start(out=bg_sb[:, 2:4, :], in_=bg_rows[:, 2:4, :])
         w3s_raw = stage.tile([P, N], U8, name="w3s_raw", offset=W3_SCALES_AT)
         nc.gpsimd.memset(w3s_raw[:].bitcast(I32), 0)
         load_scales(nc, w3s_raw, w3_scales, W3_ROW)
+        nc.sync.dma_start(out=bg_sb[:, 2:4, :], in_=bg_rows[:, 2:4, :])
 
         w2w = keep.tile([P, H], U32, name="w2w", align_bytes=64)
         w2s = [
-            stage.tile([P, 2 * P], U8, name=f"w2s{pair}", offset=W2_SCALES_AT[pair], align_bytes=64)
-            for pair in range(2)
+            stage.tile([P, (1, 3)[part] * P], U8, name=f"w2s{part}", offset=W2_SCALES_AT[part], align_bytes=64)
+            for part in range(2)
         ]
-        w2b = [keep.tile([P, 2, P, PACK], BF16, name=f"w2b{pair}", align_bytes=64) for pair in range(2)]
-        for half, cast in enumerate((nc.scalar.copy, nc.vector.tensor_copy)):
+        w2b = [
+            stage.tile([P, 2, P, PACK], BF16, name="w2b0", offset=W2B_AT, align_bytes=64),
+            stage.tile([P, 2, P, PACK], BF16, name="w2b1", offset=W2B_LAST_AT, align_bytes=64),
+        ]
+        for half, cast in enumerate((nc.vector.tensor_copy, nc.vector.tensor_copy)):
             for pair in range(2):
                 cast(
                     out=w2b[pair][:, :, half * P // 2 : (half + 1) * P // 2, :].rearrange("p u m j -> p m j u"),
                     in_=w2_raw[:, half].rearrange("p j (m t) -> p m j t", t=PACK)[:, :, :, 2 * pair : 2 * pair + 2],
                 )
+
+        def w2_scales(t0, t1):
+            return w2s[0][:] if t0 == 0 else w2s[1][:, P * (t0 - 1) : P * (t1 - 1)]
+
         for pair, u0, u1 in ((0, 0, 1), (0, 1, 2), (1, 0, 2)):
             nc.vector.quantize_mx(
                 out=w2w[:, P * (2 * pair + u0) : P * (2 * pair + u1)].bitcast(FP8X4),
-                scales=w2s[pair][:, P * u0 : P * u1],
+                scales=w2_scales(2 * pair + u0, 2 * pair + u1),
                 in_=w2b[pair][:, u0:u1].rearrange("p u m j -> p (u m j)"),
             )
-        w3w = stage.tile([P, N], U32, name="w3w", offset=W3_DEALT_AT, align_bytes=64)
-        deal(nc.gpsimd, w3w, w3w_raw, LINE // 4)
-        w3s = keep.tile([P, N], U8, name="w3s", align_bytes=64)
-        deal(nc.gpsimd, w3s, w3s_raw, LINE)
 
         def project(words, scales, t, bank_no, cols=slice(0, S)):
             bank = psum.tile([P, cols.stop - cols.start], F32, name="bank", tag=f"bank{bank_no}")
@@ -153,29 +163,38 @@ def tile_picked_nerfvol_none_po_kernel(
 
         h_all = keep.tile([P, PACK, V], F32, name="h_all", align_bytes=64)
         w_all = keep.tile([P, PACK, V], F32, name="w_all", align_bytes=64)
-        val, dens, e2, a, b, g = {}, {}, {}, {}, {}, {}
-        e1_first = stage.tile([P, 2, V], F32, name="e1_first", offset=NEAR_FIRST_AT)
+        val, dens, e1, e2, a, b, g = {}, {}, {}, {}, {}, {}, {}
+        S_BANK = (0, 1, 3, 4)
+        VAL_BANK = (3, 2, 0, 1)
+        held = stage.tile([P, 3, V], F32, name="held", offset=HELD_AT)
 
         def evacuate_val(t):
             val[t] = keep.tile([P, S], F32, name=f"val{t}")
-            scales = w2s[t // 2][:, (t % 2) * P : (t % 2 + 1) * P]
-            if t in FIRST:
+            scales = w2_scales(t, t + 1)
+            if t == 0:
                 for half in range(2):
                     cols = slice(half * S // 2, (half + 1) * S // 2)
-                    nc.vector.tensor_copy(val[t][:, cols], project(w2w, scales, t, 2 + t + 2 * half, cols)[:])
+                    copy = (nc.vector.tensor_copy, nc.scalar.copy)[half]
+                    copy(val[t][:, cols], project(w2w, scales, t, 3 + half, cols)[:])
             else:
-                nc.scalar.copy(val[t][:], project(w2w, scales, t, t - 2)[:])
+                copy = nc.vector.tensor_copy if t == 1 else nc.scalar.copy
+                copy(val[t][:], project(w2w, scales, t, VAL_BANK[t])[:])
 
         def evacuate_dens(t):
             dens[t] = keep.tile([P, S], F32, name=f"dens{t}")
-            nc.scalar.activation(dens[t][:], project(w1w, w1s[W1_ROW:P, t * P : (t + 1) * P], t, t)[:], ACT.Relu)
+            bank = project(w1w, w1s[W1_ROW:P, t * P : (t + 1) * P], t, S_BANK[t])
+            nc.scalar.activation(dens[t][:], bank[:], ACT.Relu)
 
         def exp_of(out, t, entries):
             nc.scalar.activation(out, dens[t][:].indirect(entries), ACT.Exp, scale=-1.0)
 
         def far_exp(t):
-            e2[t] = keep.tile([P, V], F32, name=f"e2_{t}", align_bytes=64)
-            exp_of(e2[t][:], t, p2_sb[:])
+            e2[t] = held[:, 2, :] if t == 1 else keep.tile([P, V], F32, name=f"e2_{t}", align_bytes=64)[:]
+            exp_of(e2[t], t, p2_sb[:])
+
+        def near_exp(t):
+            e1[t] = held[:, t, :]
+            exp_of(e1[t], t, p1_sb[:])
 
         def far_diff(t):
             a[t] = keep.tile([P, V], F32, name=f"a{t}", align_bytes=64)
@@ -183,7 +202,7 @@ def tile_picked_nerfvol_none_po_kernel(
 
         def far_weigh(t):
             b[t] = keep.tile([P, V], F32, name=f"b{t}", align_bytes=64)
-            nc.vector.scalar_tensor_tensor(b[t][:], e2[t][:], 1.0, a[t][:], ALU.subtract, ALU.mult)
+            nc.vector.scalar_tensor_tensor(b[t][:], e2[t], 1.0, a[t][:], ALU.subtract, ALU.mult)
 
         def far_blend(t):
             nc.vector.tensor_tensor(h_all[:, t, :], bg_sb[:, t, :], b[t][:], ALU.subtract)
@@ -193,32 +212,42 @@ def tile_picked_nerfvol_none_po_kernel(
             nc.vector.tensor_tensor(g[t][:], val[t][:].indirect(p1_sb[:]), h_all[:, t, :], ALU.subtract)
 
         def near_weigh(t):
-            nc.vector.scalar_tensor_tensor(w_all[:, t, :], e1_first[:, t, :], 1.0, g[t][:], ALU.subtract, ALU.mult)
+            nc.vector.scalar_tensor_tensor(w_all[:, t, :], e1[t], 1.0, g[t][:], ALU.subtract, ALU.mult)
 
-        for t in FIRST:
-            evacuate_dens(t)
+        w3w = stage.tile([P, N], U32, name="w3w", offset=W3_DEALT_AT, align_bytes=64)
+        w3s = stage.tile([P, N], U8, name="w3s", offset=W2B_LAST_AT, align_bytes=64)
+        evacuate_dens(0)
+        evacuate_dens(1)
+        evacuate_val(0)
         far_exp(0)
-        for t in FIRST:
-            evacuate_val(t)
+        far_diff(0)
+        evacuate_val(1)
         far_exp(1)
-        for step in (far_diff, far_weigh, far_blend):
-            for t in FIRST:
-                step(t)
+        near_exp(0)
+        evacuate_dens(2)
+        evacuate_val(2)
+        near_exp(1)
+        far_exp(2)
+        evacuate_val(3)
+        evacuate_dens(3)
+        far_exp(3)
+        far_weigh(0)
+        far_diff(1)
+        far_blend(0)
+        far_weigh(1)
         near_diff(0)
-        for t in LAST:
-            evacuate_dens(t)
-            evacuate_val(t)
-        far_diff(2)
-        near_diff(1)
-        for t_first, t_last in zip(FIRST, LAST):
-            exp_of(e1_first[:, t_first, :], t_first, p1_sb[:])
-            far_exp(t_last)
+        far_blend(1)
         near_weigh(0)
-        far_diff(3)
+        near_diff(1)
+        far_diff(2)
         near_weigh(1)
-        for step in (far_weigh, far_blend):
-            for t in LAST:
-                step(t)
+        far_weigh(2)
+        far_diff(3)
+        far_blend(2)
+        far_weigh(3)
+        far_blend(3)
+        deal(nc.gpsimd, w3w, w3w_raw, LINE // 4)
+        deal(nc.gpsimd, w3s, w3s_raw, LINE)
 
         zw = keep.tile([P, V], U32, name="zw", align_bytes=64)
         zs = keep.tile([P, V], U8, name="zs", align_bytes=64)

@@ -23,19 +23,22 @@ LINE = 16
 X_ROW, W1_ROW, W3_ROW = 4, 8, 12
 FIRST, LAST = (0, 1), (2, 3)
 
-W1_WORDS_AT = 0
-W2_AT = W1_WORDS_AT + 4 * H
+WORDS_AT = 0
+W2_AT = WORDS_AT + 4 * (N + H)
 ZEROS_AT = W2_AT - H // 2
-X_WORDS_AT = W2_AT + 4 * PACK * H
-BG_AT = X_WORDS_AT
-W3_WORDS_AT = BG_AT + 4 * PACK * V
-W3_SCALES_AT = W1_WORDS_AT
-W1_SCALES_AT = X_WORDS_AT + 4 * T + 4 * 3 * V
-W2_SCALES_AT = (W1_SCALES_AT - 64, W1_SCALES_AT + 64)
-HELD_AT = W2_SCALES_AT[0] + 32 - 4 * 3 * V
-W2B_AT = W2_SCALES_AT[1] + 3 * P
-W2B_LAST_AT = W2B_AT + 4 * H
-W3_DEALT_AT = W2B_LAST_AT + N
+X_WORDS_AT = W2_AT + 4 * PACK * (H + V)
+W2B_LAST_AT = X_WORDS_AT + 4 * T + N
+W1_SCALES_AT = W2B_LAST_AT + 4 * H - 64
+W2B_FIRST_AT = W1_SCALES_AT + H - 64
+W3_SCALES_DEALT_AT = W2B_LAST_AT + 64 - N
+W3_DEALT_AT = W2B_LAST_AT + 64
+DENS2_AT = W2B_FIRST_AT + 4 * H
+W2_SCALES1_AT = DENS2_AT + 4 * S - 64
+HELD_AT = W2_SCALES1_AT + P - 32
+DENS3_AT = HELD_AT + 4 * 2 * V + 32
+W2_WORDS1_AT = DENS3_AT + 4 * S - 64
+W2_SCALES0_AT = W2_WORDS1_AT + 4 * P
+W2_SPLIT = 64
 
 
 def words_i32(ap):
@@ -53,7 +56,7 @@ def load_scales(nc, plane, scales, first):
 def deal(engine, dst, src, run, t0=0, t1=PACK):
     engine.tensor_copy(
         out=dst[:].rearrange("p (t c i) -> p c t i", t=PACK, i=run)[:, :, t0:t1, :],
-        in_=src[:].rearrange("p (c i t) -> p c t i", t=PACK, i=run)[:, :, t0:t1, :],
+        in_=src.rearrange("p (c i t) -> p c t i", t=PACK, i=run)[:, :, t0:t1, :],
     )
 
 
@@ -84,6 +87,8 @@ def tile_picked_nerfvol_none_po_kernel(
         nc.vector.memset(xs[:].bitcast(I32), 0)
         nc.gpsimd.memset(zeros[:], 0)
         nc.vector.tensor_copy(w1s_raw[:].bitcast(I32), zeros[:])
+        w3s_raw = keep.tile([P, N], U8, name="w3s_raw")
+        nc.vector.memset(w3s_raw[:].bitcast(I32), 0)
 
         nc.sync.dma_start(offs_sb[:], offs)
         for part in range(2):
@@ -91,68 +96,76 @@ def tile_picked_nerfvol_none_po_kernel(
             nc.sync.dma_start(out=xw[:, cols].bitcast(I32), in_=words_i32(x_words)[:, cols])
         load_scales(nc, xs, x_scales, X_ROW)
         nc.sync.dma_start(out=xw[:, T // 2 : T].bitcast(I32), in_=words_i32(x_words)[:, T // 2 : T])
-        w1w_raw = stage.tile([P, H], U32, name="w1w_raw", offset=W1_WORDS_AT)
-        nc.sync.dma_start(out=w1w_raw[:].bitcast(I32), in_=words_i32(w1_words))
-        w2_raw = stage.tile([P, 2, PACK, H // 2], F32, name="w2_raw", offset=W2_AT)
+        words_raw = stage.tile([P, N + H], U32, name="words_raw", offset=WORDS_AT)
+        w3w_raw, w1w_raw = words_raw[:, 0:N], words_raw[:, N : N + H]
+        nc.sync.dma_start(out=w1w_raw.bitcast(I32), in_=words_i32(w1_words))
+        w2_raw = stage.tile([P, PACK * (H + V)], F32, name="w2_raw", offset=W2_AT)
+        w2_groups = (slice(0, W2_SPLIT), slice(W2_SPLIT, P))
+        w2_parts = [
+            w2_raw[:, PACK * PACK * m.start : PACK * PACK * m.stop].rearrange("p (j c) -> p j c", j=PACK)
+            for m in w2_groups
+        ]
         w2_rows = w2.rearrange("(p j) c -> p j c", j=PACK)
         load_scales(nc, w1s_raw, w1_scales, W1_ROW)
-        nc.sync.dma_start(out=w2_raw[:, 0], in_=w2_rows[:, :, 0 : H // 2])
-        nc.sync.dma_start(out=w2_raw[:, 1], in_=w2_rows[:, :, H // 2 : H])
+        for part, m in zip(w2_parts, w2_groups):
+            nc.sync.dma_start(out=part, in_=w2_rows[:, :, PACK * m.start : PACK * m.stop])
+        bg_sb = w2_raw[:, PACK * H : PACK * (H + V)].rearrange("p (t v) -> p t v", t=PACK)
+        bg_rows = bg.rearrange("(p t) v -> p t v", t=PACK)
         nc.sync.dma_start(p2_sb[:], p2)
         nc.sync.dma_start(p1_sb[:], p1)
+        nc.sync.dma_start(out=w3w_raw.bitcast(I32), in_=words_i32(w3_words))
+        nc.sync.dma_start(out=bg_sb[:, 0:2, :], in_=bg_rows[:, 0:2, :])
+        load_scales(nc, w3s_raw, w3_scales, W3_ROW)
+        nc.sync.dma_start(out=bg_sb[:, 2:4, :], in_=bg_rows[:, 2:4, :])
 
         xg_s = keep.tile([P, S], U8, name="xg_s", align_bytes=64)
         nc.vector.tensor_copy(xg_s[:], xs[:].indirect(offs_sb[:]))
         xg_w = keep.tile([P, S], U32, name="xg_w", tag="xs", align_bytes=64)
-        nc.vector.tensor_copy(xg_w[:], xw[:].indirect(offs_sb[:]))
         w1w = keep.tile([P, H], U32, name="w1w", align_bytes=64)
-        deal(nc.gpsimd, w1w, w1w_raw, LINE // 4, 0, 1)
-        deal(nc.gpsimd, w1w, w1w_raw, LINE // 4, 1, PACK)
         w1s = keep.tile([P, H], U8, name="w1s", align_bytes=64)
-        deal(nc.vector, w1s, w1s_raw, LINE, 0, 1)
-        deal(nc.vector, w1s, w1s_raw, LINE, 1, PACK)
+        deal(nc.gpsimd, w1w, w1w_raw, LINE // 4, 0, 1)
+        deal(nc.gpsimd, w1s, w1s_raw[:], LINE, 0, 1)
+        nc.vector.tensor_copy(xg_w[:, 0 : S // 2], xw[:].indirect(offs_sb[:, 0 : S // 32]))
+        nc.vector.tensor_copy(xg_w[:, S // 2 : S], xw[:].indirect(offs_sb[:, S // 32 : S // 16]))
+        deal(nc.vector, w1w, w1w_raw, LINE // 4, 1, PACK)
+        deal(nc.vector, w1s, w1s_raw[:], LINE, 1, PACK)
 
-        bg_sb = stage.tile([P, PACK, V], F32, name="bg_sb", offset=BG_AT)
-        bg_rows = bg.rearrange("(p t) v -> p t v", t=PACK)
-        nc.sync.dma_start(out=bg_sb[:, 0:2, :], in_=bg_rows[:, 0:2, :])
-        w3w_raw = stage.tile([P, N], U32, name="w3w_raw", offset=W3_WORDS_AT)
-        nc.sync.dma_start(out=w3w_raw[:].bitcast(I32), in_=words_i32(w3_words))
-        w3s_raw = stage.tile([P, N], U8, name="w3s_raw", offset=W3_SCALES_AT)
-        nc.gpsimd.memset(w3s_raw[:].bitcast(I32), 0)
-        load_scales(nc, w3s_raw, w3_scales, W3_ROW)
-        nc.sync.dma_start(out=bg_sb[:, 2:4, :], in_=bg_rows[:, 2:4, :])
 
-        w2w = keep.tile([P, H], U32, name="w2w", align_bytes=64)
+        w2w = [
+            keep.tile([P, P], U32, name="w2w0", align_bytes=64),
+            stage.tile([P, P], U32, name="w2w1", offset=W2_WORDS1_AT, align_bytes=64),
+            keep.tile([P, P], U32, name="w2w2", align_bytes=64),
+            keep.tile([P, P], U32, name="w2w3", align_bytes=64),
+        ]
         w2s = [
-            stage.tile([P, (1, 3)[part] * P], U8, name=f"w2s{part}", offset=W2_SCALES_AT[part], align_bytes=64)
-            for part in range(2)
+            stage.tile([P, P], U8, name="w2s0", offset=W2_SCALES0_AT, align_bytes=64),
+            stage.tile([P, P], U8, name="w2s1", offset=W2_SCALES1_AT, align_bytes=64),
+            keep.tile([P, P], U8, name="w2s2", align_bytes=64),
+            keep.tile([P, P], U8, name="w2s3", align_bytes=64),
         ]
         w2b = [
-            stage.tile([P, 2, P, PACK], BF16, name="w2b0", offset=W2B_AT, align_bytes=64),
-            stage.tile([P, 2, P, PACK], BF16, name="w2b1", offset=W2B_LAST_AT, align_bytes=64),
+            stage.tile([P, 2, P, PACK], BF16, name=f"w2b{pair}", offset=at, align_bytes=64)
+            for pair, at in enumerate((W2B_FIRST_AT, W2B_LAST_AT))
         ]
-        for half, cast in enumerate((nc.vector.tensor_copy, nc.vector.tensor_copy)):
+        for part, m in zip(w2_parts, w2_groups):
             for pair in range(2):
-                cast(
-                    out=w2b[pair][:, :, half * P // 2 : (half + 1) * P // 2, :].rearrange("p u m j -> p m j u"),
-                    in_=w2_raw[:, half].rearrange("p j (m t) -> p m j t", t=PACK)[:, :, :, 2 * pair : 2 * pair + 2],
+                nc.vector.tensor_copy(
+                    out=w2b[pair][:, :, m, :].rearrange("p u m j -> p m j u"),
+                    in_=part.rearrange("p j (m t) -> p m j t", t=PACK)[:, :, :, 2 * pair : 2 * pair + 2],
                 )
 
-        def w2_scales(t0, t1):
-            return w2s[0][:] if t0 == 0 else w2s[1][:, P * (t0 - 1) : P * (t1 - 1)]
-
-        for pair, u0, u1 in ((0, 0, 1), (0, 1, 2), (1, 0, 2)):
+        def quantise_w2(t):
             nc.vector.quantize_mx(
-                out=w2w[:, P * (2 * pair + u0) : P * (2 * pair + u1)].bitcast(FP8X4),
-                scales=w2_scales(2 * pair + u0, 2 * pair + u1),
-                in_=w2b[pair][:, u0:u1].rearrange("p u m j -> p (u m j)"),
+                out=w2w[t][:].bitcast(FP8X4),
+                scales=w2s[t][:],
+                in_=w2b[t // 2][:, t % 2].rearrange("p m j -> p (m j)"),
             )
 
-        def project(words, scales, t, bank_no, cols=slice(0, S)):
+        def project(words, scales, bank_no, cols=slice(0, S)):
             bank = psum.tile([P, cols.stop - cols.start], F32, name="bank", tag=f"bank{bank_no}")
             nc.tensor.matmul_mx(
                 out=bank[:],
-                lhsT=words[:, t * P : (t + 1) * P].bitcast(FP8X4),
+                lhsT=words.bitcast(FP8X4),
                 lhsT_scale=scales,
                 rhs=xg_w[:, cols].bitcast(FP8X4),
                 rhs_scale=xg_s[X_ROW:P, cols],
@@ -164,32 +177,28 @@ def tile_picked_nerfvol_none_po_kernel(
         h_all = keep.tile([P, PACK, V], F32, name="h_all", align_bytes=64)
         w_all = keep.tile([P, PACK, V], F32, name="w_all", align_bytes=64)
         val, dens, e1, e2, a, b, g = {}, {}, {}, {}, {}, {}, {}
-        S_BANK = (0, 1, 3, 4)
-        VAL_BANK = (3, 2, 0, 1)
-        held = stage.tile([P, 3, V], F32, name="held", offset=HELD_AT)
+        S_BANK = (0, 2, 3, 4)
+        VAL_BANK = (5, 7, 0, 1)
+        OUT_BANK = (2, 5, 6, 7)
+        HALVES = (slice(0, S // 2), slice(S // 2, S))
+        held = stage.tile([P, 2, V], F32, name="held", offset=HELD_AT)
+        s_bank = {}
 
         def evacuate_val(t):
             val[t] = keep.tile([P, S], F32, name=f"val{t}")
-            scales = w2_scales(t, t + 1)
-            if t == 0:
-                for half in range(2):
-                    cols = slice(half * S // 2, (half + 1) * S // 2)
-                    copy = (nc.vector.tensor_copy, nc.scalar.copy)[half]
-                    copy(val[t][:, cols], project(w2w, scales, t, 3 + half, cols)[:])
-            else:
-                copy = nc.vector.tensor_copy if t == 1 else nc.scalar.copy
-                copy(val[t][:], project(w2w, scales, t, VAL_BANK[t])[:])
+            nc.scalar.copy(val[t][:], project(w2w[t][:], w2s[t][:], VAL_BANK[t])[:])
+
+        def project_s(t, bank_no, cols=slice(0, S)):
+            return project(w1w[:, t * P : (t + 1) * P], w1s[W1_ROW:P, t * P : (t + 1) * P], bank_no, cols)
 
         def evacuate_dens(t):
-            dens[t] = keep.tile([P, S], F32, name=f"dens{t}")
-            bank = project(w1w, w1s[W1_ROW:P, t * P : (t + 1) * P], t, S_BANK[t])
-            nc.scalar.activation(dens[t][:], bank[:], ACT.Relu)
+            nc.scalar.activation(dens[t][:], s_bank[t][:], ACT.Relu)
 
         def exp_of(out, t, entries):
             nc.scalar.activation(out, dens[t][:].indirect(entries), ACT.Exp, scale=-1.0)
 
         def far_exp(t):
-            e2[t] = held[:, 2, :] if t == 1 else keep.tile([P, V], F32, name=f"e2_{t}", align_bytes=64)[:]
+            e2[t] = keep.tile([P, V], F32, name=f"e2_{t}", align_bytes=64)[:]
             exp_of(e2[t], t, p2_sb[:])
 
         def near_exp(t):
@@ -215,39 +224,59 @@ def tile_picked_nerfvol_none_po_kernel(
             nc.vector.scalar_tensor_tensor(w_all[:, t, :], e1[t], 1.0, g[t][:], ALU.subtract, ALU.mult)
 
         w3w = stage.tile([P, N], U32, name="w3w", offset=W3_DEALT_AT, align_bytes=64)
-        w3s = stage.tile([P, N], U8, name="w3s", offset=W2B_LAST_AT, align_bytes=64)
-        evacuate_dens(0)
+        w3s = stage.tile([P, N], U8, name="w3s", offset=W3_SCALES_DEALT_AT, align_bytes=64)
+        dens[0] = keep.tile([P, S], F32, name="dens0")
+        dens[1] = keep.tile([P, S], F32, name="dens1")
+        dens[2] = stage.tile([P, S], F32, name="dens2", offset=DENS2_AT)
+        dens[3] = stage.tile([P, S], F32, name="dens3", offset=DENS3_AT)
+        through = [keep.tile([P, S], F32, name=f"through{t}") for t in FIRST]
+        dimmed = [keep.tile([P, S], F32, name=f"dimmed{t}") for t in FIRST]
+        e2_first = keep.tile([P, 2, V], F32, name="e2_first")
+        behind = keep.tile([P, 2, V], F32, name="behind")
+        far = keep.tile([P, 2, V], F32, name="far")
+
+        def dim(t, bank_no, cols=slice(0, S)):
+            bank = project(w2w[t][:], w2s[t][:], bank_no, cols)
+            nc.vector.scalar_tensor_tensor(
+                dimmed[t][:, cols], through[t][:, cols], 1.0, bank[:], ALU.subtract, ALU.mult
+            )
+
+        def near_own(t):
+            nc.vector.tensor_scalar(h_all[:, t, :], dimmed[t][:].indirect(p1_sb[:]), -1.0, 0.0, ALU.mult, ALU.add)
+
+        for half, cols in enumerate(HALVES):
+            nc.scalar.activation(dens[0][:, cols], project_s(0, half, cols)[:], ACT.Relu)
+        for t in (1, 2, 3):
+            s_bank[t] = project_s(t, S_BANK[t])
+        nc.scalar.activation(through[0][:, HALVES[0]], dens[0][:, HALVES[0]], ACT.Exp, scale=-1.0)
         evacuate_dens(1)
-        evacuate_val(0)
-        far_exp(0)
-        far_diff(0)
-        evacuate_val(1)
-        far_exp(1)
-        near_exp(0)
-        evacuate_dens(2)
+        nc.scalar.activation(through[0][:, HALVES[1]], dens[0][:, HALVES[1]], ACT.Exp, scale=-1.0)
+        nc.scalar.activation(through[1][:], dens[1][:], ACT.Exp, scale=-1.0)
+        for t in FIRST:
+            exp_of(e2_first[:, t, :], t, p2_sb[:])
+        for t in range(PACK):
+            quantise_w2(t)
+        deal(nc.gpsimd, w3w, w3w_raw, LINE // 4)
+        deal(nc.gpsimd, w3s, w3s_raw[:], LINE)
+        for half, cols in enumerate(HALVES):
+            dim(0, VAL_BANK[0] + half, cols)
+        dim(1, VAL_BANK[1])
+        near_own(0)
         evacuate_val(2)
-        near_exp(1)
-        far_exp(2)
+        evacuate_dens(2)
         evacuate_val(3)
         evacuate_dens(3)
+        far_exp(2)
         far_exp(3)
-        far_weigh(0)
-        far_diff(1)
-        far_blend(0)
-        far_weigh(1)
-        near_diff(0)
-        far_blend(1)
-        near_weigh(0)
-        near_diff(1)
-        far_diff(2)
-        near_weigh(1)
-        far_weigh(2)
-        far_diff(3)
-        far_blend(2)
-        far_weigh(3)
-        far_blend(3)
-        deal(nc.gpsimd, w3w, w3w_raw, LINE // 4)
-        deal(nc.gpsimd, w3s, w3s_raw, LINE)
+        near_exp(0)
+        near_exp(1)
+        nc.vector.tensor_tensor(behind[:], e2_first[:], bg_sb[:, 0:2, :], ALU.mult)
+        near_own(1)
+        for t in FIRST:
+            nc.vector.tensor_tensor(far[:, t, :], dimmed[t][:].indirect(p2_sb[:]), behind[:, t, :], ALU.subtract)
+        for step in (far_diff, far_weigh, far_blend):
+            for t in LAST:
+                step(t)
 
         zw = keep.tile([P, V], U32, name="zw", align_bytes=64)
         zs = keep.tile([P, V], U8, name="zs", align_bytes=64)
@@ -258,51 +287,77 @@ def tile_picked_nerfvol_none_po_kernel(
         of = [keep.tile([P, PACK, P], F32, name=f"of{half}", align_bytes=64) for half in range(2)]
         e1_last = [keep.tile([P, 2, P], F32, name=f"e1_last{half}") for half in range(2)]
         g_last = [keep.tile([P, 2, P], F32, name=f"g_last{half}") for half in range(2)]
-        out_banks = []
+        RAYS = (slice(0, P), slice(P, V))
+        entries = [p1_sb[:, half * P // 16 : (half + 1) * P // 16] for half in range(2)]
+        out_rows = out_0.rearrange("(p t) v -> p t v", t=PACK)
+        out_banks = {}
         for half in range(2):
-            rays = slice(half * P, (half + 1) * P)
-            entries = p1_sb[:, half * P // 16 : (half + 1) * P // 16]
             for u, t in enumerate(LAST):
-                exp_of(e1_last[half][:, u, :], t, entries)
-                nc.vector.tensor_tensor(
-                    g_last[half][:, u, :], val[t][:].indirect(entries), h_all[:, t, rays], ALU.subtract
-                )
-            nc.vector.scalar_tensor_tensor(
-                w_all[:, 2:4, rays], e1_last[half][:], 1.0, g_last[half][:], ALU.subtract, ALU.mult
+                exp_of(e1_last[half][:, u, :], t, entries[half])
+
+        def last_diff(half, u):
+            t = LAST[u]
+            nc.vector.tensor_tensor(
+                g_last[half][:, u, :], val[t][:].indirect(entries[half]), h_all[:, t, RAYS[half]], ALU.subtract
             )
+
+        def last_weigh(half):
+            nc.vector.scalar_tensor_tensor(
+                w_all[:, 2:4, RAYS[half]], e1_last[half][:], 1.0, g_last[half][:], ALU.subtract, ALU.mult
+            )
+
+        def blend(half):
+            rays = RAYS[half]
             nc.vector.tensor_tensor(
                 by_word(zb[half]), by_tile(h_all[:, :, rays]), by_tile(w_all[:, :, rays]), ALU.subtract
             )
+
+        def quantise(words, scales, src, half):
             nc.vector.quantize_mx(
-                out=zw[:, rays].bitcast(FP8X4), scales=zs[:, rays], in_=zb[half][:].rearrange("p v t -> p (v t)")
+                out=words[:, RAYS[half]].bitcast(FP8X4),
+                scales=scales[:, RAYS[half]],
+                in_=src[half][:].rearrange("p v t -> p (v t)"),
             )
-            banks = [
-                psum.tile([P, 2, P], F32, name="out_bank", tag=f"bank{4 + 2 * half + pair}") for pair in range(2)
-            ]
+
+        def last_product(half):
+            quantise(zw, zs, zb, half)
             for t in range(PACK):
+                if t % 2 == 0:
+                    out_banks[half, t // 2] = psum.tile(
+                        [P, 2, P], F32, name="out_bank", tag=f"bank{OUT_BANK[2 * half + t // 2]}"
+                    )
                 nc.tensor.matmul_mx(
-                    out=banks[t // 2][:, t % 2, :],
+                    out=out_banks[half, t // 2][:, t % 2, :],
                     lhsT=w3w[:, t * P : (t + 1) * P].bitcast(FP8X4),
                     lhsT_scale=w3s[W3_ROW:P, t * P : (t + 1) * P],
-                    rhs=zw[:, rays].bitcast(FP8X4),
-                    rhs_scale=zs[:, rays],
+                    rhs=zw[:, RAYS[half]].bitcast(FP8X4),
+                    rhs_scale=zs[:, RAYS[half]],
                     start=True,
                     stop=True,
                 )
-            out_banks.append(banks)
 
-        out_rows = out_0.rearrange("(p t) v -> p t v", t=PACK)
-        out_words = words_i32(out_1)
-        for half, (second_copy, queue) in enumerate(((nc.vector.tensor_copy, nc.sync), (nc.scalar.copy, nc.scalar))):
-            rays = slice(half * P, (half + 1) * P)
-            nc.scalar.copy(of[half][:, 0:2, :], out_banks[half][0][:])
-            second_copy(of[half][:, 2:4, :], out_banks[half][1][:])
-            queue.dma_start(out=out_rows[:, :, rays], in_=of[half][:])
-            nc.vector.tensor_copy(out=by_word(ob[half]), in_=by_tile(of[half][:]))
-            nc.vector.quantize_mx(
-                out=ow[:, rays].bitcast(FP8X4), scales=osc[:, rays], in_=ob[half][:].rearrange("p v t -> p (v t)")
-            )
-            nc.sync.dma_start(out=out_words[:, rays], in_=ow[:, rays].bitcast(I32))
+        last_diff(0, 0)
+        last_diff(0, 1)
+        nc.vector.tensor_tensor(w_all[:, 0:2, :], held[:], far[:], ALU.mult)
+        last_weigh(0)
+        last_diff(1, 0)
+        blend(0)
+        last_diff(1, 1)
+        last_product(0)
+        nc.scalar.copy(of[0][:, 0:2, :], out_banks[0, 0][:])
+        last_weigh(1)
+        blend(1)
+        last_product(1)
+        nc.vector.tensor_copy(of[0][:, 2:4, :], out_banks[0, 1][:])
+        nc.sync.dma_start(out=out_rows[:, :, RAYS[0]], in_=of[0][:])
+        nc.vector.tensor_copy(out=by_word(ob[0]), in_=by_tile(of[0][:]))
+        quantise(ow, osc, ob, 0)
+        nc.scalar.copy(of[1][:, 0:2, :], out_banks[1, 0][:])
+        nc.scalar.copy(of[1][:, 2:4, :], out_banks[1, 1][:])
+        nc.scalar.dma_start(out=out_rows[:, :, RAYS[1]], in_=of[1][:])
+        nc.vector.tensor_copy(out=by_word(ob[1]), in_=by_tile(of[1][:]))
+        quantise(ow, osc, ob, 1)
+        nc.sync.dma_start(out=words_i32(out_1), in_=ow[:].bitcast(I32))
         for r in range(PACK):
             queue = nc.sync if r % 2 else nc.scalar
             queue.dma_start(out=out_2[0].bitcast(I32)[r:BLOCKS:PACK, :], in_=osc[:].bitcast(I32)[r:P:QUAD, :])

@@ -19,44 +19,51 @@ P = 128
 PACK = 4
 QUAD = 32
 BLOCKS = 16
+GROUP = 16
 LINE = 16
+ALIGN = 64
+STEP = 32
 X_ROW, W1_ROW, W3_ROW = 4, 8, 12
 FIRST, LAST = (0, 1), (2, 3)
+SAMPLES = (slice(0, S // 2), slice(S // 2, S))
+RAYS = (slice(0, V // 2), slice(V // 2, V))
+
+S_BANKS = ((0, 1), (2,), (3,), (4,))
+VAL_BANKS = ((5, 6), (7,), (0,), (1,))
+OUT_BANKS = ((2, 5), (6, 7))
 
 WORDS_AT = 0
-W2_AT = WORDS_AT + 4 * (N + H)
-ZEROS_AT = W2_AT - H // 2
-X_WORDS_AT = W2_AT + 4 * PACK * (H + V)
+FLOATS_AT = WORDS_AT + 4 * (N + H)
+ZEROS_AT = FLOATS_AT - H // 2
+X_WORDS_AT = FLOATS_AT + 4 * PACK * (H + V)
 W2B_LAST_AT = X_WORDS_AT + 4 * T + N
-W1_SCALES_AT = W2B_LAST_AT + 4 * H - 64
-W2B_FIRST_AT = W1_SCALES_AT + H - 64
-W3_SCALES_DEALT_AT = W2B_LAST_AT + 64 - N
-W3_DEALT_AT = W2B_LAST_AT + 64
+W1_SCALES_AT = W2B_LAST_AT + 4 * H - ALIGN
+W2B_FIRST_AT = W1_SCALES_AT + H - ALIGN
+W3_SCALES_AT = W2B_LAST_AT + ALIGN - N
+W3_WORDS_AT = W2B_LAST_AT + ALIGN
 DENS2_AT = W2B_FIRST_AT + 4 * H
-W2_SCALES1_AT = DENS2_AT + 4 * S - 64
-HELD_AT = W2_SCALES1_AT + P - 32
-DENS3_AT = HELD_AT + 4 * 2 * V + 32
-W2_WORDS1_AT = DENS3_AT + 4 * S - 64
-W2_SCALES0_AT = W2_WORDS1_AT + 4 * P
-W2_SPLIT = 64
+W2_SCALES1_AT = DENS2_AT + 4 * S - ALIGN
+NEAR_AT = W2_SCALES1_AT + P - STEP
+DENS3_AT = NEAR_AT + 4 * PACK * V + STEP
+W2_WORDS1_AT = DENS3_AT + 4 * S - ALIGN
 
 
 def words_i32(ap):
     return ap[0].rearrange("p n t -> p (n t)").bitcast(I32)
 
 
-def load_scales(nc, plane, scales, first):
-    for r in range(PACK):
-        nc.sync.dma_start(
+def load_scales(queue, plane, scales, first, rows=range(PACK)):
+    for r in rows:
+        queue.dma_start(
             out=plane[:].bitcast(I32)[first + r : P : QUAD, :],
             in_=scales[0].bitcast(I32)[r:BLOCKS:PACK, :],
         )
 
 
-def deal(engine, dst, src, run, t0=0, t1=PACK):
+def deal(engine, dst, src, run, tiles=slice(0, PACK)):
     engine.tensor_copy(
-        out=dst[:].rearrange("p (t c i) -> p c t i", t=PACK, i=run)[:, :, t0:t1, :],
-        in_=src.rearrange("p (c i t) -> p c t i", t=PACK, i=run)[:, :, t0:t1, :],
+        out=dst.rearrange("p (t c i) -> p c t i", t=PACK, i=run)[:, :, tiles, :],
+        in_=src.rearrange("p (c i t) -> p c t i", t=PACK, i=run)[:, :, tiles, :],
     )
 
 
@@ -68,6 +75,10 @@ def by_word(tile):
     return tile[:].rearrange("p (c i) t -> p c t i", i=PACK)
 
 
+def entries(offsets, part):
+    return offsets[:, part.start // GROUP : part.stop // GROUP]
+
+
 def tile_picked_nerfvol_none_po_kernel(
     tc, x_words, x_scales, w1_words, w1_scales, w2, bg, w3_words, w3_scales, offs, p1, p2, out_0, out_1, out_2
 ):
@@ -77,240 +88,178 @@ def tile_picked_nerfvol_none_po_kernel(
         stage = ctx.enter_context(tc.tile_pool(name="stage", bufs=1))
         psum = ctx.enter_context(tc.psum_pool(name="psum", bufs=1))
 
-        offs_sb = keep.tile([P, S // 16], U16, name="offs_sb")
-        p1_sb = keep.tile([P, V // 16], U16, name="p1_sb")
-        p2_sb = keep.tile([P, V // 16], U16, name="p2_sb")
+        offs_sb = keep.tile([P, S // GROUP], U16, name="offs_sb")
+        p1_sb = keep.tile([P, V // GROUP], U16, name="p1_sb")
+        p2_sb = keep.tile([P, V // GROUP], U16, name="p2_sb")
         xw = stage.tile([P, T], U32, name="xw", offset=X_WORDS_AT)
-        xs = keep.tile([P, T], U8, name="xs", tag="xs", align_bytes=64)
-        w1s_raw = stage.tile([P, H], U8, name="w1s_raw", offset=W1_SCALES_AT, align_bytes=64)
+        xs = keep.tile([P, T], U8, name="xs", tag="xs", align_bytes=ALIGN)
+        w1s_raw = stage.tile([P, H], U8, name="w1s_raw", offset=W1_SCALES_AT, align_bytes=ALIGN)
         zeros = stage.tile([P, H // 4], I32, name="zeros", offset=ZEROS_AT)
+        w3s_raw = keep.tile([P, N], U8, name="w3s_raw")
         nc.vector.memset(xs[:].bitcast(I32), 0)
         nc.gpsimd.memset(zeros[:], 0)
         nc.vector.tensor_copy(w1s_raw[:].bitcast(I32), zeros[:])
-        w3s_raw = keep.tile([P, N], U8, name="w3s_raw")
         nc.vector.memset(w3s_raw[:].bitcast(I32), 0)
 
-        nc.sync.dma_start(offs_sb[:], offs)
-        for part in range(2):
-            cols = slice(part * T // 4, (part + 1) * T // 4)
-            nc.sync.dma_start(out=xw[:, cols].bitcast(I32), in_=words_i32(x_words)[:, cols])
-        load_scales(nc, xs, x_scales, X_ROW)
-        nc.sync.dma_start(out=xw[:, T // 2 : T].bitcast(I32), in_=words_i32(x_words)[:, T // 2 : T])
         words_raw = stage.tile([P, N + H], U32, name="words_raw", offset=WORDS_AT)
         w3w_raw, w1w_raw = words_raw[:, 0:N], words_raw[:, N : N + H]
-        nc.sync.dma_start(out=w1w_raw.bitcast(I32), in_=words_i32(w1_words))
-        w2_raw = stage.tile([P, PACK * (H + V)], F32, name="w2_raw", offset=W2_AT)
-        w2_groups = (slice(0, W2_SPLIT), slice(W2_SPLIT, P))
-        w2_parts = [
-            w2_raw[:, PACK * PACK * m.start : PACK * PACK * m.stop].rearrange("p (j c) -> p j c", j=PACK)
-            for m in w2_groups
-        ]
-        w2_rows = w2.rearrange("(p j) c -> p j c", j=PACK)
-        load_scales(nc, w1s_raw, w1_scales, W1_ROW)
-        for part, m in zip(w2_parts, w2_groups):
-            nc.sync.dma_start(out=part, in_=w2_rows[:, :, PACK * m.start : PACK * m.stop])
-        bg_sb = w2_raw[:, PACK * H : PACK * (H + V)].rearrange("p (t v) -> p t v", t=PACK)
+        floats = stage.tile([P, PACK * (H + V)], F32, name="floats", offset=FLOATS_AT)
+        w2_raw = floats[:, 0 : PACK * H].rearrange("p (half j c) -> p half j c", half=2, j=PACK)
+        bg_sb = floats[:, PACK * H : PACK * (H + V)].rearrange("p (t v) -> p t v", t=PACK)
+        w2_rows = w2.rearrange("(p j) (half c) -> p half j c", j=PACK, half=2)
         bg_rows = bg.rearrange("(p t) v -> p t v", t=PACK)
+
+        def load_x_words(start, stop):
+            nc.sync.dma_start(out=xw[:, start:stop].bitcast(I32), in_=words_i32(x_words)[:, start:stop])
+
+        nc.sync.dma_start(offs_sb[:], offs)
+        load_x_words(0, T // 4)
+        load_x_words(T // 4, T // 2)
+        load_scales(nc.sync, xs, x_scales, X_ROW)
+        load_x_words(T // 2, T)
+        nc.sync.dma_start(out=w1w_raw.bitcast(I32), in_=words_i32(w1_words))
+        load_scales(nc.sync, w1s_raw, w1_scales, W1_ROW)
+        for half in range(2):
+            nc.sync.dma_start(out=w2_raw[:, half], in_=w2_rows[:, half])
         nc.sync.dma_start(p2_sb[:], p2)
         nc.sync.dma_start(p1_sb[:], p1)
         nc.sync.dma_start(out=w3w_raw.bitcast(I32), in_=words_i32(w3_words))
-        nc.sync.dma_start(out=bg_sb[:, 0:2, :], in_=bg_rows[:, 0:2, :])
-        load_scales(nc, w3s_raw, w3_scales, W3_ROW)
-        nc.sync.dma_start(out=bg_sb[:, 2:4, :], in_=bg_rows[:, 2:4, :])
+        for pair in range(2):
+            nc.sync.dma_start(out=bg_sb[:, 2 * pair : 2 * pair + 2, :], in_=bg_rows[:, 2 * pair : 2 * pair + 2, :])
+        load_scales(nc.gpsimd, w3s_raw, w3_scales, W3_ROW, range(0, 2))
+        load_scales(nc.sync, w3s_raw, w3_scales, W3_ROW, range(2, PACK))
 
-        xg_s = keep.tile([P, S], U8, name="xg_s", align_bytes=64)
+        xg_s = keep.tile([P, S], U8, name="xg_s", align_bytes=ALIGN)
         nc.vector.tensor_copy(xg_s[:], xs[:].indirect(offs_sb[:]))
-        xg_w = keep.tile([P, S], U32, name="xg_w", tag="xs", align_bytes=64)
-        w1w = keep.tile([P, H], U32, name="w1w", align_bytes=64)
-        w1s = keep.tile([P, H], U8, name="w1s", align_bytes=64)
-        deal(nc.gpsimd, w1w, w1w_raw, LINE // 4, 0, 1)
-        deal(nc.gpsimd, w1s, w1s_raw[:], LINE, 0, 1)
-        nc.vector.tensor_copy(xg_w[:, 0 : S // 2], xw[:].indirect(offs_sb[:, 0 : S // 32]))
-        nc.vector.tensor_copy(xg_w[:, S // 2 : S], xw[:].indirect(offs_sb[:, S // 32 : S // 16]))
-        deal(nc.vector, w1w, w1w_raw, LINE // 4, 1, PACK)
-        deal(nc.vector, w1s, w1s_raw[:], LINE, 1, PACK)
+        xg_w = keep.tile([P, S], U32, name="xg_w", tag="xs", align_bytes=ALIGN)
+        w1w = keep.tile([P, H], U32, name="w1w", align_bytes=ALIGN)
+        w1s = keep.tile([P, H], U8, name="w1s", align_bytes=ALIGN)
+        deal(nc.gpsimd, w1w[:], w1w_raw, LINE // 4, slice(0, 1))
+        deal(nc.gpsimd, w1s[:], w1s_raw[:], LINE, slice(0, 1))
+        for part in SAMPLES:
+            nc.vector.tensor_copy(xg_w[:, part], xw[:].indirect(entries(offs_sb, part)))
+        deal(nc.vector, w1w[:], w1w_raw, LINE // 4, slice(1, PACK))
+        deal(nc.vector, w1s[:], w1s_raw[:], LINE, slice(1, PACK))
 
-
-        w2w = [
-            keep.tile([P, P], U32, name="w2w0", align_bytes=64),
-            stage.tile([P, P], U32, name="w2w1", offset=W2_WORDS1_AT, align_bytes=64),
-            keep.tile([P, P], U32, name="w2w2", align_bytes=64),
-            keep.tile([P, P], U32, name="w2w3", align_bytes=64),
-        ]
-        w2s = [
-            stage.tile([P, P], U8, name="w2s0", offset=W2_SCALES0_AT, align_bytes=64),
-            stage.tile([P, P], U8, name="w2s1", offset=W2_SCALES1_AT, align_bytes=64),
-            keep.tile([P, P], U8, name="w2s2", align_bytes=64),
-            keep.tile([P, P], U8, name="w2s3", align_bytes=64),
-        ]
         w2b = [
-            stage.tile([P, 2, P, PACK], BF16, name=f"w2b{pair}", offset=at, align_bytes=64)
+            stage.tile([P, 2, P, PACK], BF16, name=f"w2b{pair}", offset=at, align_bytes=ALIGN)
             for pair, at in enumerate((W2B_FIRST_AT, W2B_LAST_AT))
         ]
-        for part, m in zip(w2_parts, w2_groups):
+        for half in range(2):
             for pair in range(2):
                 nc.vector.tensor_copy(
-                    out=w2b[pair][:, :, m, :].rearrange("p u m j -> p m j u"),
-                    in_=part.rearrange("p j (m t) -> p m j t", t=PACK)[:, :, :, 2 * pair : 2 * pair + 2],
+                    out=w2b[pair][:, :, half * P // 2 : (half + 1) * P // 2, :].rearrange("p u m j -> p m j u"),
+                    in_=w2_raw[:, half].rearrange("p j (m t) -> p m j t", t=PACK)[:, :, :, 2 * pair : 2 * pair + 2],
                 )
+        w2w = {t: keep.tile([P, P], U32, name=f"w2w{t}", align_bytes=ALIGN) for t in (0, 2, 3)}
+        w2s = {t: keep.tile([P, P], U8, name=f"w2s{t}", align_bytes=ALIGN) for t in (0, 2, 3)}
+        w2w[1] = stage.tile([P, P], U32, name="w2w1", offset=W2_WORDS1_AT, align_bytes=ALIGN)
+        w2s[1] = stage.tile([P, P], U8, name="w2s1", offset=W2_SCALES1_AT, align_bytes=ALIGN)
 
-        def quantise_w2(t):
-            nc.vector.quantize_mx(
-                out=w2w[t][:].bitcast(FP8X4),
-                scales=w2s[t][:],
-                in_=w2b[t // 2][:, t % 2].rearrange("p m j -> p (m j)"),
-            )
-
-        def project(words, scales, bank_no, cols=slice(0, S)):
-            bank = psum.tile([P, cols.stop - cols.start], F32, name="bank", tag=f"bank{bank_no}")
+        def project(words, scales, bank_no, part=slice(0, S)):
+            bank = psum.tile([P, part.stop - part.start], F32, name="bank", tag=f"bank{bank_no}")
             nc.tensor.matmul_mx(
                 out=bank[:],
                 lhsT=words.bitcast(FP8X4),
                 lhsT_scale=scales,
-                rhs=xg_w[:, cols].bitcast(FP8X4),
-                rhs_scale=xg_s[X_ROW:P, cols],
+                rhs=xg_w[:, part].bitcast(FP8X4),
+                rhs_scale=xg_s[X_ROW:P, part],
                 start=True,
                 stop=True,
             )
             return bank
 
-        h_all = keep.tile([P, PACK, V], F32, name="h_all", align_bytes=64)
-        w_all = keep.tile([P, PACK, V], F32, name="w_all", align_bytes=64)
-        val, dens, e1, e2, a, b, g = {}, {}, {}, {}, {}, {}, {}
-        S_BANK = (0, 2, 3, 4)
-        VAL_BANK = (5, 7, 0, 1)
-        OUT_BANK = (2, 5, 6, 7)
-        HALVES = (slice(0, S // 2), slice(S // 2, S))
-        held = stage.tile([P, 2, V], F32, name="held", offset=HELD_AT)
-        s_bank = {}
+        def project_s(t, bank_no, part=slice(0, S)):
+            return project(w1w[:, t * P : (t + 1) * P], w1s[W1_ROW:P, t * P : (t + 1) * P], bank_no, part)
 
-        def evacuate_val(t):
-            val[t] = keep.tile([P, S], F32, name=f"val{t}")
-            nc.scalar.copy(val[t][:], project(w2w[t][:], w2s[t][:], VAL_BANK[t])[:])
+        def project_val(t, bank_no, part=slice(0, S)):
+            return project(w2w[t][:], w2s[t][:], bank_no, part)
 
-        def project_s(t, bank_no, cols=slice(0, S)):
-            return project(w1w[:, t * P : (t + 1) * P], w1s[W1_ROW:P, t * P : (t + 1) * P], bank_no, cols)
+        dens = [keep.tile([P, S], F32, name=f"dens{t}") for t in FIRST] + [
+            stage.tile([P, S], F32, name=f"dens{t}", offset=at) for t, at in zip(LAST, (DENS2_AT, DENS3_AT))
+        ]
+        e_all = keep.tile([P, S], F32, name="e_all")
+        e2 = keep.tile([P, PACK, V], F32, name="e2")
+        e1 = stage.tile([P, PACK, V], F32, name="e1", offset=NEAR_AT)
 
-        def evacuate_dens(t):
+        def exp_at(out, t, offsets):
+            nc.scalar.activation(out, dens[t][:].indirect(offsets), ACT.Exp, scale=-1.0)
+
+        for bank_no, part in zip(S_BANKS[0], SAMPLES):
+            nc.scalar.activation(dens[0][:, part], project_s(0, bank_no, part)[:], ACT.Relu)
+        s_bank = {t: project_s(t, S_BANKS[t][0]) for t in range(1, PACK)}
+        nc.scalar.activation(e_all[:, SAMPLES[0]], dens[0][:, SAMPLES[0]], ACT.Exp, scale=-1.0)
+        nc.scalar.activation(dens[1][:], s_bank[1][:], ACT.Relu)
+        nc.scalar.activation(e_all[:, SAMPLES[1]], dens[0][:, SAMPLES[1]], ACT.Exp, scale=-1.0)
+        for t in FIRST:
+            exp_at(e2[:, t, :], t, p2_sb[:])
+
+        for t in range(PACK):
+            nc.vector.quantize_mx(
+                out=w2w[t][:].bitcast(FP8X4), scales=w2s[t][:], in_=w2b[t // 2][:, t % 2].rearrange("p m j -> p (m j)")
+            )
+
+        w3w = stage.tile([P, N], U32, name="w3w", offset=W3_WORDS_AT, align_bytes=ALIGN)
+        w3s = stage.tile([P, N], U8, name="w3s", offset=W3_SCALES_AT, align_bytes=ALIGN)
+        deal(nc.gpsimd, w3w[:], w3w_raw, LINE // 4)
+        deal(nc.gpsimd, w3s[:], w3s_raw[:], LINE)
+
+        base = keep.tile([P, PACK, V], F32, name="base", align_bytes=ALIGN)
+        cut = keep.tile([P, PACK, V], F32, name="cut", align_bytes=ALIGN)
+        dim = keep.tile([P, S], F32, name="dim")
+        val = {t: keep.tile([P, S], F32, name=f"val{t}") for t in range(1, PACK)}
+        for bank_no, part in zip(VAL_BANKS[0], SAMPLES):
+            bank = project_val(0, bank_no, part)
+            nc.vector.scalar_tensor_tensor(dim[:, part], e_all[:, part], 1.0, bank[:], ALU.subtract, ALU.mult)
+        nc.vector.tensor_copy(val[1][:], project_val(1, VAL_BANKS[1][0])[:])
+
+        for t in LAST:
+            nc.scalar.copy(val[t][:], project_val(t, VAL_BANKS[t][0])[:])
             nc.scalar.activation(dens[t][:], s_bank[t][:], ACT.Relu)
+        for t in LAST:
+            exp_at(e2[:, t, :], t, p2_sb[:])
+        for t in range(PACK):
+            exp_at(e1[:, t, :], t, p1_sb[:])
 
-        def exp_of(out, t, entries):
-            nc.scalar.activation(out, dens[t][:].indirect(entries), ACT.Exp, scale=-1.0)
-
-        def far_exp(t):
-            e2[t] = keep.tile([P, V], F32, name=f"e2_{t}", align_bytes=64)[:]
-            exp_of(e2[t], t, p2_sb[:])
-
-        def near_exp(t):
-            e1[t] = held[:, t, :]
-            exp_of(e1[t], t, p1_sb[:])
+        e2_bg = keep.tile([P, V], F32, name="e2_bg")
+        far = keep.tile([P, V], F32, name="far")
+        a = {t: keep.tile([P, V], F32, name=f"a{t}") for t in val}
+        b = {t: keep.tile([P, V], F32, name=f"b{t}") for t in val}
+        g = keep.tile([P, PACK - 1, V], F32, name="g")
 
         def far_diff(t):
-            a[t] = keep.tile([P, V], F32, name=f"a{t}", align_bytes=64)
             nc.vector.tensor_tensor(a[t][:], val[t][:].indirect(p2_sb[:]), bg_sb[:, t, :], ALU.subtract)
 
         def far_weigh(t):
-            b[t] = keep.tile([P, V], F32, name=f"b{t}", align_bytes=64)
-            nc.vector.scalar_tensor_tensor(b[t][:], e2[t], 1.0, a[t][:], ALU.subtract, ALU.mult)
+            nc.vector.scalar_tensor_tensor(b[t][:], e2[:, t, :], 1.0, a[t][:], ALU.subtract, ALU.mult)
 
         def far_blend(t):
-            nc.vector.tensor_tensor(h_all[:, t, :], bg_sb[:, t, :], b[t][:], ALU.subtract)
+            nc.vector.tensor_tensor(base[:, t, :], bg_sb[:, t, :], b[t][:], ALU.subtract)
 
         def near_diff(t):
-            g[t] = keep.tile([P, V], F32, name=f"g{t}")
-            nc.vector.tensor_tensor(g[t][:], val[t][:].indirect(p1_sb[:]), h_all[:, t, :], ALU.subtract)
+            nc.vector.tensor_tensor(g[:, t - 1, :], val[t][:].indirect(p1_sb[:]), base[:, t, :], ALU.subtract)
 
-        def near_weigh(t):
-            nc.vector.scalar_tensor_tensor(w_all[:, t, :], e1[t], 1.0, g[t][:], ALU.subtract, ALU.mult)
-
-        w3w = stage.tile([P, N], U32, name="w3w", offset=W3_DEALT_AT, align_bytes=64)
-        w3s = stage.tile([P, N], U8, name="w3s", offset=W3_SCALES_DEALT_AT, align_bytes=64)
-        dens[0] = keep.tile([P, S], F32, name="dens0")
-        dens[1] = keep.tile([P, S], F32, name="dens1")
-        dens[2] = stage.tile([P, S], F32, name="dens2", offset=DENS2_AT)
-        dens[3] = stage.tile([P, S], F32, name="dens3", offset=DENS3_AT)
-        through = [keep.tile([P, S], F32, name=f"through{t}") for t in FIRST]
-        dimmed = [keep.tile([P, S], F32, name=f"dimmed{t}") for t in FIRST]
-        e2_first = keep.tile([P, 2, V], F32, name="e2_first")
-        behind = keep.tile([P, 2, V], F32, name="behind")
-        far = keep.tile([P, 2, V], F32, name="far")
-
-        def dim(t, bank_no, cols=slice(0, S)):
-            bank = project(w2w[t][:], w2s[t][:], bank_no, cols)
-            nc.vector.scalar_tensor_tensor(
-                dimmed[t][:, cols], through[t][:, cols], 1.0, bank[:], ALU.subtract, ALU.mult
-            )
-
-        def near_own(t):
-            nc.vector.tensor_scalar(h_all[:, t, :], dimmed[t][:].indirect(p1_sb[:]), -1.0, 0.0, ALU.mult, ALU.add)
-
-        for half, cols in enumerate(HALVES):
-            nc.scalar.activation(dens[0][:, cols], project_s(0, half, cols)[:], ACT.Relu)
-        for t in (1, 2, 3):
-            s_bank[t] = project_s(t, S_BANK[t])
-        nc.scalar.activation(through[0][:, HALVES[0]], dens[0][:, HALVES[0]], ACT.Exp, scale=-1.0)
-        evacuate_dens(1)
-        nc.scalar.activation(through[0][:, HALVES[1]], dens[0][:, HALVES[1]], ACT.Exp, scale=-1.0)
-        nc.scalar.activation(through[1][:], dens[1][:], ACT.Exp, scale=-1.0)
-        for t in FIRST:
-            exp_of(e2_first[:, t, :], t, p2_sb[:])
-        for t in range(PACK):
-            quantise_w2(t)
-        deal(nc.gpsimd, w3w, w3w_raw, LINE // 4)
-        deal(nc.gpsimd, w3s, w3s_raw[:], LINE)
-        for half, cols in enumerate(HALVES):
-            dim(0, VAL_BANK[0] + half, cols)
-        dim(1, VAL_BANK[1])
-        near_own(0)
-        evacuate_val(2)
-        evacuate_dens(2)
-        evacuate_val(3)
-        evacuate_dens(3)
-        far_exp(2)
-        far_exp(3)
-        near_exp(0)
-        near_exp(1)
-        nc.vector.tensor_tensor(behind[:], e2_first[:], bg_sb[:, 0:2, :], ALU.mult)
-        near_own(1)
-        for t in FIRST:
-            nc.vector.tensor_tensor(far[:, t, :], dimmed[t][:].indirect(p2_sb[:]), behind[:, t, :], ALU.subtract)
-        for step in (far_diff, far_weigh, far_blend):
+        nc.vector.tensor_scalar(base[:, 0, :], dim[:].indirect(p1_sb[:]), -1.0, 0.0, ALU.mult, ALU.add)
+        nc.vector.tensor_tensor(e2_bg[:], e2[:, 0, :], bg_sb[:, 0, :], ALU.mult)
+        far_diff(1)
+        nc.vector.tensor_tensor(far[:], dim[:].indirect(p2_sb[:]), e2_bg[:], ALU.subtract)
+        far_weigh(1)
+        far_diff(2)
+        far_blend(1)
+        far_diff(3)
+        near_diff(1)
+        for step in (far_weigh, far_blend, near_diff):
             for t in LAST:
                 step(t)
+        nc.vector.tensor_tensor(cut[:, 0, :], e1[:, 0, :], far[:], ALU.mult)
 
-        zw = keep.tile([P, V], U32, name="zw", align_bytes=64)
-        zs = keep.tile([P, V], U8, name="zs", align_bytes=64)
-        ow = keep.tile([P, V], U32, name="ow", align_bytes=64)
-        osc = keep.tile([P, V], U8, name="osc", align_bytes=64)
-        zb = [keep.tile([P, P, PACK], BF16, name=f"zb{half}", align_bytes=64) for half in range(2)]
-        ob = [keep.tile([P, P, PACK], BF16, name=f"ob{half}", align_bytes=64) for half in range(2)]
-        of = [keep.tile([P, PACK, P], F32, name=f"of{half}", align_bytes=64) for half in range(2)]
-        e1_last = [keep.tile([P, 2, P], F32, name=f"e1_last{half}") for half in range(2)]
-        g_last = [keep.tile([P, 2, P], F32, name=f"g_last{half}") for half in range(2)]
-        RAYS = (slice(0, P), slice(P, V))
-        entries = [p1_sb[:, half * P // 16 : (half + 1) * P // 16] for half in range(2)]
-        out_rows = out_0.rearrange("(p t) v -> p t v", t=PACK)
-        out_banks = {}
-        for half in range(2):
-            for u, t in enumerate(LAST):
-                exp_of(e1_last[half][:, u, :], t, entries[half])
-
-        def last_diff(half, u):
-            t = LAST[u]
-            nc.vector.tensor_tensor(
-                g_last[half][:, u, :], val[t][:].indirect(entries[half]), h_all[:, t, RAYS[half]], ALU.subtract
-            )
-
-        def last_weigh(half):
-            nc.vector.scalar_tensor_tensor(
-                w_all[:, 2:4, RAYS[half]], e1_last[half][:], 1.0, g_last[half][:], ALU.subtract, ALU.mult
-            )
-
-        def blend(half):
-            rays = RAYS[half]
-            nc.vector.tensor_tensor(
-                by_word(zb[half]), by_tile(h_all[:, :, rays]), by_tile(w_all[:, :, rays]), ALU.subtract
-            )
+        zw = keep.tile([P, V], U32, name="zw", align_bytes=ALIGN)
+        zs = keep.tile([P, V], U8, name="zs", align_bytes=ALIGN)
+        ow = keep.tile([P, V], U32, name="ow", align_bytes=ALIGN)
+        osc = keep.tile([P, V], U8, name="osc", align_bytes=ALIGN)
+        zb = [keep.tile([P, V // 2, PACK], BF16, name=f"zb{half}", align_bytes=ALIGN) for half in range(2)]
+        ob = [keep.tile([P, V // 2, PACK], BF16, name=f"ob{half}", align_bytes=ALIGN) for half in range(2)]
+        of = [keep.tile([P, PACK, V // 2], F32, name=f"of{half}", align_bytes=ALIGN) for half in range(2)]
 
         def quantise(words, scales, src, half):
             nc.vector.quantize_mx(
@@ -319,44 +268,35 @@ def tile_picked_nerfvol_none_po_kernel(
                 in_=src[half][:].rearrange("p v t -> p (v t)"),
             )
 
-        def last_product(half):
+        for rays in RAYS:
+            nc.vector.scalar_tensor_tensor(
+                cut[:, 1:PACK, rays], e1[:, 1:PACK, rays], 1.0, g[:, :, rays], ALU.subtract, ALU.mult
+            )
+        for half, rays in enumerate(RAYS):
+            nc.vector.tensor_tensor(by_word(zb[half]), by_tile(base[:, :, rays]), by_tile(cut[:, :, rays]), ALU.subtract)
+        out_banks = []
+        for half, rays in enumerate(RAYS):
             quantise(zw, zs, zb, half)
+            banks = [psum.tile([P, 2, V // 2], F32, name="out_bank", tag=f"bank{no}") for no in OUT_BANKS[half]]
             for t in range(PACK):
-                if t % 2 == 0:
-                    out_banks[half, t // 2] = psum.tile(
-                        [P, 2, P], F32, name="out_bank", tag=f"bank{OUT_BANK[2 * half + t // 2]}"
-                    )
                 nc.tensor.matmul_mx(
-                    out=out_banks[half, t // 2][:, t % 2, :],
+                    out=banks[t // 2][:, t % 2, :],
                     lhsT=w3w[:, t * P : (t + 1) * P].bitcast(FP8X4),
                     lhsT_scale=w3s[W3_ROW:P, t * P : (t + 1) * P],
-                    rhs=zw[:, RAYS[half]].bitcast(FP8X4),
-                    rhs_scale=zs[:, RAYS[half]],
+                    rhs=zw[:, rays].bitcast(FP8X4),
+                    rhs_scale=zs[:, rays],
                     start=True,
                     stop=True,
                 )
+            out_banks.append(banks)
 
-        last_diff(0, 0)
-        last_diff(0, 1)
-        nc.vector.tensor_tensor(w_all[:, 0:2, :], held[:], far[:], ALU.mult)
-        last_weigh(0)
-        last_diff(1, 0)
-        blend(0)
-        last_diff(1, 1)
-        last_product(0)
-        nc.scalar.copy(of[0][:, 0:2, :], out_banks[0, 0][:])
-        last_weigh(1)
-        blend(1)
-        last_product(1)
-        nc.vector.tensor_copy(of[0][:, 2:4, :], out_banks[0, 1][:])
-        nc.sync.dma_start(out=out_rows[:, :, RAYS[0]], in_=of[0][:])
-        nc.vector.tensor_copy(out=by_word(ob[0]), in_=by_tile(of[0][:]))
-        quantise(ow, osc, ob, 0)
-        nc.scalar.copy(of[1][:, 0:2, :], out_banks[1, 0][:])
-        nc.scalar.copy(of[1][:, 2:4, :], out_banks[1, 1][:])
-        nc.scalar.dma_start(out=out_rows[:, :, RAYS[1]], in_=of[1][:])
-        nc.vector.tensor_copy(out=by_word(ob[1]), in_=by_tile(of[1][:]))
-        quantise(ow, osc, ob, 1)
+        out_rows = out_0.rearrange("(p t) v -> p t v", t=PACK)
+        for half, (second_copy, queue) in enumerate(((nc.vector.tensor_copy, nc.sync), (nc.scalar.copy, nc.scalar))):
+            nc.scalar.copy(of[half][:, 0:2, :], out_banks[half][0][:])
+            second_copy(of[half][:, 2:4, :], out_banks[half][1][:])
+            queue.dma_start(out=out_rows[:, :, RAYS[half]], in_=of[half][:])
+            nc.vector.tensor_copy(out=by_word(ob[half]), in_=by_tile(of[half][:]))
+            quantise(ow, osc, ob, half)
         nc.sync.dma_start(out=words_i32(out_1), in_=ow[:].bitcast(I32))
         for r in range(PACK):
             queue = nc.sync if r % 2 else nc.scalar

@@ -41,11 +41,6 @@ W1_SCALES_AT = W2B_LAST_AT + 4 * H - ALIGN
 W2B_FIRST_AT = W1_SCALES_AT + H - ALIGN
 W3_SCALES_AT = W2B_LAST_AT + ALIGN - N
 W3_WORDS_AT = W2B_LAST_AT + ALIGN
-DENS2_AT = W2B_FIRST_AT + 4 * H
-W2_SCALES1_AT = DENS2_AT + 4 * S - ALIGN
-NEAR_AT = W2_SCALES1_AT + P - STEP
-DENS3_AT = NEAR_AT + 4 * PACK * V + STEP
-W2_WORDS1_AT = DENS3_AT + 4 * S - ALIGN
 
 
 def words_i32(ap):
@@ -145,16 +140,18 @@ def tile_picked_nerfvol_none_po_kernel(
             stage.tile([P, 2, P, PACK], BF16, name=f"w2b{pair}", offset=at, align_bytes=ALIGN)
             for pair, at in enumerate((W2B_FIRST_AT, W2B_LAST_AT))
         ]
-        for half in range(2):
+
+        def cast_w2(half):
             for pair in range(2):
                 nc.vector.tensor_copy(
                     out=w2b[pair][:, :, half * P // 2 : (half + 1) * P // 2, :].rearrange("p u m j -> p m j u"),
                     in_=w2_raw[:, half].rearrange("p j (m t) -> p m j t", t=PACK)[:, :, :, 2 * pair : 2 * pair + 2],
                 )
-        w2w = {t: keep.tile([P, P], U32, name=f"w2w{t}", align_bytes=ALIGN) for t in (0, 2, 3)}
-        w2s = {t: keep.tile([P, P], U8, name=f"w2s{t}", align_bytes=ALIGN) for t in (0, 2, 3)}
-        w2w[1] = stage.tile([P, P], U32, name="w2w1", offset=W2_WORDS1_AT, align_bytes=ALIGN)
-        w2s[1] = stage.tile([P, P], U8, name="w2s1", offset=W2_SCALES1_AT, align_bytes=ALIGN)
+
+        cast_w2(0)
+        cast_w2(1)
+        w2w = [keep.tile([P, P], U32, name=f"w2w{t}", align_bytes=ALIGN) for t in range(PACK)]
+        w2s = [keep.tile([P, P], U8, name=f"w2s{t}", align_bytes=ALIGN) for t in range(PACK)]
 
         def project(words, scales, bank_no, part=slice(0, S)):
             bank = psum.tile([P, part.stop - part.start], F32, name="bank", tag=f"bank{bank_no}")
@@ -175,24 +172,32 @@ def tile_picked_nerfvol_none_po_kernel(
         def project_val(t, bank_no, part=slice(0, S)):
             return project(w2w[t][:], w2s[t][:], bank_no, part)
 
-        dens = [keep.tile([P, S], F32, name=f"dens{t}") for t in FIRST] + [
-            stage.tile([P, S], F32, name=f"dens{t}", offset=at) for t, at in zip(LAST, (DENS2_AT, DENS3_AT))
-        ]
-        e_all = keep.tile([P, S], F32, name="e_all")
-        e2 = keep.tile([P, PACK, V], F32, name="e2")
-        e1 = stage.tile([P, PACK, V], F32, name="e1", offset=NEAR_AT)
+        dens = [keep.tile([P, S], F32, name=f"dens{t}") for t in range(PACK)]
+        e_all = [keep.tile([P, S], F32, name=f"e_all{t}") for t in range(PACK)]
+        e2 = keep.tile([P, V], F32, name="e2")
+        e1 = keep.tile([P, PACK, V], F32, name="e1")
 
         def exp_at(out, t, offsets):
             nc.scalar.activation(out, dens[t][:].indirect(offsets), ACT.Exp, scale=-1.0)
 
+        def exp_all(t, part=slice(0, S)):
+            nc.scalar.activation(e_all[t][:, part], dens[t][:, part], ACT.Exp, scale=-1.0)
+
         for bank_no, part in zip(S_BANKS[0], SAMPLES):
             nc.scalar.activation(dens[0][:, part], project_s(0, bank_no, part)[:], ACT.Relu)
         s_bank = {t: project_s(t, S_BANKS[t][0]) for t in range(1, PACK)}
-        nc.scalar.activation(e_all[:, SAMPLES[0]], dens[0][:, SAMPLES[0]], ACT.Exp, scale=-1.0)
+        exp_all(0, SAMPLES[0])
         nc.scalar.activation(dens[1][:], s_bank[1][:], ACT.Relu)
-        nc.scalar.activation(e_all[:, SAMPLES[1]], dens[0][:, SAMPLES[1]], ACT.Exp, scale=-1.0)
-        for t in FIRST:
-            exp_at(e2[:, t, :], t, p2_sb[:])
+        exp_all(0, SAMPLES[1])
+        nc.scalar.activation(dens[2][:], s_bank[2][:], ACT.Relu)
+        exp_all(1)
+        nc.scalar.activation(dens[3][:], s_bank[3][:], ACT.Relu)
+        exp_all(2)
+        exp_at(e1[:, 0, :], 0, p1_sb[:])
+        exp_all(3)
+        exp_at(e2[:], 3, p2_sb[:])
+        for t in range(1, PACK):
+            exp_at(e1[:, t, :], t, p1_sb[:])
 
         for t in range(PACK):
             nc.vector.quantize_mx(
@@ -204,54 +209,43 @@ def tile_picked_nerfvol_none_po_kernel(
         deal(nc.gpsimd, w3w[:], w3w_raw, LINE // 4)
         deal(nc.gpsimd, w3s[:], w3s_raw[:], LINE)
 
-        base = keep.tile([P, PACK, V], F32, name="base", align_bytes=ALIGN)
+        near = keep.tile([P, PACK, V], F32, name="near", align_bytes=ALIGN)
         cut = keep.tile([P, PACK, V], F32, name="cut", align_bytes=ALIGN)
-        dim = keep.tile([P, S], F32, name="dim")
-        val = {t: keep.tile([P, S], F32, name=f"val{t}") for t in range(1, PACK)}
+        far = keep.tile([P, PACK, V], F32, name="far", align_bytes=ALIGN)
+        lit = keep.tile([P, PACK, V], F32, name="lit", align_bytes=ALIGN)
+        dim = [keep.tile([P, S], F32, name=f"dim{t}") for t in range(PACK)]
+
+        def weigh(t, bank_no, part=slice(0, S)):
+            bank = project_val(t, bank_no, part)
+            nc.vector.scalar_tensor_tensor(dim[t][:, part], e_all[t][:, part], 1.0, bank[:], ALU.subtract, ALU.mult)
+
+        def light(t):
+            nc.vector.tensor_tensor(lit[:, t, :], e_all[t][:].indirect(p2_sb[:]), bg_sb[:, t, :], ALU.mult)
+
+        def far_sum(t, rays=slice(0, V)):
+            nc.vector.tensor_tensor(
+                far[:, t, rays], dim[t][:].indirect(entries(p2_sb, rays)), lit[:, t, rays], ALU.subtract
+            )
+
+        def near_at(t, rays=slice(0, V)):
+            nc.scalar.activation(near[:, t, rays], dim[t][:].indirect(entries(p1_sb, rays)), ACT.Copy)
+
         for bank_no, part in zip(VAL_BANKS[0], SAMPLES):
-            bank = project_val(0, bank_no, part)
-            nc.vector.scalar_tensor_tensor(dim[:, part], e_all[:, part], 1.0, bank[:], ALU.subtract, ALU.mult)
-        nc.vector.tensor_copy(val[1][:], project_val(1, VAL_BANKS[1][0])[:])
-
-        for t in LAST:
-            nc.scalar.copy(val[t][:], project_val(t, VAL_BANKS[t][0])[:])
-            nc.scalar.activation(dens[t][:], s_bank[t][:], ACT.Relu)
-        for t in LAST:
-            exp_at(e2[:, t, :], t, p2_sb[:])
-        for t in range(PACK):
-            exp_at(e1[:, t, :], t, p1_sb[:])
-
-        e2_bg = keep.tile([P, V], F32, name="e2_bg")
-        far = keep.tile([P, V], F32, name="far")
-        a = {t: keep.tile([P, V], F32, name=f"a{t}") for t in val}
-        b = {t: keep.tile([P, V], F32, name=f"b{t}") for t in val}
-        g = keep.tile([P, PACK - 1, V], F32, name="g")
-
-        def far_diff(t):
-            nc.vector.tensor_tensor(a[t][:], val[t][:].indirect(p2_sb[:]), bg_sb[:, t, :], ALU.subtract)
-
-        def far_weigh(t):
-            nc.vector.scalar_tensor_tensor(b[t][:], e2[:, t, :], 1.0, a[t][:], ALU.subtract, ALU.mult)
-
-        def far_blend(t):
-            nc.vector.tensor_tensor(base[:, t, :], bg_sb[:, t, :], b[t][:], ALU.subtract)
-
-        def near_diff(t):
-            nc.vector.tensor_tensor(g[:, t - 1, :], val[t][:].indirect(p1_sb[:]), base[:, t, :], ALU.subtract)
-
-        nc.vector.tensor_scalar(base[:, 0, :], dim[:].indirect(p1_sb[:]), -1.0, 0.0, ALU.mult, ALU.add)
-        nc.vector.tensor_tensor(e2_bg[:], e2[:, 0, :], bg_sb[:, 0, :], ALU.mult)
-        far_diff(1)
-        nc.vector.tensor_tensor(far[:], dim[:].indirect(p2_sb[:]), e2_bg[:], ALU.subtract)
-        far_weigh(1)
-        far_diff(2)
-        far_blend(1)
-        far_diff(3)
-        near_diff(1)
-        for step in (far_weigh, far_blend, near_diff):
+            weigh(0, bank_no, part)
+        weigh(1, VAL_BANKS[1][0])
+        weigh(2, VAL_BANKS[2][0])
+        light(0)
+        weigh(3, VAL_BANKS[3][0])
+        far_sum(0)
+        light(1)
+        light(2)
+        far_sum(1)
+        nc.vector.tensor_tensor(lit[:, 3, :], e2[:], bg_sb[:, 3, :], ALU.mult)
+        for t in FIRST:
+            near_at(t)
+        for rays in RAYS:
             for t in LAST:
-                step(t)
-        nc.vector.tensor_tensor(cut[:, 0, :], e1[:, 0, :], far[:], ALU.mult)
+                near_at(t, rays)
 
         zw = keep.tile([P, V], U32, name="zw", align_bytes=ALIGN)
         zs = keep.tile([P, V], U8, name="zs", align_bytes=ALIGN)
@@ -268,15 +262,25 @@ def tile_picked_nerfvol_none_po_kernel(
                 in_=src[half][:].rearrange("p v t -> p (v t)"),
             )
 
-        for rays in RAYS:
-            nc.vector.scalar_tensor_tensor(
-                cut[:, 1:PACK, rays], e1[:, 1:PACK, rays], 1.0, g[:, :, rays], ALU.subtract, ALU.mult
-            )
-        for half, rays in enumerate(RAYS):
-            nc.vector.tensor_tensor(by_word(zb[half]), by_tile(base[:, :, rays]), by_tile(cut[:, :, rays]), ALU.subtract)
+        def pass_on(rays):
+            nc.vector.scalar_tensor_tensor(cut[:, :, rays], e1[:, :, rays], -1.0, far[:, :, rays], ALU.mult, ALU.mult)
+
+        def blend(half):
+            rays = RAYS[half]
+            nc.vector.tensor_tensor(by_word(zb[half]), by_tile(cut[:, :, rays]), by_tile(near[:, :, rays]), ALU.subtract)
+
+        far_sum(2, RAYS[0])
+        far_sum(3, RAYS[0])
+        far_sum(2, RAYS[1])
+        pass_on(RAYS[0])
+        far_sum(3, RAYS[1])
+        blend(0)
+        pass_on(RAYS[1])
+        quantise(zw, zs, zb, 0)
+        blend(1)
+        quantise(zw, zs, zb, 1)
         out_banks = []
         for half, rays in enumerate(RAYS):
-            quantise(zw, zs, zb, half)
             banks = [psum.tile([P, 2, V // 2], F32, name="out_bank", tag=f"bank{no}") for no in OUT_BANKS[half]]
             for t in range(PACK):
                 nc.tensor.matmul_mx(
@@ -291,7 +295,7 @@ def tile_picked_nerfvol_none_po_kernel(
             out_banks.append(banks)
 
         out_rows = out_0.rearrange("(p t) v -> p t v", t=PACK)
-        for half, (second_copy, queue) in enumerate(((nc.vector.tensor_copy, nc.sync), (nc.scalar.copy, nc.scalar))):
+        for half, (second_copy, queue) in enumerate(((nc.scalar.copy, nc.sync), (nc.vector.tensor_copy, nc.scalar))):
             nc.scalar.copy(of[half][:, 0:2, :], out_banks[half][0][:])
             second_copy(of[half][:, 2:4, :], out_banks[half][1][:])
             queue.dma_start(out=out_rows[:, :, RAYS[half]], in_=of[half][:])

@@ -39,8 +39,10 @@ X_WORDS_AT = FLOATS_AT + 4 * PACK * (H + V)
 W2B_LAST_AT = X_WORDS_AT + 4 * T + N
 W1_SCALES_AT = W2B_LAST_AT + 4 * H - ALIGN
 W2B_FIRST_AT = W1_SCALES_AT + H - ALIGN
-W3_SCALES_AT = W2B_LAST_AT + ALIGN - N
 W3_WORDS_AT = W2B_LAST_AT + ALIGN
+W3_SCALES_AT = W2B_FIRST_AT + 4 * H
+DENS2_AT = W3_SCALES_AT + N - ALIGN
+NEAR_EXP_AT = DENS2_AT + ALIGN
 
 
 def words_i32(ap):
@@ -56,7 +58,7 @@ def load_scales(queue, plane, scales, first, rows=range(PACK)):
 
 
 def deal(engine, dst, src, run, tiles=slice(0, PACK)):
-    engine.tensor_copy(
+    engine(
         out=dst.rearrange("p (t c i) -> p c t i", t=PACK, i=run)[:, :, tiles, :],
         in_=src.rearrange("p (c i t) -> p c t i", t=PACK, i=run)[:, :, tiles, :],
     )
@@ -91,7 +93,7 @@ def tile_picked_nerfvol_none_po_kernel(
         w1s_raw = stage.tile([P, H], U8, name="w1s_raw", offset=W1_SCALES_AT, align_bytes=ALIGN)
         zeros = stage.tile([P, H // 4], I32, name="zeros", offset=ZEROS_AT)
         w3s_raw = keep.tile([P, N], U8, name="w3s_raw")
-        nc.vector.memset(xs[:].bitcast(I32), 0)
+        nc.gpsimd.memset(xs[:].bitcast(I32), 0)
         nc.gpsimd.memset(zeros[:], 0)
         nc.vector.tensor_copy(w1s_raw[:].bitcast(I32), zeros[:])
         nc.vector.memset(w3s_raw[:].bitcast(I32), 0)
@@ -109,9 +111,8 @@ def tile_picked_nerfvol_none_po_kernel(
 
         nc.sync.dma_start(offs_sb[:], offs)
         load_x_words(0, T // 4)
-        load_x_words(T // 4, T // 2)
         load_scales(nc.sync, xs, x_scales, X_ROW)
-        load_x_words(T // 2, T)
+        load_x_words(T // 4, T)
         nc.sync.dma_start(out=w1w_raw.bitcast(I32), in_=words_i32(w1_words))
         load_scales(nc.sync, w1s_raw, w1_scales, W1_ROW)
         for half in range(2):
@@ -129,12 +130,12 @@ def tile_picked_nerfvol_none_po_kernel(
         xg_w = keep.tile([P, S], U32, name="xg_w", tag="xs", align_bytes=ALIGN)
         w1w = keep.tile([P, H], U32, name="w1w", align_bytes=ALIGN)
         w1s = keep.tile([P, H], U8, name="w1s", align_bytes=ALIGN)
-        deal(nc.gpsimd, w1w[:], w1w_raw, LINE // 4, slice(0, 1))
-        deal(nc.gpsimd, w1s[:], w1s_raw[:], LINE, slice(0, 1))
+        deal(nc.gpsimd.tensor_copy, w1w[:], w1w_raw, LINE // 4, slice(0, 1))
+        deal(nc.gpsimd.tensor_copy, w1s[:], w1s_raw[:], LINE, slice(0, 1))
         for part in SAMPLES:
             nc.vector.tensor_copy(xg_w[:, part], xw[:].indirect(entries(offs_sb, part)))
-        deal(nc.vector, w1w[:], w1w_raw, LINE // 4, slice(1, PACK))
-        deal(nc.vector, w1s[:], w1s_raw[:], LINE, slice(1, PACK))
+        deal(nc.vector.tensor_copy, w1w[:], w1w_raw, LINE // 4, slice(1, PACK))
+        deal(nc.vector.tensor_copy, w1s[:], w1s_raw[:], LINE, slice(1, PACK))
 
         w2b = [
             stage.tile([P, 2, P, PACK], BF16, name=f"w2b{pair}", offset=at, align_bytes=ALIGN)
@@ -172,13 +173,14 @@ def tile_picked_nerfvol_none_po_kernel(
         def project_val(t, bank_no, part=slice(0, S)):
             return project(w2w[t][:], w2s[t][:], bank_no, part)
 
-        dens = [keep.tile([P, S], F32, name=f"dens{t}") for t in range(PACK)]
+        dens = {t: keep.tile([P, S], F32, name=f"dens{t}") for t in (0, 1, 3)}
+        dens[2] = stage.tile([P, S], F32, name="dens2", offset=DENS2_AT)
         e_all = [keep.tile([P, S], F32, name=f"e_all{t}") for t in range(PACK)]
         e2 = keep.tile([P, V], F32, name="e2")
-        e1 = keep.tile([P, PACK, V], F32, name="e1")
+        e1 = stage.tile([P, PACK, V], F32, name="e1", offset=NEAR_EXP_AT)
 
         def exp_at(out, t, offsets):
-            nc.scalar.activation(out, dens[t][:].indirect(offsets), ACT.Exp, scale=-1.0)
+            nc.scalar.activation(out, e_all[t][:].indirect(offsets), ACT.Copy)
 
         def exp_all(t, part=slice(0, S)):
             nc.scalar.activation(e_all[t][:, part], dens[t][:, part], ACT.Exp, scale=-1.0)
@@ -189,12 +191,12 @@ def tile_picked_nerfvol_none_po_kernel(
         exp_all(0, SAMPLES[0])
         nc.scalar.activation(dens[1][:], s_bank[1][:], ACT.Relu)
         exp_all(0, SAMPLES[1])
-        nc.scalar.activation(dens[2][:], s_bank[2][:], ACT.Relu)
         exp_all(1)
+        nc.scalar.activation(dens[2][:], s_bank[2][:], ACT.Relu)
         nc.scalar.activation(dens[3][:], s_bank[3][:], ACT.Relu)
         exp_all(2)
-        exp_at(e1[:, 0, :], 0, p1_sb[:])
         exp_all(3)
+        exp_at(e1[:, 0, :], 0, p1_sb[:])
         exp_at(e2[:], 3, p2_sb[:])
         for t in range(1, PACK):
             exp_at(e1[:, t, :], t, p1_sb[:])
@@ -206,8 +208,8 @@ def tile_picked_nerfvol_none_po_kernel(
 
         w3w = stage.tile([P, N], U32, name="w3w", offset=W3_WORDS_AT, align_bytes=ALIGN)
         w3s = stage.tile([P, N], U8, name="w3s", offset=W3_SCALES_AT, align_bytes=ALIGN)
-        deal(nc.gpsimd, w3w[:], w3w_raw, LINE // 4)
-        deal(nc.gpsimd, w3s[:], w3s_raw[:], LINE)
+        deal(nc.gpsimd.tensor_copy, w3w[:], w3w_raw, LINE // 4)
+        deal(nc.gpsimd.tensor_copy, w3s[:], w3s_raw[:], LINE)
 
         near = keep.tile([P, PACK, V], F32, name="near", align_bytes=ALIGN)
         cut = keep.tile([P, PACK, V], F32, name="cut", align_bytes=ALIGN)
@@ -234,10 +236,10 @@ def tile_picked_nerfvol_none_po_kernel(
             weigh(0, bank_no, part)
         weigh(1, VAL_BANKS[1][0])
         weigh(2, VAL_BANKS[2][0])
-        light(0)
         weigh(3, VAL_BANKS[3][0])
-        far_sum(0)
+        light(0)
         light(1)
+        far_sum(0)
         light(2)
         far_sum(1)
         nc.vector.tensor_tensor(lit[:, 3, :], e2[:], bg_sb[:, 3, :], ALU.mult)
@@ -269,15 +271,14 @@ def tile_picked_nerfvol_none_po_kernel(
             rays = RAYS[half]
             nc.vector.tensor_tensor(by_word(zb[half]), by_tile(cut[:, :, rays]), by_tile(near[:, :, rays]), ALU.subtract)
 
-        far_sum(2, RAYS[0])
+        far_sum(2)
         far_sum(3, RAYS[0])
-        far_sum(2, RAYS[1])
-        pass_on(RAYS[0])
         far_sum(3, RAYS[1])
-        blend(0)
+        pass_on(RAYS[0])
         pass_on(RAYS[1])
-        quantise(zw, zs, zb, 0)
+        blend(0)
         blend(1)
+        quantise(zw, zs, zb, 0)
         quantise(zw, zs, zb, 1)
         out_banks = []
         for half, rays in enumerate(RAYS):
@@ -301,7 +302,7 @@ def tile_picked_nerfvol_none_po_kernel(
             queue.dma_start(out=out_rows[:, :, RAYS[half]], in_=of[half][:])
             nc.vector.tensor_copy(out=by_word(ob[half]), in_=by_tile(of[half][:]))
             quantise(ow, osc, ob, half)
-        nc.sync.dma_start(out=words_i32(out_1), in_=ow[:].bitcast(I32))
+            nc.sync.dma_start(out=words_i32(out_1)[:, RAYS[half]], in_=ow[:, RAYS[half]].bitcast(I32))
         for r in range(PACK):
             queue = nc.sync if r % 2 else nc.scalar
             queue.dma_start(out=out_2[0].bitcast(I32)[r:BLOCKS:PACK, :], in_=osc[:].bitcast(I32)[r:P:QUAD, :])

@@ -43,6 +43,10 @@ W3_WORDS_AT = W2B_LAST_AT + ALIGN
 W3_SCALES_AT = W2B_FIRST_AT + 4 * H
 DENS2_AT = W3_SCALES_AT + N - ALIGN
 NEAR_EXP_AT = DENS2_AT + ALIGN
+DENS1_AT = NEAR_EXP_AT + 4 * PACK * V
+LIT_LAST_AT = DENS1_AT + 4 * S
+DENS3_AT = LIT_LAST_AT + 4 * 2 * V - ALIGN
+FAR_AT = DENS3_AT + ALIGN
 
 
 def words_i32(ap):
@@ -151,8 +155,8 @@ def tile_picked_nerfvol_none_po_kernel(
 
         cast_w2(0)
         cast_w2(1)
-        w2w = [keep.tile([P, P], U32, name=f"w2w{t}", align_bytes=ALIGN) for t in range(PACK)]
-        w2s = [keep.tile([P, P], U8, name=f"w2s{t}", align_bytes=ALIGN) for t in range(PACK)]
+        w2w = keep.tile([P, H], U32, name="w2w", align_bytes=ALIGN)
+        w2s = keep.tile([P, H], U8, name="w2s", align_bytes=ALIGN)
 
         def project(words, scales, bank_no, part=slice(0, S)):
             bank = psum.tile([P, part.stop - part.start], F32, name="bank", tag=f"bank{bank_no}")
@@ -171,10 +175,11 @@ def tile_picked_nerfvol_none_po_kernel(
             return project(w1w[:, t * P : (t + 1) * P], w1s[W1_ROW:P, t * P : (t + 1) * P], bank_no, part)
 
         def project_val(t, bank_no, part=slice(0, S)):
-            return project(w2w[t][:], w2s[t][:], bank_no, part)
+            return project(w2w[:, t * P : (t + 1) * P], w2s[:, t * P : (t + 1) * P], bank_no, part)
 
-        dens = {t: keep.tile([P, S], F32, name=f"dens{t}") for t in (0, 1, 3)}
-        dens[2] = stage.tile([P, S], F32, name="dens2", offset=DENS2_AT)
+        dens = [keep.tile([P, S], F32, name="dens0")] + [
+            stage.tile([P, S], F32, name=f"dens{t}", offset=at) for t, at in ((1, DENS1_AT), (2, DENS2_AT), (3, DENS3_AT))
+        ]
         e_all = [keep.tile([P, S], F32, name=f"e_all{t}") for t in range(PACK)]
         e2 = keep.tile([P, V], F32, name="e2")
         e1 = stage.tile([P, PACK, V], F32, name="e1", offset=NEAR_EXP_AT)
@@ -201,9 +206,12 @@ def tile_picked_nerfvol_none_po_kernel(
         for t in range(1, PACK):
             exp_at(e1[:, t, :], t, p1_sb[:])
 
-        for t in range(PACK):
+        for pair, first, count in ((0, 0, 1), (0, 1, 1), (1, 0, 2)):
+            cols = slice((2 * pair + first) * P, (2 * pair + first + count) * P)
             nc.vector.quantize_mx(
-                out=w2w[t][:].bitcast(FP8X4), scales=w2s[t][:], in_=w2b[t // 2][:, t % 2].rearrange("p m j -> p (m j)")
+                out=w2w[:, cols].bitcast(FP8X4),
+                scales=w2s[:, cols],
+                in_=w2b[pair][:, first : first + count].rearrange("p u m j -> p (u m j)"),
             )
 
         w3w = stage.tile([P, N], U32, name="w3w", offset=W3_WORDS_AT, align_bytes=ALIGN)
@@ -213,8 +221,11 @@ def tile_picked_nerfvol_none_po_kernel(
 
         near = keep.tile([P, PACK, V], F32, name="near", align_bytes=ALIGN)
         cut = keep.tile([P, PACK, V], F32, name="cut", align_bytes=ALIGN)
-        far = keep.tile([P, PACK, V], F32, name="far", align_bytes=ALIGN)
-        lit = keep.tile([P, PACK, V], F32, name="lit", align_bytes=ALIGN)
+        far = stage.tile([P, PACK, V], F32, name="far", offset=FAR_AT, align_bytes=ALIGN)
+        lit_pairs = [
+            stage.tile([P, 2, V], F32, name=f"lit{pair}", offset=at) for pair, at in enumerate((DENS1_AT, LIT_LAST_AT))
+        ]
+        lit = [lit_pairs[t // 2][:, t % 2, :] for t in range(PACK)]
         dim = [keep.tile([P, S], F32, name=f"dim{t}") for t in range(PACK)]
 
         def weigh(t, bank_no, part=slice(0, S)):
@@ -222,11 +233,11 @@ def tile_picked_nerfvol_none_po_kernel(
             nc.vector.scalar_tensor_tensor(dim[t][:, part], e_all[t][:, part], 1.0, bank[:], ALU.subtract, ALU.mult)
 
         def light(t):
-            nc.vector.tensor_tensor(lit[:, t, :], e_all[t][:].indirect(p2_sb[:]), bg_sb[:, t, :], ALU.mult)
+            nc.vector.tensor_tensor(lit[t], e_all[t][:].indirect(p2_sb[:]), bg_sb[:, t, :], ALU.mult)
 
         def far_sum(t, rays=slice(0, V)):
             nc.vector.tensor_tensor(
-                far[:, t, rays], dim[t][:].indirect(entries(p2_sb, rays)), lit[:, t, rays], ALU.subtract
+                far[:, t, rays], dim[t][:].indirect(entries(p2_sb, rays)), lit[t][:, rays], ALU.subtract
             )
 
         def near_at(t, rays=slice(0, V)):
@@ -235,14 +246,14 @@ def tile_picked_nerfvol_none_po_kernel(
         for bank_no, part in zip(VAL_BANKS[0], SAMPLES):
             weigh(0, bank_no, part)
         weigh(1, VAL_BANKS[1][0])
-        weigh(2, VAL_BANKS[2][0])
-        weigh(3, VAL_BANKS[3][0])
         light(0)
         light(1)
+        weigh(2, VAL_BANKS[2][0])
+        weigh(3, VAL_BANKS[3][0])
         far_sum(0)
         light(2)
         far_sum(1)
-        nc.vector.tensor_tensor(lit[:, 3, :], e2[:], bg_sb[:, 3, :], ALU.mult)
+        nc.vector.tensor_tensor(lit[3], e2[:], bg_sb[:, 3, :], ALU.mult)
         for t in FIRST:
             near_at(t)
         for rays in RAYS:

@@ -32,13 +32,9 @@ S_BANKS = ((0, 1), (2,), (3,), (4,))
 VAL_BANKS = ((5, 6), (7,), (0,), (1,))
 OUT_BANKS = ((2, 5), (6, 7))
 
-WORDS_AT = 0
-FLOATS_AT = WORDS_AT + 4 * (N + H)
-ZEROS_AT = FLOATS_AT - H // 2
-X_WORDS_AT = FLOATS_AT + 4 * PACK * (H + V)
-W2B_LAST_AT = X_WORDS_AT + 4 * T + N
-W1_SCALES_AT = W2B_LAST_AT + 4 * H - ALIGN
-W2B_FIRST_AT = W1_SCALES_AT + H - ALIGN
+W2B_LAST_AT = 0
+W1_WORDS_AT = W2B_LAST_AT + 4 * H - ALIGN
+W2B_FIRST_AT = W1_WORDS_AT + 4 * H - ALIGN
 W3_WORDS_AT = W2B_LAST_AT + ALIGN
 W3_SCALES_AT = W2B_FIRST_AT + 4 * H
 DENS2_AT = W3_SCALES_AT + N - ALIGN
@@ -92,19 +88,17 @@ def tile_picked_nerfvol_none_po_kernel(
         offs_sb = keep.tile([P, S // GROUP], U16, name="offs_sb")
         p1_sb = keep.tile([P, V // GROUP], U16, name="p1_sb")
         p2_sb = keep.tile([P, V // GROUP], U16, name="p2_sb")
-        xw = stage.tile([P, T], U32, name="xw", offset=X_WORDS_AT)
+        xw = keep.tile([P, T], U32, name="xw")
         xs = keep.tile([P, T], U8, name="xs", tag="xs", align_bytes=ALIGN)
-        w1s_raw = stage.tile([P, H], U8, name="w1s_raw", offset=W1_SCALES_AT, align_bytes=ALIGN)
-        zeros = stage.tile([P, H // 4], I32, name="zeros", offset=ZEROS_AT)
+        w1s_raw = keep.tile([P, H], U8, name="w1s_raw")
         w3s_raw = keep.tile([P, N], U8, name="w3s_raw")
         nc.gpsimd.memset(xs[:].bitcast(I32), 0)
-        nc.gpsimd.memset(zeros[:], 0)
-        nc.vector.tensor_copy(w1s_raw[:].bitcast(I32), zeros[:])
+        nc.vector.memset(w1s_raw[:].bitcast(I32), 0)
         nc.vector.memset(w3s_raw[:].bitcast(I32), 0)
 
-        words_raw = stage.tile([P, N + H], U32, name="words_raw", offset=WORDS_AT)
-        w3w_raw, w1w_raw = words_raw[:, 0:N], words_raw[:, N : N + H]
-        floats = stage.tile([P, PACK * (H + V)], F32, name="floats", offset=FLOATS_AT)
+        w3w_raw = keep.tile([P, N], U32, name="w3w_raw")[:]
+        w1w_raw = stage.tile([P, H], U32, name="w1w_raw", offset=W1_WORDS_AT, align_bytes=ALIGN)[:]
+        floats = keep.tile([P, PACK * (H + V)], F32, name="floats")
         w2_raw = floats[:, 0 : PACK * H].rearrange("p (half j c) -> p half j c", half=2, j=PACK)
         bg_sb = floats[:, PACK * H : PACK * (H + V)].rearrange("p (t v) -> p t v", t=PACK)
         w2_rows = w2.rearrange("(p j) (half c) -> p half j c", j=PACK, half=2)
@@ -117,8 +111,8 @@ def tile_picked_nerfvol_none_po_kernel(
         load_x_words(0, T // 4)
         load_scales(nc.sync, xs, x_scales, X_ROW)
         load_x_words(T // 4, T)
-        nc.sync.dma_start(out=w1w_raw.bitcast(I32), in_=words_i32(w1_words))
         load_scales(nc.sync, w1s_raw, w1_scales, W1_ROW)
+        nc.sync.dma_start(out=w1w_raw.bitcast(I32), in_=words_i32(w1_words))
         for half in range(2):
             nc.sync.dma_start(out=w2_raw[:, half], in_=w2_rows[:, half])
         nc.sync.dma_start(p2_sb[:], p2)
@@ -134,12 +128,13 @@ def tile_picked_nerfvol_none_po_kernel(
         xg_w = keep.tile([P, S], U32, name="xg_w", tag="xs", align_bytes=ALIGN)
         w1w = keep.tile([P, H], U32, name="w1w", align_bytes=ALIGN)
         w1s = keep.tile([P, H], U8, name="w1s", align_bytes=ALIGN)
-        deal(nc.gpsimd.tensor_copy, w1w[:], w1w_raw, LINE // 4, slice(0, 1))
-        deal(nc.gpsimd.tensor_copy, w1s[:], w1s_raw[:], LINE, slice(0, 1))
+        deal(nc.gpsimd.tensor_copy, w1s[:], w1s_raw[:], LINE, slice(0, 2))
+        for t in FIRST:
+            deal(nc.gpsimd.tensor_copy, w1w[:], w1w_raw, LINE // 4, slice(t, t + 1))
         for part in SAMPLES:
             nc.vector.tensor_copy(xg_w[:, part], xw[:].indirect(entries(offs_sb, part)))
-        deal(nc.vector.tensor_copy, w1w[:], w1w_raw, LINE // 4, slice(1, PACK))
-        deal(nc.vector.tensor_copy, w1s[:], w1s_raw[:], LINE, slice(1, PACK))
+        deal(nc.vector.tensor_copy, w1s[:], w1s_raw[:], LINE, slice(2, PACK))
+        deal(nc.vector.tensor_copy, w1w[:], w1w_raw, LINE // 4, slice(2, PACK))
 
         w2b = [
             stage.tile([P, 2, P, PACK], BF16, name=f"w2b{pair}", offset=at, align_bytes=ALIGN)

@@ -22,7 +22,6 @@ BLOCKS = 16
 GROUP = 16
 LINE = 16
 ALIGN = 64
-STEP = 32
 X_ROW, W1_ROW, W3_ROW = 4, 8, 12
 FIRST, LAST = (0, 1), (2, 3)
 SAMPLES = (slice(0, S // 2), slice(S // 2, S))
@@ -33,16 +32,19 @@ VAL_BANKS = ((5, 6), (7,), (0,), (1,))
 OUT_BANKS = ((2, 5), (6, 7))
 
 W2B_LAST_AT = 0
-W1_WORDS_AT = W2B_LAST_AT + 4 * H - ALIGN
-W2B_FIRST_AT = W1_WORDS_AT + 4 * H - ALIGN
+W2B_FIRST_AT = W2B_LAST_AT + 4 * H
 W3_WORDS_AT = W2B_LAST_AT + ALIGN
 W3_SCALES_AT = W2B_FIRST_AT + 4 * H
 DENS2_AT = W3_SCALES_AT + N - ALIGN
-NEAR_EXP_AT = DENS2_AT + ALIGN
-DENS1_AT = NEAR_EXP_AT + 4 * PACK * V
+E1_AT = DENS2_AT + ALIGN
+DENS1_AT = E1_AT + 4 * PACK * V
+LIT_FIRST_AT = DENS1_AT
 LIT_LAST_AT = DENS1_AT + 4 * S
 DENS3_AT = LIT_LAST_AT + 4 * 2 * V - ALIGN
 FAR_AT = DENS3_AT + ALIGN
+W2_FIRST_AT = FAR_AT + 4 * PACK * V
+W1_WORDS_LAST_AT = W2_FIRST_AT
+W1_SCALES_LAST_AT = W1_WORDS_LAST_AT + 4 * 2 * P
 
 
 def words_i32(ap):
@@ -57,9 +59,9 @@ def load_scales(queue, plane, scales, first, rows=range(PACK)):
         )
 
 
-def deal(engine, dst, src, run, tiles=slice(0, PACK)):
-    engine(
-        out=dst.rearrange("p (t c i) -> p c t i", t=PACK, i=run)[:, :, tiles, :],
+def deal(move, dst, src, run, tiles=slice(0, PACK)):
+    move(
+        out=dst.rearrange("p (t c i) -> p c t i", t=tiles.stop - tiles.start, i=run),
         in_=src.rearrange("p (c i t) -> p c t i", t=PACK, i=run)[:, :, tiles, :],
     )
 
@@ -97,10 +99,12 @@ def tile_picked_nerfvol_none_po_kernel(
         nc.vector.memset(w3s_raw[:].bitcast(I32), 0)
 
         w3w_raw = keep.tile([P, N], U32, name="w3w_raw")[:]
-        w1w_raw = stage.tile([P, H], U32, name="w1w_raw", offset=W1_WORDS_AT, align_bytes=ALIGN)[:]
-        floats = keep.tile([P, PACK * (H + V)], F32, name="floats")
-        w2_raw = floats[:, 0 : PACK * H].rearrange("p (half j c) -> p half j c", half=2, j=PACK)
-        bg_sb = floats[:, PACK * H : PACK * (H + V)].rearrange("p (t v) -> p t v", t=PACK)
+        w1w_raw = keep.tile([P, H], U32, name="w1w_raw")[:]
+        w2_raw = [
+            stage.tile([P, PACK, H // 2], F32, name="w2_first", offset=W2_FIRST_AT, align_bytes=ALIGN),
+            keep.tile([P, PACK, H // 2], F32, name="w2_last"),
+        ]
+        bg_sb = keep.tile([P, PACK, V], F32, name="bg_sb")
         w2_rows = w2.rearrange("(p j) (half c) -> p half j c", j=PACK, half=2)
         bg_rows = bg.rearrange("(p t) v -> p t v", t=PACK)
 
@@ -114,7 +118,7 @@ def tile_picked_nerfvol_none_po_kernel(
         load_scales(nc.sync, w1s_raw, w1_scales, W1_ROW)
         nc.sync.dma_start(out=w1w_raw.bitcast(I32), in_=words_i32(w1_words))
         for half in range(2):
-            nc.sync.dma_start(out=w2_raw[:, half], in_=w2_rows[:, half])
+            nc.sync.dma_start(out=w2_raw[half][:], in_=w2_rows[:, half])
         nc.sync.dma_start(p2_sb[:], p2)
         nc.sync.dma_start(p1_sb[:], p1)
         nc.sync.dma_start(out=w3w_raw.bitcast(I32), in_=words_i32(w3_words))
@@ -126,15 +130,19 @@ def tile_picked_nerfvol_none_po_kernel(
         xg_s = keep.tile([P, S], U8, name="xg_s", align_bytes=ALIGN)
         nc.vector.tensor_copy(xg_s[:], xs[:].indirect(offs_sb[:]))
         xg_w = keep.tile([P, S], U32, name="xg_w", tag="xs", align_bytes=ALIGN)
-        w1w = keep.tile([P, H], U32, name="w1w", align_bytes=ALIGN)
-        w1s = keep.tile([P, H], U8, name="w1s", align_bytes=ALIGN)
-        deal(nc.gpsimd.tensor_copy, w1s[:], w1s_raw[:], LINE, slice(0, 2))
+        w1w = [
+            keep.tile([P, 2 * P], U32, name="w1w_first", align_bytes=ALIGN),
+            stage.tile([P, 2 * P], U32, name="w1w_last", offset=W1_WORDS_LAST_AT, align_bytes=ALIGN),
+        ]
+        w1s = [
+            keep.tile([P, 2 * P], U8, name="w1s_first", align_bytes=ALIGN),
+            stage.tile([P, 2 * P], U8, name="w1s_last", offset=W1_SCALES_LAST_AT, align_bytes=ALIGN),
+        ]
+        deal(nc.gpsimd.tensor_copy, w1s[0][:], w1s_raw[:], LINE, slice(0, 2))
         for t in FIRST:
-            deal(nc.gpsimd.tensor_copy, w1w[:], w1w_raw, LINE // 4, slice(t, t + 1))
+            deal(nc.gpsimd.tensor_copy, w1w[0][:, t * P : (t + 1) * P], w1w_raw, LINE // 4, slice(t, t + 1))
         for part in SAMPLES:
             nc.vector.tensor_copy(xg_w[:, part], xw[:].indirect(entries(offs_sb, part)))
-        deal(nc.vector.tensor_copy, w1s[:], w1s_raw[:], LINE, slice(2, PACK))
-        deal(nc.vector.tensor_copy, w1w[:], w1w_raw, LINE // 4, slice(2, PACK))
 
         w2b = [
             stage.tile([P, 2, P, PACK], BF16, name=f"w2b{pair}", offset=at, align_bytes=ALIGN)
@@ -145,10 +153,12 @@ def tile_picked_nerfvol_none_po_kernel(
             for pair in range(2):
                 nc.vector.tensor_copy(
                     out=w2b[pair][:, :, half * P // 2 : (half + 1) * P // 2, :].rearrange("p u m j -> p m j u"),
-                    in_=w2_raw[:, half].rearrange("p j (m t) -> p m j t", t=PACK)[:, :, :, 2 * pair : 2 * pair + 2],
+                    in_=w2_raw[half][:].rearrange("p j (m t) -> p m j t", t=PACK)[:, :, :, 2 * pair : 2 * pair + 2],
                 )
 
         cast_w2(0)
+        deal(nc.vector.tensor_copy, w1s[1][:], w1s_raw[:], LINE, slice(2, PACK))
+        deal(nc.vector.tensor_copy, w1w[1][:], w1w_raw, LINE // 4, slice(2, PACK))
         cast_w2(1)
         w2w = keep.tile([P, H], U32, name="w2w", align_bytes=ALIGN)
         w2s = keep.tile([P, H], U8, name="w2s", align_bytes=ALIGN)
@@ -167,19 +177,21 @@ def tile_picked_nerfvol_none_po_kernel(
             return bank
 
         def project_s(t, bank_no, part=slice(0, S)):
-            return project(w1w[:, t * P : (t + 1) * P], w1s[W1_ROW:P, t * P : (t + 1) * P], bank_no, part)
+            cols = slice(t % 2 * P, (t % 2 + 1) * P)
+            return project(w1w[t // 2][:, cols], w1s[t // 2][W1_ROW:P, cols], bank_no, part)
 
         def project_val(t, bank_no, part=slice(0, S)):
             return project(w2w[:, t * P : (t + 1) * P], w2s[:, t * P : (t + 1) * P], bank_no, part)
 
         dens = [keep.tile([P, S], F32, name="dens0")] + [
-            stage.tile([P, S], F32, name=f"dens{t}", offset=at) for t, at in ((1, DENS1_AT), (2, DENS2_AT), (3, DENS3_AT))
+            stage.tile([P, S], F32, name=f"dens{t}", offset=at)
+            for t, at in enumerate((DENS1_AT, DENS2_AT, DENS3_AT), start=1)
         ]
         e_all = [keep.tile([P, S], F32, name=f"e_all{t}") for t in range(PACK)]
         e2 = keep.tile([P, V], F32, name="e2")
-        e1 = stage.tile([P, PACK, V], F32, name="e1", offset=NEAR_EXP_AT)
+        e1 = stage.tile([P, PACK, V], F32, name="e1", offset=E1_AT)
 
-        def exp_at(out, t, offsets):
+        def e_at(out, t, offsets):
             nc.scalar.activation(out, e_all[t][:].indirect(offsets), ACT.Copy)
 
         def exp_all(t, part=slice(0, S)):
@@ -192,14 +204,14 @@ def tile_picked_nerfvol_none_po_kernel(
         nc.scalar.activation(dens[1][:], s_bank[1][:], ACT.Relu)
         exp_all(0, SAMPLES[1])
         exp_all(1)
-        nc.scalar.activation(dens[2][:], s_bank[2][:], ACT.Relu)
-        nc.scalar.activation(dens[3][:], s_bank[3][:], ACT.Relu)
-        exp_all(2)
-        exp_all(3)
-        exp_at(e1[:, 0, :], 0, p1_sb[:])
-        exp_at(e2[:], 3, p2_sb[:])
+        for t in LAST:
+            nc.scalar.activation(dens[t][:], s_bank[t][:], ACT.Relu)
+        for t in LAST:
+            exp_all(t)
+        e_at(e1[:, 0, :], 0, p1_sb[:])
+        e_at(e2[:], 3, p2_sb[:])
         for t in range(1, PACK):
-            exp_at(e1[:, t, :], t, p1_sb[:])
+            e_at(e1[:, t, :], t, p1_sb[:])
 
         for pair, first, count in ((0, 0, 1), (0, 1, 1), (1, 0, 2)):
             cols = slice((2 * pair + first) * P, (2 * pair + first + count) * P)
@@ -218,7 +230,8 @@ def tile_picked_nerfvol_none_po_kernel(
         cut = keep.tile([P, PACK, V], F32, name="cut", align_bytes=ALIGN)
         far = stage.tile([P, PACK, V], F32, name="far", offset=FAR_AT, align_bytes=ALIGN)
         lit_pairs = [
-            stage.tile([P, 2, V], F32, name=f"lit{pair}", offset=at) for pair, at in enumerate((DENS1_AT, LIT_LAST_AT))
+            stage.tile([P, 2, V], F32, name=f"lit{pair}", offset=at)
+            for pair, at in enumerate((LIT_FIRST_AT, LIT_LAST_AT))
         ]
         lit = [lit_pairs[t // 2][:, t % 2, :] for t in range(PACK)]
         dim = [keep.tile([P, S], F32, name=f"dim{t}") for t in range(PACK)]
@@ -241,10 +254,10 @@ def tile_picked_nerfvol_none_po_kernel(
         for bank_no, part in zip(VAL_BANKS[0], SAMPLES):
             weigh(0, bank_no, part)
         weigh(1, VAL_BANKS[1][0])
-        light(0)
-        light(1)
-        weigh(2, VAL_BANKS[2][0])
-        weigh(3, VAL_BANKS[3][0])
+        for t in FIRST:
+            light(t)
+        for t in LAST:
+            weigh(t, VAL_BANKS[t][0])
         far_sum(0)
         light(2)
         far_sum(1)
@@ -278,14 +291,14 @@ def tile_picked_nerfvol_none_po_kernel(
             nc.vector.tensor_tensor(by_word(zb[half]), by_tile(cut[:, :, rays]), by_tile(near[:, :, rays]), ALU.subtract)
 
         far_sum(2)
-        far_sum(3, RAYS[0])
-        far_sum(3, RAYS[1])
-        pass_on(RAYS[0])
-        pass_on(RAYS[1])
-        blend(0)
-        blend(1)
-        quantise(zw, zs, zb, 0)
-        quantise(zw, zs, zb, 1)
+        for rays in RAYS:
+            far_sum(3, rays)
+        for rays in RAYS:
+            pass_on(rays)
+        for half in range(2):
+            blend(half)
+        for half in range(2):
+            quantise(zw, zs, zb, half)
         out_banks = []
         for half, rays in enumerate(RAYS):
             banks = [psum.tile([P, 2, V // 2], F32, name="out_bank", tag=f"bank{no}") for no in OUT_BANKS[half]]
@@ -302,7 +315,7 @@ def tile_picked_nerfvol_none_po_kernel(
             out_banks.append(banks)
 
         out_rows = out_0.rearrange("(p t) v -> p t v", t=PACK)
-        for half, (second_copy, queue) in enumerate(((nc.scalar.copy, nc.sync), (nc.vector.tensor_copy, nc.scalar))):
+        for half, (second_copy, queue) in enumerate(((nc.vector.tensor_copy, nc.sync), (nc.scalar.copy, nc.scalar))):
             nc.scalar.copy(of[half][:, 0:2, :], out_banks[half][0][:])
             second_copy(of[half][:, 2:4, :], out_banks[half][1][:])
             queue.dma_start(out=out_rows[:, :, RAYS[half]], in_=of[half][:])

@@ -23,28 +23,28 @@ GROUP = 16
 LINE = 16
 ALIGN = 64
 X_ROW, W1_ROW, W3_ROW = 4, 8, 12
-FIRST, LAST = (0, 1), (2, 3)
+FIRST, LAST = slice(0, 2), slice(2, 4)
 SAMPLES = (slice(0, S // 2), slice(S // 2, S))
 RAYS = (slice(0, V // 2), slice(V // 2, V))
 
 S_BANKS = ((0, 1), (2,), (3,), (4,))
 VAL_BANKS = ((5, 6), (7,), (0,), (1,))
-OUT_BANKS = ((2, 5), (6, 7))
+OUT_BANKS = ((2, 3), (4, 5))
 
-W2B_LAST_AT = 0
-W2B_FIRST_AT = W2B_LAST_AT + 4 * H
-W3_WORDS_AT = W2B_LAST_AT + ALIGN
+NEAR_AT = 0
+VEIL3_AT = NEAR_AT
+W2B_LAST_AT = NEAR_AT + 4 * PACK * V
+W3_WORDS_AT = W2B_LAST_AT
+W2B_FIRST_AT = W3_WORDS_AT + 4 * H
 W3_SCALES_AT = W2B_FIRST_AT + 4 * H
-DENS2_AT = W3_SCALES_AT + N - ALIGN
-E1_AT = DENS2_AT + ALIGN
-DENS1_AT = E1_AT + 4 * PACK * V
-LIT_FIRST_AT = DENS1_AT
-LIT_LAST_AT = DENS1_AT + 4 * S
-DENS3_AT = LIT_LAST_AT + 4 * 2 * V - ALIGN
-FAR_AT = DENS3_AT + ALIGN
-W2_FIRST_AT = FAR_AT + 4 * PACK * V
-W1_WORDS_LAST_AT = W2_FIRST_AT
-W1_SCALES_LAST_AT = W1_WORDS_LAST_AT + 4 * 2 * P
+VEIL0_AT = W3_SCALES_AT
+VEIL2_AT = VEIL0_AT + 4 * S
+LIT_AT = VEIL2_AT
+E_FAR_AT = LIT_AT + 4 * PACK * V
+W1W_LAST_AT = E_FAR_AT + 4 * PACK * V - ALIGN
+E_NEAR_AT = W1W_LAST_AT + ALIGN
+W2_LAST_AT = E_NEAR_AT + 4 * PACK * V
+VEIL1_AT = W2_LAST_AT
 
 
 def words_i32(ap):
@@ -101,8 +101,8 @@ def tile_picked_nerfvol_none_po_kernel(
         w3w_raw = keep.tile([P, N], U32, name="w3w_raw")[:]
         w1w_raw = keep.tile([P, H], U32, name="w1w_raw")[:]
         w2_raw = [
-            stage.tile([P, PACK, H // 2], F32, name="w2_first", offset=W2_FIRST_AT, align_bytes=ALIGN),
-            keep.tile([P, PACK, H // 2], F32, name="w2_last"),
+            keep.tile([P, PACK, H // 2], F32, name="w2_first"),
+            stage.tile([P, PACK, H // 2], F32, name="w2_last", offset=W2_LAST_AT, align_bytes=ALIGN),
         ]
         bg_sb = keep.tile([P, PACK, V], F32, name="bg_sb")
         w2_rows = w2.rearrange("(p j) (half c) -> p half j c", j=PACK, half=2)
@@ -122,8 +122,7 @@ def tile_picked_nerfvol_none_po_kernel(
         nc.sync.dma_start(p2_sb[:], p2)
         nc.sync.dma_start(p1_sb[:], p1)
         nc.sync.dma_start(out=w3w_raw.bitcast(I32), in_=words_i32(w3_words))
-        for pair in range(2):
-            nc.sync.dma_start(out=bg_sb[:, 2 * pair : 2 * pair + 2, :], in_=bg_rows[:, 2 * pair : 2 * pair + 2, :])
+        nc.sync.dma_start(out=bg_sb[:], in_=bg_rows)
         load_scales(nc.gpsimd, w3s_raw, w3_scales, W3_ROW, range(0, 2))
         load_scales(nc.sync, w3s_raw, w3_scales, W3_ROW, range(2, PACK))
 
@@ -131,37 +130,17 @@ def tile_picked_nerfvol_none_po_kernel(
         nc.vector.tensor_copy(xg_s[:], xs[:].indirect(offs_sb[:]))
         xg_w = keep.tile([P, S], U32, name="xg_w", tag="xs", align_bytes=ALIGN)
         w1w = [
-            keep.tile([P, 2 * P], U32, name="w1w_first", align_bytes=ALIGN),
-            stage.tile([P, 2 * P], U32, name="w1w_last", offset=W1_WORDS_LAST_AT, align_bytes=ALIGN),
+            keep.tile([P, 2 * P], U32, name="w1w0", align_bytes=ALIGN),
+            stage.tile([P, 2 * P], U32, name="w1w1", offset=W1W_LAST_AT, align_bytes=ALIGN),
         ]
-        w1s = [
-            keep.tile([P, 2 * P], U8, name="w1s_first", align_bytes=ALIGN),
-            stage.tile([P, 2 * P], U8, name="w1s_last", offset=W1_SCALES_LAST_AT, align_bytes=ALIGN),
-        ]
-        deal(nc.gpsimd.tensor_copy, w1s[0][:], w1s_raw[:], LINE, slice(0, 2))
-        for t in FIRST:
+        w1s = [keep.tile([P, 2 * P], U8, name=f"w1s{pair}", align_bytes=ALIGN) for pair in range(2)]
+        deal(nc.gpsimd.tensor_copy, w1s[0][:], w1s_raw[:], LINE, FIRST)
+        for t in range(2):
             deal(nc.gpsimd.tensor_copy, w1w[0][:, t * P : (t + 1) * P], w1w_raw, LINE // 4, slice(t, t + 1))
         for part in SAMPLES:
             nc.vector.tensor_copy(xg_w[:, part], xw[:].indirect(entries(offs_sb, part)))
-
-        w2b = [
-            stage.tile([P, 2, P, PACK], BF16, name=f"w2b{pair}", offset=at, align_bytes=ALIGN)
-            for pair, at in enumerate((W2B_FIRST_AT, W2B_LAST_AT))
-        ]
-
-        def cast_w2(half):
-            for pair in range(2):
-                nc.vector.tensor_copy(
-                    out=w2b[pair][:, :, half * P // 2 : (half + 1) * P // 2, :].rearrange("p u m j -> p m j u"),
-                    in_=w2_raw[half][:].rearrange("p j (m t) -> p m j t", t=PACK)[:, :, :, 2 * pair : 2 * pair + 2],
-                )
-
-        cast_w2(0)
-        deal(nc.vector.tensor_copy, w1s[1][:], w1s_raw[:], LINE, slice(2, PACK))
-        deal(nc.vector.tensor_copy, w1w[1][:], w1w_raw, LINE // 4, slice(2, PACK))
-        cast_w2(1)
-        w2w = keep.tile([P, H], U32, name="w2w", align_bytes=ALIGN)
-        w2s = keep.tile([P, H], U8, name="w2s", align_bytes=ALIGN)
+        deal(nc.vector.tensor_copy, w1s[1][:], w1s_raw[:], LINE, LAST)
+        deal(nc.vector.tensor_copy, w1w[1][:], w1w_raw, LINE // 4, LAST)
 
         def project(words, scales, bank_no, part=slice(0, S)):
             bank = psum.tile([P, part.stop - part.start], F32, name="bank", tag=f"bank{bank_no}")
@@ -176,44 +155,52 @@ def tile_picked_nerfvol_none_po_kernel(
             )
             return bank
 
-        def project_s(t, bank_no, part=slice(0, S)):
+        raw = [keep.tile([P, S], F32, name=f"raw{t}") for t in range(PACK)]
+
+        def expose(t, bank_no, part=slice(0, S)):
             cols = slice(t % 2 * P, (t % 2 + 1) * P)
-            return project(w1w[t // 2][:, cols], w1s[t // 2][W1_ROW:P, cols], bank_no, part)
-
-        def project_val(t, bank_no, part=slice(0, S)):
-            return project(w2w[:, t * P : (t + 1) * P], w2s[:, t * P : (t + 1) * P], bank_no, part)
-
-        dens = [keep.tile([P, S], F32, name="dens0")] + [
-            stage.tile([P, S], F32, name=f"dens{t}", offset=at)
-            for t, at in enumerate((DENS1_AT, DENS2_AT, DENS3_AT), start=1)
-        ]
-        e_all = [keep.tile([P, S], F32, name=f"e_all{t}") for t in range(PACK)]
-        e2 = keep.tile([P, V], F32, name="e2")
-        e1 = stage.tile([P, PACK, V], F32, name="e1", offset=E1_AT)
-
-        def e_at(out, t, offsets):
-            nc.scalar.activation(out, e_all[t][:].indirect(offsets), ACT.Copy)
-
-        def exp_all(t, part=slice(0, S)):
-            nc.scalar.activation(e_all[t][:, part], dens[t][:, part], ACT.Exp, scale=-1.0)
+            bank = project(w1w[t // 2][:, cols], w1s[t // 2][W1_ROW:P, cols], bank_no, part)
+            nc.scalar.activation(raw[t][:, part], bank[:], ACT.Exp, scale=-1.0)
 
         for bank_no, part in zip(S_BANKS[0], SAMPLES):
-            nc.scalar.activation(dens[0][:, part], project_s(0, bank_no, part)[:], ACT.Relu)
-        s_bank = {t: project_s(t, S_BANKS[t][0]) for t in range(1, PACK)}
-        exp_all(0, SAMPLES[0])
-        nc.scalar.activation(dens[1][:], s_bank[1][:], ACT.Relu)
-        exp_all(0, SAMPLES[1])
-        exp_all(1)
-        for t in LAST:
-            nc.scalar.activation(dens[t][:], s_bank[t][:], ACT.Relu)
-        for t in LAST:
-            exp_all(t)
-        e_at(e1[:, 0, :], 0, p1_sb[:])
-        e_at(e2[:], 3, p2_sb[:])
+            expose(0, bank_no, part)
         for t in range(1, PACK):
-            e_at(e1[:, t, :], t, p1_sb[:])
+            expose(t, S_BANKS[t][0])
 
-        for pair, first, count in ((0, 0, 1), (0, 1, 1), (1, 0, 2)):
+        def fetch(out, table, offsets):
+            nc.scalar.activation(out, table[:].indirect(offsets), ACT.Copy)
+
+        e_near = stage.tile([P, PACK, V], F32, name="e_near", offset=E_NEAR_AT, align_bytes=ALIGN)
+        e_far = stage.tile([P, PACK, V], F32, name="e_far", offset=E_FAR_AT, align_bytes=ALIGN)
+        for t in range(PACK):
+            fetch(e_far[:, t, :], raw[t], p2_sb[:])
+        for t in range(PACK):
+            fetch(e_near[:, t, :], raw[t], p1_sb[:])
+
+        w2b = [
+            stage.tile([P, 2, P, PACK], BF16, name=f"w2b{pair}", offset=at, align_bytes=ALIGN)
+            for pair, at in enumerate((W2B_FIRST_AT, W2B_LAST_AT))
+        ]
+        veil = [
+            stage.tile([P, S], F32, name="veil0", offset=VEIL0_AT),
+            stage.tile([P, S], F32, name="veil1", offset=VEIL1_AT),
+            stage.tile([P, S], F32, name="veil2", offset=VEIL2_AT),
+            stage.tile([P, S], F32, name="veil3", offset=VEIL3_AT),
+        ]
+        w2w = keep.tile([P, H], U32, name="w2w", align_bytes=ALIGN)
+        w2s = keep.tile([P, H], U8, name="w2s", align_bytes=ALIGN)
+
+        def cast_w2(half):
+            for pair in range(2):
+                nc.vector.tensor_copy(
+                    out=w2b[pair][:, :, half * P // 2 : (half + 1) * P // 2, :].rearrange("p u m j -> p m j u"),
+                    in_=w2_raw[half][:].rearrange("p j (m t) -> p m j t", t=PACK)[:, :, :, 2 * pair : 2 * pair + 2],
+                )
+
+        def clamp(t):
+            nc.vector.tensor_scalar(veil[t][:], raw[t][:], 1.0, -1.0, ALU.min, ALU.mult)
+
+        def quantise_w2(pair, first, count):
             cols = slice((2 * pair + first) * P, (2 * pair + first + count) * P)
             nc.vector.quantize_mx(
                 out=w2w[:, cols].bitcast(FP8X4),
@@ -221,52 +208,53 @@ def tile_picked_nerfvol_none_po_kernel(
                 in_=w2b[pair][:, first : first + count].rearrange("p u m j -> p (u m j)"),
             )
 
+        cast_w2(0)
+        clamp(0)
+        cast_w2(1)
+        quantise_w2(0, 0, 1)
+        quantise_w2(0, 1, 1)
+        quantise_w2(1, 0, 2)
+        clamp(1)
+        clamp(2)
+        clamp(3)
+
         w3w = stage.tile([P, N], U32, name="w3w", offset=W3_WORDS_AT, align_bytes=ALIGN)
         w3s = stage.tile([P, N], U8, name="w3s", offset=W3_SCALES_AT, align_bytes=ALIGN)
         deal(nc.gpsimd.tensor_copy, w3w[:], w3w_raw, LINE // 4)
         deal(nc.gpsimd.tensor_copy, w3s[:], w3s_raw[:], LINE)
 
-        near = keep.tile([P, PACK, V], F32, name="near", align_bytes=ALIGN)
-        cut = keep.tile([P, PACK, V], F32, name="cut", align_bytes=ALIGN)
-        far = stage.tile([P, PACK, V], F32, name="far", offset=FAR_AT, align_bytes=ALIGN)
-        lit_pairs = [
-            stage.tile([P, 2, V], F32, name=f"lit{pair}", offset=at)
-            for pair, at in enumerate((LIT_FIRST_AT, LIT_LAST_AT))
-        ]
-        lit = [lit_pairs[t // 2][:, t % 2, :] for t in range(PACK)]
-        dim = [keep.tile([P, S], F32, name=f"dim{t}") for t in range(PACK)]
+        tint = [keep.tile([P, S], F32, name=f"tint{t}") for t in range(PACK)]
 
         def weigh(t, bank_no, part=slice(0, S)):
-            bank = project_val(t, bank_no, part)
-            nc.vector.scalar_tensor_tensor(dim[t][:, part], e_all[t][:, part], 1.0, bank[:], ALU.subtract, ALU.mult)
-
-        def light(t):
-            nc.vector.tensor_tensor(lit[t], e_all[t][:].indirect(p2_sb[:]), bg_sb[:, t, :], ALU.mult)
-
-        def far_sum(t, rays=slice(0, V)):
-            nc.vector.tensor_tensor(
-                far[:, t, rays], dim[t][:].indirect(entries(p2_sb, rays)), lit[t][:, rays], ALU.subtract
-            )
-
-        def near_at(t, rays=slice(0, V)):
-            nc.scalar.activation(near[:, t, rays], dim[t][:].indirect(entries(p1_sb, rays)), ACT.Copy)
+            bank = project(w2w[:, t * P : (t + 1) * P], w2s[:, t * P : (t + 1) * P], bank_no, part)
+            nc.vector.scalar_tensor_tensor(tint[t][:, part], veil[t][:, part], 1.0, bank[:], ALU.add, ALU.mult)
 
         for bank_no, part in zip(VAL_BANKS[0], SAMPLES):
             weigh(0, bank_no, part)
-        weigh(1, VAL_BANKS[1][0])
-        for t in FIRST:
-            light(t)
-        for t in LAST:
+        for t in range(1, PACK):
             weigh(t, VAL_BANKS[t][0])
-        far_sum(0)
-        light(2)
-        far_sum(1)
-        nc.vector.tensor_tensor(lit[3], e2[:], bg_sb[:, 3, :], ALU.mult)
-        for t in FIRST:
-            near_at(t)
+
+        lit = stage.tile([P, PACK, V], F32, name="lit", offset=LIT_AT, align_bytes=ALIGN)
+        near = stage.tile([P, PACK, V], F32, name="near", offset=NEAR_AT, align_bytes=ALIGN)
+        far = keep.tile([P, PACK, V], F32, name="far", align_bytes=ALIGN)
+        cut = keep.tile([P, PACK, V], F32, name="cut", align_bytes=ALIGN)
+
+        for t in range(2):
+            fetch(near[:, t, :], tint[t], p1_sb[:])
         for rays in RAYS:
-            for t in LAST:
-                near_at(t, rays)
+            for t in range(2, PACK):
+                fetch(near[:, t, rays], tint[t], entries(p1_sb, rays))
+
+        for tiles in (FIRST, LAST):
+            nc.vector.scalar_tensor_tensor(
+                lit[:, tiles, :], e_far[:, tiles, :], 1.0, bg_sb[:, tiles, :], ALU.min, ALU.mult
+            )
+        for t in range(3):
+            nc.vector.tensor_tensor(far[:, t, :], tint[t][:].indirect(p2_sb[:]), lit[:, t, :], ALU.add)
+        for rays in RAYS:
+            nc.vector.tensor_tensor(
+                far[:, 3, rays], tint[3][:].indirect(entries(p2_sb, rays)), lit[:, 3, rays], ALU.add
+            )
 
         zw = keep.tile([P, V], U32, name="zw", align_bytes=ALIGN)
         zs = keep.tile([P, V], U8, name="zs", align_bytes=ALIGN)
@@ -283,20 +271,10 @@ def tile_picked_nerfvol_none_po_kernel(
                 in_=src[half][:].rearrange("p v t -> p (v t)"),
             )
 
-        def pass_on(rays):
-            nc.vector.scalar_tensor_tensor(cut[:, :, rays], e1[:, :, rays], -1.0, far[:, :, rays], ALU.mult, ALU.mult)
-
-        def blend(half):
-            rays = RAYS[half]
-            nc.vector.tensor_tensor(by_word(zb[half]), by_tile(cut[:, :, rays]), by_tile(near[:, :, rays]), ALU.subtract)
-
-        far_sum(2)
         for rays in RAYS:
-            far_sum(3, rays)
-        for rays in RAYS:
-            pass_on(rays)
-        for half in range(2):
-            blend(half)
+            nc.vector.scalar_tensor_tensor(cut[:, :, rays], e_near[:, :, rays], 1.0, far[:, :, rays], ALU.min, ALU.mult)
+        for half, rays in enumerate(RAYS):
+            nc.vector.tensor_tensor(by_word(zb[half]), by_tile(cut[:, :, rays]), by_tile(near[:, :, rays]), ALU.add)
         for half in range(2):
             quantise(zw, zs, zb, half)
         out_banks = []

@@ -33,12 +33,10 @@ OUT_BANKS = ((2, 3), (4, 5))
 
 NEAR_AT = 0
 VEIL3_AT = NEAR_AT
-W2B_LAST_AT = NEAR_AT + 4 * PACK * V
-W3_WORDS_AT = W2B_LAST_AT
-W2B_FIRST_AT = W3_WORDS_AT + 4 * H
-W3_SCALES_AT = W2B_FIRST_AT + 4 * H
-VEIL0_AT = W3_SCALES_AT
-VEIL2_AT = VEIL0_AT + 4 * S
+W3_WORDS_AT = NEAR_AT + 4 * PACK * V
+W3_SCALES_AT = W3_WORDS_AT + 4 * N
+CLEAR_AT = W3_SCALES_AT - QUAD
+VEIL2_AT = W3_SCALES_AT + N
 LIT_AT = VEIL2_AT
 E_FAR_AT = LIT_AT + 4 * PACK * V
 W1W_LAST_AT = E_FAR_AT + 4 * PACK * V - ALIGN
@@ -94,9 +92,13 @@ def tile_picked_nerfvol_none_po_kernel(
         xs = keep.tile([P, T], U8, name="xs", tag="xs", align_bytes=ALIGN)
         w1s_raw = keep.tile([P, H], U8, name="w1s_raw")
         w3s_raw = keep.tile([P, N], U8, name="w3s_raw")
+        zero = keep.tile([P, 1], F32, name="zero")
+        clear = stage.tile([P, 2 * QUAD // 4], F32, name="clear", offset=CLEAR_AT)
         nc.gpsimd.memset(xs[:].bitcast(I32), 0)
+        nc.vector.memset(zero[:], 0.0)
         nc.vector.memset(w1s_raw[:].bitcast(I32), 0)
         nc.vector.memset(w3s_raw[:].bitcast(I32), 0)
+        nc.scalar.activation(clear[:, 0:1], zero[:], ACT.Exp)
 
         w3w_raw = keep.tile([P, N], U32, name="w3w_raw")[:]
         w1w_raw = keep.tile([P, H], U32, name="w1w_raw")[:]
@@ -134,13 +136,11 @@ def tile_picked_nerfvol_none_po_kernel(
             stage.tile([P, 2 * P], U32, name="w1w1", offset=W1W_LAST_AT, align_bytes=ALIGN),
         ]
         w1s = [keep.tile([P, 2 * P], U8, name=f"w1s{pair}", align_bytes=ALIGN) for pair in range(2)]
-        deal(nc.gpsimd.tensor_copy, w1s[0][:], w1s_raw[:], LINE, FIRST)
-        for t in range(2):
-            deal(nc.gpsimd.tensor_copy, w1w[0][:, t * P : (t + 1) * P], w1w_raw, LINE // 4, slice(t, t + 1))
+        for pair, tiles in enumerate((FIRST, LAST)):
+            deal(nc.gpsimd.tensor_copy, w1s[pair][:], w1s_raw[:], LINE, tiles)
+            deal(nc.scalar.copy, w1w[pair][:], w1w_raw, LINE // 4, tiles)
         for part in SAMPLES:
             nc.vector.tensor_copy(xg_w[:, part], xw[:].indirect(entries(offs_sb, part)))
-        deal(nc.vector.tensor_copy, w1s[1][:], w1s_raw[:], LINE, LAST)
-        deal(nc.vector.tensor_copy, w1w[1][:], w1w_raw, LINE // 4, LAST)
 
         def project(words, scales, bank_no, part=slice(0, S)):
             bank = psum.tile([P, part.stop - part.start], F32, name="bank", tag=f"bank{bank_no}")
@@ -177,12 +177,9 @@ def tile_picked_nerfvol_none_po_kernel(
         for t in range(PACK):
             fetch(e_near[:, t, :], raw[t], p1_sb[:])
 
-        w2b = [
-            stage.tile([P, 2, P, PACK], BF16, name=f"w2b{pair}", offset=at, align_bytes=ALIGN)
-            for pair, at in enumerate((W2B_FIRST_AT, W2B_LAST_AT))
-        ]
+        w2b = [keep.tile([P, 2, P, PACK], BF16, name=f"w2b{pair}", align_bytes=ALIGN) for pair in range(2)]
         veil = [
-            stage.tile([P, S], F32, name="veil0", offset=VEIL0_AT),
+            keep.tile([P, S], F32, name="veil0"),
             stage.tile([P, S], F32, name="veil1", offset=VEIL1_AT),
             stage.tile([P, S], F32, name="veil2", offset=VEIL2_AT),
             stage.tile([P, S], F32, name="veil3", offset=VEIL3_AT),
@@ -198,7 +195,7 @@ def tile_picked_nerfvol_none_po_kernel(
                 )
 
         def clamp(t):
-            nc.vector.tensor_scalar(veil[t][:], raw[t][:], 1.0, -1.0, ALU.min, ALU.mult)
+            nc.vector.tensor_scalar(veil[t][:], raw[t][:], clear[:, 0:1], -1.0, ALU.min, ALU.mult)
 
         def quantise_w2(pair, first, count):
             cols = slice((2 * pair + first) * P, (2 * pair + first + count) * P)

@@ -236,6 +236,8 @@ def tile_picked_nerfvol_none_po_kernel(
         far = keep.tile([P, PACK, V], F32, name="far", align_bytes=ALIGN)
         cut = keep.tile([P, PACK, V], F32, name="cut", align_bytes=ALIGN)
 
+        tint_far = keep.tile([P, V], F32, name="tint_far", align_bytes=ALIGN)
+        fetch(tint_far[:], tint[0], p2_sb[:])
         for t in range(2):
             fetch(near[:, t, :], tint[t], p1_sb[:])
         for rays in RAYS:
@@ -246,12 +248,10 @@ def tile_picked_nerfvol_none_po_kernel(
             nc.vector.scalar_tensor_tensor(
                 lit[:, tiles, :], e_far[:, tiles, :], 1.0, bg_sb[:, tiles, :], ALU.min, ALU.mult
             )
-        for t in range(3):
+        for t in range(1, PACK):
             nc.vector.tensor_tensor(far[:, t, :], tint[t][:].indirect(p2_sb[:]), lit[:, t, :], ALU.add)
         for rays in RAYS:
-            nc.vector.tensor_tensor(
-                far[:, 3, rays], tint[3][:].indirect(entries(p2_sb, rays)), lit[:, 3, rays], ALU.add
-            )
+            nc.vector.tensor_tensor(far[:, 0, rays], tint_far[:, rays], lit[:, 0, rays], ALU.add)
 
         zw = keep.tile([P, V], U32, name="zw", align_bytes=ALIGN)
         zs = keep.tile([P, V], U8, name="zs", align_bytes=ALIGN)

@@ -36,7 +36,9 @@ VEIL3_AT = NEAR_AT
 W3_WORDS_AT = NEAR_AT + 4 * PACK * V
 W3_SCALES_AT = W3_WORDS_AT + 4 * N
 CLEAR_AT = W3_SCALES_AT - QUAD
-VEIL2_AT = W3_SCALES_AT + N
+CLEAR_BYTES = N + 2 * QUAD
+DARK_AT = W3_SCALES_AT + N
+VEIL2_AT = DARK_AT + 4 * V
 LIT_AT = VEIL2_AT
 E_FAR_AT = LIT_AT + 4 * PACK * V
 W1W_LAST_AT = E_FAR_AT + 4 * PACK * V - ALIGN
@@ -93,7 +95,7 @@ def tile_picked_nerfvol_none_po_kernel(
         w1s_raw = keep.tile([P, H], U8, name="w1s_raw")
         w3s_raw = keep.tile([P, N], U8, name="w3s_raw")
         zero = keep.tile([P, 1], F32, name="zero")
-        clear = stage.tile([P, 2 * QUAD // 4], F32, name="clear", offset=CLEAR_AT)
+        clear = stage.tile([P, CLEAR_BYTES // 4], F32, name="clear", offset=CLEAR_AT)
         nc.gpsimd.memset(xs[:].bitcast(I32), 0)
         nc.vector.memset(zero[:], 0.0)
         nc.vector.memset(w1s_raw[:].bitcast(I32), 0)
@@ -170,13 +172,6 @@ def tile_picked_nerfvol_none_po_kernel(
         def fetch(out, table, offsets):
             nc.scalar.activation(out, table[:].indirect(offsets), ACT.Copy)
 
-        e_near = stage.tile([P, PACK, V], F32, name="e_near", offset=E_NEAR_AT, align_bytes=ALIGN)
-        e_far = stage.tile([P, PACK, V], F32, name="e_far", offset=E_FAR_AT, align_bytes=ALIGN)
-        for t in range(PACK):
-            fetch(e_far[:, t, :], raw[t], p2_sb[:])
-        for t in range(PACK):
-            fetch(e_near[:, t, :], raw[t], p1_sb[:])
-
         w2b = [keep.tile([P, 2, P, PACK], BF16, name=f"w2b{pair}", align_bytes=ALIGN) for pair in range(2)]
         veil = [
             keep.tile([P, S], F32, name="veil0"),
@@ -217,6 +212,16 @@ def tile_picked_nerfvol_none_po_kernel(
 
         w3w = stage.tile([P, N], U32, name="w3w", offset=W3_WORDS_AT, align_bytes=ALIGN)
         w3s = stage.tile([P, N], U8, name="w3s", offset=W3_SCALES_AT, align_bytes=ALIGN)
+        e_near = stage.tile([P, PACK, V], F32, name="e_near", offset=E_NEAR_AT, align_bytes=ALIGN)
+        e_far = stage.tile([P, PACK, V], F32, name="e_far", offset=E_FAR_AT, align_bytes=ALIGN)
+        fetch(e_far[:, 0, :], veil[0], p2_sb[:])
+        for t in range(1, PACK):
+            fetch(e_far[:, t, :], raw[t], p2_sb[:])
+        for t in range(PACK):
+            fetch(e_near[:, t, :], raw[t], p1_sb[:])
+
+        dark = stage.tile([P, V], F32, name="dark", offset=DARK_AT, align_bytes=ALIGN)
+        nc.gpsimd.tensor_tensor(dark[:], e_far[:, 0, :], bg_sb[:, 0, :], ALU.mult)
         deal(nc.gpsimd.tensor_copy, w3w[:], w3w_raw, LINE // 4)
         deal(nc.gpsimd.tensor_copy, w3s[:], w3s_raw[:], LINE)
 
@@ -236,22 +241,23 @@ def tile_picked_nerfvol_none_po_kernel(
         far = keep.tile([P, PACK, V], F32, name="far", align_bytes=ALIGN)
         cut = keep.tile([P, PACK, V], F32, name="cut", align_bytes=ALIGN)
 
-        tint_far = keep.tile([P, V], F32, name="tint_far", align_bytes=ALIGN)
-        fetch(tint_far[:], tint[0], p2_sb[:])
+        first, last = RAYS
+        tint_far = keep.tile([P, V // 2], F32, name="tint_far", align_bytes=ALIGN)
+        fetch(tint_far[:], tint[0], entries(p2_sb, last))
         for t in range(2):
             fetch(near[:, t, :], tint[t], p1_sb[:])
         for rays in RAYS:
             for t in range(2, PACK):
                 fetch(near[:, t, rays], tint[t], entries(p1_sb, rays))
 
-        for tiles in (FIRST, LAST):
+        for tiles in (slice(1, 2), LAST):
             nc.vector.scalar_tensor_tensor(
                 lit[:, tiles, :], e_far[:, tiles, :], 1.0, bg_sb[:, tiles, :], ALU.min, ALU.mult
             )
         for t in range(1, PACK):
             nc.vector.tensor_tensor(far[:, t, :], tint[t][:].indirect(p2_sb[:]), lit[:, t, :], ALU.add)
-        for rays in RAYS:
-            nc.vector.tensor_tensor(far[:, 0, rays], tint_far[:, rays], lit[:, 0, rays], ALU.add)
+        nc.vector.tensor_tensor(far[:, 0, first], tint[0][:].indirect(entries(p2_sb, first)), dark[:, first], ALU.subtract)
+        nc.vector.tensor_tensor(far[:, 0, last], tint_far[:], dark[:, last], ALU.subtract)
 
         zw = keep.tile([P, V], U32, name="zw", align_bytes=ALIGN)
         zs = keep.tile([P, V], U8, name="zs", align_bytes=ALIGN)

@@ -33,18 +33,19 @@ OUT_BANKS = ((2, 3), (4, 5))
 
 NEAR_AT = 0
 VEIL3_AT = NEAR_AT
-W3_WORDS_AT = NEAR_AT + 4 * PACK * V
-W3_SCALES_AT = W3_WORDS_AT + 4 * N
+DARK_AT = NEAR_AT + 4 * PACK * V
+W3_SCALES_AT = DARK_AT + 4 * V
 CLEAR_AT = W3_SCALES_AT - QUAD
-CLEAR_BYTES = N + 2 * QUAD
-DARK_AT = W3_SCALES_AT + N
-VEIL2_AT = DARK_AT + 4 * V
+CLEAR_BYTES = 2 * QUAD
+VEIL2_AT = W3_SCALES_AT + N
 LIT_AT = VEIL2_AT
 E_FAR_AT = LIT_AT + 4 * PACK * V
 W1W_LAST_AT = E_FAR_AT + 4 * PACK * V - ALIGN
 E_NEAR_AT = W1W_LAST_AT + ALIGN
 W2_LAST_AT = E_NEAR_AT + 4 * PACK * V
 VEIL1_AT = W2_LAST_AT
+TINT3_AT = W2_LAST_AT + 4 * PACK * H // 2
+W3_WORDS_AT = TINT3_AT
 
 
 def words_i32(ap):
@@ -210,7 +211,6 @@ def tile_picked_nerfvol_none_po_kernel(
         clamp(2)
         clamp(3)
 
-        w3w = stage.tile([P, N], U32, name="w3w", offset=W3_WORDS_AT, align_bytes=ALIGN)
         w3s = stage.tile([P, N], U8, name="w3s", offset=W3_SCALES_AT, align_bytes=ALIGN)
         e_near = stage.tile([P, PACK, V], F32, name="e_near", offset=E_NEAR_AT, align_bytes=ALIGN)
         e_far = stage.tile([P, PACK, V], F32, name="e_far", offset=E_FAR_AT, align_bytes=ALIGN)
@@ -222,10 +222,10 @@ def tile_picked_nerfvol_none_po_kernel(
 
         dark = stage.tile([P, V], F32, name="dark", offset=DARK_AT, align_bytes=ALIGN)
         nc.gpsimd.tensor_tensor(dark[:], e_far[:, 0, :], bg_sb[:, 0, :], ALU.mult)
-        deal(nc.gpsimd.tensor_copy, w3w[:], w3w_raw, LINE // 4)
         deal(nc.gpsimd.tensor_copy, w3s[:], w3s_raw[:], LINE)
 
-        tint = [keep.tile([P, S], F32, name=f"tint{t}") for t in range(PACK)]
+        tint = [keep.tile([P, S], F32, name=f"tint{t}") for t in range(3)]
+        tint.append(stage.tile([P, S], F32, name="tint3", offset=TINT3_AT))
 
         def weigh(t, bank_no, part=slice(0, S)):
             bank = project(w2w[:, t * P : (t + 1) * P], w2s[:, t * P : (t + 1) * P], bank_no, part)
@@ -258,6 +258,10 @@ def tile_picked_nerfvol_none_po_kernel(
             nc.vector.tensor_tensor(far[:, t, :], tint[t][:].indirect(p2_sb[:]), lit[:, t, :], ALU.add)
         nc.vector.tensor_tensor(far[:, 0, first], tint[0][:].indirect(entries(p2_sb, first)), dark[:, first], ALU.subtract)
         nc.vector.tensor_tensor(far[:, 0, last], tint_far[:], dark[:, last], ALU.subtract)
+
+        w3w = stage.tile([P, N], U32, name="w3w", offset=W3_WORDS_AT, align_bytes=ALIGN)
+        for tiles in (FIRST, LAST):
+            deal(nc.scalar.copy, w3w[:, tiles.start * P : tiles.stop * P], w3w_raw, LINE // 4, tiles)
 
         zw = keep.tile([P, V], U32, name="zw", align_bytes=ALIGN)
         zs = keep.tile([P, V], U8, name="zs", align_bytes=ALIGN)

from contextlib import ExitStack

import concourse.mybir as mybir

K, T, S, V, N, H = 512, 2048, 512, 256, 512, 512
FLOPS = 2 * K * S * H * 2 + 2 * H * N * V

F32 = mybir.dt.float32
BF16 = mybir.dt.bfloat16
I32 = mybir.dt.int32
U32 = mybir.dt.uint32
U16 = mybir.dt.uint16
U8 = mybir.dt.uint8
FP8X4 = mybir.dt.float8_e4m3fn_x4
ALU = mybir.AluOpType
ACT = mybir.ActivationFunctionType

P = 128
PACK = 4
QUAD = 32
BLOCKS = 16
GROUP = 16
LINE = 16
ALIGN = 64
X_ROW, W1_ROW, W3_ROW = 4, 8, 12
FIRST, LAST = slice(0, 2), slice(2, 4)
SAMPLES = (slice(0, S // 2), slice(S // 2, S))
RAYS = (slice(0, V // 2), slice(V // 2, V))

S_BANKS = ((0, 1), (2,), (3,), (4,))
VAL_BANKS = ((5, 6), (7,), (0,), (1,))
OUT_BANKS = ((2, 3), (4, 5))

NEAR_AT = 0
VEIL3_AT = NEAR_AT
DARK_AT = NEAR_AT + 4 * PACK * V
W3_SCALES_AT = DARK_AT + 4 * V
CLEAR_AT = W3_SCALES_AT - QUAD
CLEAR_BYTES = 2 * QUAD
VEIL2_AT = W3_SCALES_AT + N
LIT_AT = VEIL2_AT
E_FAR_AT = LIT_AT + 4 * PACK * V
W1W_LAST_AT = E_FAR_AT + 4 * PACK * V - ALIGN
E_NEAR_AT = W1W_LAST_AT + ALIGN
W2_LAST_AT = E_NEAR_AT + 4 * PACK * V
VEIL1_AT = W2_LAST_AT
TINT3_AT = W2_LAST_AT + 4 * PACK * H // 2
W3_WORDS_AT = TINT3_AT


def words_i32(ap):
    return ap[0].rearrange("p n t -> p (n t)").bitcast(I32)


def load_scales(queue, plane, scales, first, rows=range(PACK)):
    for r in rows:
        queue.dma_start(
            out=plane[:].bitcast(I32)[first + r : P : QUAD, :],
            in_=scales[0].bitcast(I32)[r:BLOCKS:PACK, :],
        )


def deal(move, dst, src, run, tiles=slice(0, PACK)):
    move(
        out=dst.rearrange("p (t c i) -> p c t i", t=tiles.stop - tiles.start, i=run),
        in_=src.rearrange("p (c i t) -> p c t i", t=PACK, i=run)[:, :, tiles, :],
    )


def by_tile(ap):
    return ap.rearrange("p t (c i) -> p c t i", i=PACK)


def by_word(tile):
    return tile[:].rearrange("p (c i) t -> p c t i", i=PACK)


def entries(offsets, part):
    return offsets[:, part.start // GROUP : part.stop // GROUP]


def tile_picked_nerfvol_none_po_kernel(
    tc, x_words, x_scales, w1_words, w1_scales, w2, bg, w3_words, w3_scales, offs, p1, p2, out_0, out_1, out_2
):
    nc = tc.nc
    with ExitStack() as ctx:
        keep = ctx.enter_context(tc.tile_pool(name="keep", bufs=1))
        stage = ctx.enter_context(tc.tile_pool(name="stage", bufs=1))
        psum = ctx.enter_context(tc.psum_pool(name="psum", bufs=1))

        offs_sb = keep.tile([P, S // GROUP], U16, name="offs_sb")
        p1_sb = keep.tile([P, V // GROUP], U16, name="p1_sb")
        p2_sb = keep.tile([P, V // GROUP], U16, name="p2_sb")
        xw = keep.tile([P, T], U32, name="xw")
        xs = keep.tile([P, T], U8, name="xs", tag="xs", align_bytes=ALIGN)
        w1s_raw = keep.tile([P, H], U8, name="w1s_raw")
        w3s_raw = keep.tile([P, N], U8, name="w3s_raw")
        zero = keep.tile([P, 1], F32, name="zero")
        clear = stage.tile([P, CLEAR_BYTES // 4], F32, name="clear", offset=CLEAR_AT)
        nc.gpsimd.memset(xs[:].bitcast(I32), 0)
        nc.vector.memset(zero[:], 0.0)
        nc.vector.memset(w1s_raw[:].bitcast(I32), 0)
        nc.vector.memset(w3s_raw[:].bitcast(I32), 0)
        nc.scalar.activation(clear[:, 0:1], zero[:], ACT.Exp)

        w3w_raw = keep.tile([P, N], U32, name="w3w_raw")[:]
        w1w_raw = keep.tile([P, H], U32, name="w1w_raw")[:]
        w2_raw = [
            keep.tile([P, PACK, H // 2], F32, name="w2_first"),
            stage.tile([P, PACK, H // 2], F32, name="w2_last", offset=W2_LAST_AT, align_bytes=ALIGN),
        ]
        bg_sb = keep.tile([P, PACK, V], F32, name="bg_sb")
        w2_rows = w2.rearrange("(p j) (half c) -> p half j c", j=PACK, half=2)
        bg_rows = bg.rearrange("(p t) v -> p t v", t=PACK)

        def load_x_words(start, stop):
            nc.sync.dma_start(out=xw[:, start:stop].bitcast(I32), in_=words_i32(x_words)[:, start:stop])

        nc.sync.dma_start(offs_sb[:], offs)
        load_x_words(0, T // 4)
        load_scales(nc.sync, xs, x_scales, X_ROW)
        load_x_words(T // 4, T)
        load_scales(nc.sync, w1s_raw, w1_scales, W1_ROW)
        nc.sync.dma_start(out=w1w_raw.bitcast(I32), in_=words_i32(w1_words))
        for half in range(2):
            nc.sync.dma_start(out=w2_raw[half][:], in_=w2_rows[:, half])
        nc.sync.dma_start(p2_sb[:], p2)
        nc.sync.dma_start(p1_sb[:], p1)
        nc.sync.dma_start(out=w3w_raw.bitcast(I32), in_=words_i32(w3_words))
        nc.sync.dma_start(out=bg_sb[:], in_=bg_rows)
        load_scales(nc.gpsimd, w3s_raw, w3_scales, W3_ROW, range(0, 2))
        load_scales(nc.sync, w3s_raw, w3_scales, W3_ROW, range(2, PACK))

        xg_s = keep.tile([P, S], U8, name="xg_s", align_bytes=ALIGN)
        nc.vector.tensor_copy(xg_s[:], xs[:].indirect(offs_sb[:]))
        xg_w = keep.tile([P, S], U32, name="xg_w", tag="xs", align_bytes=ALIGN)
        w1w = [
            keep.tile([P, 2 * P], U32, name="w1w0", align_bytes=ALIGN),
            stage.tile([P, 2 * P], U32, name="w1w1", offset=W1W_LAST_AT, align_bytes=ALIGN),
        ]
        w1s = [keep.tile([P, 2 * P], U8, name=f"w1s{pair}", align_bytes=ALIGN) for pair in range(2)]
        for pair, tiles in enumerate((FIRST, LAST)):
            deal(nc.gpsimd.tensor_copy, w1s[pair][:], w1s_raw[:], LINE, tiles)
            deal(nc.scalar.copy, w1w[pair][:], w1w_raw, LINE // 4, tiles)
        for part in SAMPLES:
            nc.vector.tensor_copy(xg_w[:, part], xw[:].indirect(entries(offs_sb, part)))

        def project(words, scales, bank_no, part=slice(0, S)):
            bank = psum.tile([P, part.stop - part.start], F32, name="bank", tag=f"bank{bank_no}")
            nc.tensor.matmul_mx(
                out=bank[:],
                lhsT=words.bitcast(FP8X4),
                lhsT_scale=scales,
                rhs=xg_w[:, part].bitcast(FP8X4),
                rhs_scale=xg_s[X_ROW:P, part],
                start=True,
                stop=True,
            )
            return bank

        raw = [keep.tile([P, S], F32, name=f"raw{t}") for t in range(PACK)]

        def expose(t, bank_no, part=slice(0, S)):
            cols = slice(t % 2 * P, (t % 2 + 1) * P)
            bank = project(w1w[t // 2][:, cols], w1s[t // 2][W1_ROW:P, cols], bank_no, part)
            nc.scalar.activation(raw[t][:, part], bank[:], ACT.Exp, scale=-1.0)

        for bank_no, part in zip(S_BANKS[0], SAMPLES):
            expose(0, bank_no, part)
        for t in range(1, PACK):
            expose(t, S_BANKS[t][0])

        def fetch(out, table, offsets):
            nc.scalar.activation(out, table[:].indirect(offsets), ACT.Copy)

        w2b = [keep.tile([P, 2, P, PACK], BF16, name=f"w2b{pair}", align_bytes=ALIGN) for pair in range(2)]
        veil = [
            keep.tile([P, S], F32, name="veil0"),
            stage.tile([P, S], F32, name="veil1", offset=VEIL1_AT),
            stage.tile([P, S], F32, name="veil2", offset=VEIL2_AT),
            stage.tile([P, S], F32, name="veil3", offset=VEIL3_AT),
        ]
        w2w = keep.tile([P, H], U32, name="w2w", align_bytes=ALIGN)
        w2s = keep.tile([P, H], U8, name="w2s", align_bytes=ALIGN)

        def cast_w2(half):
            for pair in range(2):
                nc.vector.tensor_copy(
                    out=w2b[pair][:, :, half * P // 2 : (half + 1) * P // 2, :].rearrange("p u m j -> p m j u"),
                    in_=w2_raw[half][:].rearrange("p j (m t) -> p m j t", t=PACK)[:, :, :, 2 * pair : 2 * pair + 2],
                )

        def clamp(t):
            nc.vector.tensor_scalar(veil[t][:], raw[t][:], clear[:, 0:1], -1.0, ALU.min, ALU.mult)

        def quantise_w2(pair, first, count):
            cols = slice((2 * pair + first) * P, (2 * pair + first + count) * P)
            nc.vector.quantize_mx(
                out=w2w[:, cols].bitcast(FP8X4),
                scales=w2s[:, cols],
                in_=w2b[pair][:, first : first + count].rearrange("p u m j -> p (u m j)"),
            )

        cast_w2(0)
        clamp(0)
        cast_w2(1)
        quantise_w2(0, 0, 1)
        quantise_w2(0, 1, 1)
        quantise_w2(1, 0, 2)
        clamp(1)
        clamp(2)
        clamp(3)

        w3s = stage.tile([P, N], U8, name="w3s", offset=W3_SCALES_AT, align_bytes=ALIGN)
        e_near = stage.tile([P, PACK, V], F32, name="e_near", offset=E_NEAR_AT, align_bytes=ALIGN)
        e_far = stage.tile([P, PACK, V], F32, name="e_far", offset=E_FAR_AT, align_bytes=ALIGN)
        fetch(e_far[:, 0, :], veil[0], p2_sb[:])
        for t in range(1, PACK):
            fetch(e_far[:, t, :], raw[t], p2_sb[:])
        for t in range(PACK):
            fetch(e_near[:, t, :], raw[t], p1_sb[:])

        dark = stage.tile([P, V], F32, name="dark", offset=DARK_AT, align_bytes=ALIGN)
        nc.gpsimd.tensor_tensor(dark[:], e_far[:, 0, :], bg_sb[:, 0, :], ALU.mult)
        deal(nc.gpsimd.tensor_copy, w3s[:], w3s_raw[:], LINE)

        tint = [keep.tile([P, S], F32, name=f"tint{t}") for t in range(3)]
        tint.append(stage.tile([P, S], F32, name="tint3", offset=TINT3_AT))

        def weigh(t, bank_no, part=slice(0, S)):
            bank = project(w2w[:, t * P : (t + 1) * P], w2s[:, t * P : (t + 1) * P], bank_no, part)
            nc.vector.scalar_tensor_tensor(tint[t][:, part], veil[t][:, part], 1.0, bank[:], ALU.add, ALU.mult)

        for bank_no, part in zip(VAL_BANKS[0], SAMPLES):
            weigh(0, bank_no, part)
        for t in range(1, PACK):
            weigh(t, VAL_BANKS[t][0])

        lit = stage.tile([P, PACK, V], F32, name="lit", offset=LIT_AT, align_bytes=ALIGN)
        near = stage.tile([P, PACK, V], F32, name="near", offset=NEAR_AT, align_bytes=ALIGN)
        far = keep.tile([P, PACK, V], F32, name="far", align_bytes=ALIGN)
        cut = keep.tile([P, PACK, V], F32, name="cut", align_bytes=ALIGN)

        first, last = RAYS
        tint_far = keep.tile([P, V // 2], F32, name="tint_far", align_bytes=ALIGN)
        fetch(tint_far[:], tint[0], entries(p2_sb, last))
        for t in range(2):
            fetch(near[:, t, :], tint[t], p1_sb[:])
        for rays in RAYS:
            for t in range(2, PACK):
                fetch(near[:, t, rays], tint[t], entries(p1_sb, rays))

        for tiles in (slice(1, 2), LAST):
            nc.vector.scalar_tensor_tensor(
                lit[:, tiles, :], e_far[:, tiles, :], 1.0, bg_sb[:, tiles, :], ALU.min, ALU.mult
            )
        for t in range(1, PACK):
            nc.vector.tensor_tensor(far[:, t, :], tint[t][:].indirect(p2_sb[:]), lit[:, t, :], ALU.add)
        nc.vector.tensor_tensor(far[:, 0, first], tint[0][:].indirect(entries(p2_sb, first)), dark[:, first], ALU.subtract)
        nc.vector.tensor_tensor(far[:, 0, last], tint_far[:], dark[:, last], ALU.subtract)

        w3w = stage.tile([P, N], U32, name="w3w", offset=W3_WORDS_AT, align_bytes=ALIGN)
        for tiles in (FIRST, LAST):
            deal(nc.scalar.copy, w3w[:, tiles.start * P : tiles.stop * P], w3w_raw, LINE // 4, tiles)

        zw = keep.tile([P, V], U32, name="zw", align_bytes=ALIGN)
        zs = keep.tile([P, V], U8, name="zs", align_bytes=ALIGN)
        ow = keep.tile([P, V], U32, name="ow", align_bytes=ALIGN)
        osc = keep.tile([P, V], U8, name="osc", align_bytes=ALIGN)
        zb = [keep.tile([P, V // 2, PACK], BF16, name=f"zb{half}", align_bytes=ALIGN) for half in range(2)]
        ob = [keep.tile([P, V // 2, PACK], BF16, name=f"ob{half}", align_bytes=ALIGN) for half in range(2)]
        of = [keep.tile([P, PACK, V // 2], F32, name=f"of{half}", align_bytes=ALIGN) for half in range(2)]

        def quantise(words, scales, src, half):
            nc.vector.quantize_mx(
                out=words[:, RAYS[half]].bitcast(FP8X4),
                scales=scales[:, RAYS[half]],
                in_=src[half][:].rearrange("p v t -> p (v t)"),
            )

        for rays in RAYS:
            nc.vector.scalar_tensor_tensor(cut[:, :, rays], e_near[:, :, rays], 1.0, far[:, :, rays], ALU.min, ALU.mult)
        for half, rays in enumerate(RAYS):
            nc.vector.tensor_tensor(by_word(zb[half]), by_tile(cut[:, :, rays]), by_tile(near[:, :, rays]), ALU.add)
        for half in range(2):
            quantise(zw, zs, zb, half)
        out_banks = []
        for half, rays in enumerate(RAYS):
            banks = [psum.tile([P, 2, V // 2], F32, name="out_bank", tag=f"bank{no}") for no in OUT_BANKS[half]]
            for t in range(PACK):
                nc.tensor.matmul_mx(
                    out=banks[t // 2][:, t % 2, :],
                    lhsT=w3w[:, t * P : (t + 1) * P].bitcast(FP8X4),
                    lhsT_scale=w3s[W3_ROW:P, t * P : (t + 1) * P],
                    rhs=zw[:, rays].bitcast(FP8X4),
                    rhs_scale=zs[:, rays],
                    start=True,
                    stop=True,
                )
            out_banks.append(banks)

        out_rows = out_0.rearrange("(p t) v -> p t v", t=PACK)
        for half, (second_copy, queue) in enumerate(((nc.vector.tensor_copy, nc.sync), (nc.scalar.copy, nc.scalar))):
            nc.scalar.copy(of[half][:, 0:2, :], out_banks[half][0][:])
            second_copy(of[half][:, 2:4, :], out_banks[half][1][:])
            queue.dma_start(out=out_rows[:, :, RAYS[half]], in_=of[half][:])
            nc.vector.tensor_copy(out=by_word(ob[half]), in_=by_tile(of[half][:]))
            quantise(ow, osc, ob, half)
            nc.sync.dma_start(out=words_i32(out_1)[:, RAYS[half]], in_=ow[:, RAYS[half]].bitcast(I32))
        for r in range(PACK):
            queue = nc.sync if r % 2 else nc.scalar
            queue.dma_start(out=out_2[0].bitcast(I32)[r:BLOCKS:PACK, :], in_=osc[:].bitcast(I32)[r:P:QUAD, :])
